import numpy as np
import ml_dtypes


def mxq(x, axis, fmt="e4m3"):
    dtype, down = {"e4m3": (ml_dtypes.float8_e4m3fn, 7), "e5m2": (ml_dtypes.float8_e5m2, 14)}[fmt]
    v = np.moveaxis(np.asarray(x, np.float32).astype(ml_dtypes.bfloat16).astype(np.float64), axis, -1)
    blocks = v.reshape(v.shape[:-1] + (-1, 32))
    amax = np.abs(blocks).max(-1, keepdims=True)
    byte = np.maximum(np.where(amax > 0, np.frexp(amax)[1] - 1 + 127, 0) - down, 1)
    scale = np.exp2(byte - 127.0)
    codes = (blocks / scale).astype(np.float32).astype(dtype).astype(np.float64)
    return np.moveaxis((codes * scale).reshape(v.shape), -1, axis)


WIDE = False


def mx_kscale(k):
    if not WIDE:
        return np.ones(k)
    levels = np.array([10, -10, 5, -5, 0])
    if k % 512:
        return np.exp2(np.random.permutation(np.resize(levels, k // 32))).repeat(32)
    a = np.empty((k // 512, 16))
    for p in range(k // 512):
        a[p, :8] = np.random.permutation(np.resize(levels, 8))
        for g in range(8):
            far = levels[np.abs(levels - a[p, g]) >= 10]
            a[p, g + 8] = far[np.random.randint(len(far))]
    return np.exp2(a.ravel()).repeat(32)


def f64(x):
    return np.asarray(x).astype(np.float64)


def striped(idx):
    return np.tile(idx.reshape(-1, 16).T, (8, 1)).astype(np.uint16)


def unstriped(offs):
    return offs[:16].T.reshape(-1).astype(np.int64)


E2M1 = np.array([0.0, 0.5, 1.0, 1.5, 2.0, 3.0, 4.0, 6.0, -0.0, -0.5, -1.0, -1.5, -2.0, -3.0, -4.0, -6.0])


def pack_weight(w, fmt):
    k, n = w.shape
    w = f64(np.asarray(w, np.float32).astype(ml_dtypes.bfloat16)).reshape(k // 32, 32, n)
    amax = np.abs(w).max(1)
    if fmt == "e4m3":
        byte = np.frexp(amax)[1] - 1 + 127 - 7
    else:
        mant, ex = np.frexp(amax / 6.0)
        byte = np.where(mant > 0.5, ex, ex - 1) + 127
    byte = np.clip(np.where(amax > 0, byte, 1), 1, 254)
    scaled = (w * np.exp2(127.0 - byte)[:, None, :]).reshape(k, n).astype(np.float32)
    by_word = np.ascontiguousarray(scaled.reshape(k // 512, 128, 4, n).transpose(0, 1, 3, 2))
    if fmt == "e4m3":
        words = by_word.astype(ml_dtypes.float8_e4m3fn).view(np.uint8)
    else:
        c = by_word.astype(ml_dtypes.float4_e2m1fn).view(np.uint8) & 0xF
        words = (c[..., 0::2] | (c[..., 1::2] << 4)).reshape(k // 512, 128, 2 * n)
    return np.ascontiguousarray(words), np.ascontiguousarray(byte.astype(np.uint8).reshape(k // 512, 16, n))


def unpack_weight(words, scales, fmt):
    g, _, n = scales.shape
    words = np.ascontiguousarray(words).reshape(g, 128, n, -1)
    if fmt == "e4m3":
        vals = words.view(ml_dtypes.float8_e4m3fn).astype(np.float64)
    else:
        nib = np.empty((g, 128, n, 4), np.uint8)
        nib[..., 0::2] = words & 0xF
        nib[..., 1::2] = words >> 4
        vals = E2M1[nib]
    vals = vals * np.repeat(np.exp2(scales.astype(np.float64) - 127.0), 8, axis=1)[..., None]
    return vals.transpose(0, 1, 3, 2).reshape(g * 512, n)


def gelu(v):
    return 0.5 * v * (1.0 + np.tanh(np.sqrt(2.0 / np.pi) * (v + 0.044715 * v**3)))


K, T, S, T2, H, N, P = 1024, 2048, 1024, 2048, 1024, 512, 128

def setup_inputs():
    n = np.random.standard_normal
    s = mx_kscale(K)[:, None]
    u = mx_kscale(H)[:, None]
    tab_words, tab_scales = pack_weight(n((K, T)) * s, "e4m3")
    w4_words, w4_scales = pack_weight(n((H, N)) / np.sqrt(H) / u, "e2m1")
    return {
        "tab_words": tab_words, "tab_scales": tab_scales,
        "offs": striped(np.random.permutation(T)[:S]),
        "w1": (n((K, H)) / np.sqrt(K) / s * u.T).astype(np.float32),
        "b1": (0.5 * n(H) * u[:, 0]).astype(np.float32),
        "wgs": np.exp(0.3 * n((P, S))).astype(np.float32),
        "offs2": striped(np.random.permutation(T2)[:S]),
        "old": (n((H, T2)) * u).astype(np.float32),
        "w4_words": w4_words, "w4_scales": w4_scales,
        "b4": (0.5 * n(N)).astype(np.float32),
    }

def reference(tab_words, tab_scales, offs, w1, b1, wgs, offs2, old, w4_words, w4_scales, b4):
    v = unpack_weight(tab_words, tab_scales, "e4m3")[:, unstriped(offs)]
    a = mxq(f64(w1), 0, "e4m3").T @ v
    h = np.abs(a + f64(b1)[:, None])
    page = np.zeros((H, T2))
    page[:, unstriped(offs2)] = np.tile(f64(wgs), (H // P, 1)) * h
    z = np.maximum(page, f64(old))
    zq = mxq(z, 0, "e4m3")
    w4 = unpack_weight(w4_words, w4_scales, "e2m1")
    y = w4.T @ zq
    return y + f64(b4)[:, None]

@@ -1,0 +1,262 @@
+from contextlib import ExitStack
+
+import concourse.mybir as mybir
+
+K, T, S, T2, H, N = 1024, 2048, 1024, 2048, 1024, 512
+P = 128
+PACK = 4
+KP = P * PACK
+BANK = 512
+FLOPS = 2 * K * H * S + 2 * H * N * T2
+
+F32 = mybir.dt.float32
+BF16 = mybir.dt.bfloat16
+I32 = mybir.dt.int32
+U32 = mybir.dt.uint32
+U16 = mybir.dt.uint16
+U8 = mybir.dt.uint8
+FP8X4 = mybir.dt.float8_e4m3fn_x4
+FP4X4 = mybir.dt.float4_e2m1fn_x4
+ALU = mybir.AluOpType
+ACT = mybir.ActivationFunctionType
+
+
+def tile_list_recommender_slot_memory_kernel(
+    tc, tab_words, tab_scales, offs, w1, b1, wgs, offs2, old, w4_words, w4_scales, b4, out
+):
+    nc = tc.nc
+    with ExitStack() as ctx:
+        held = ctx.enter_context(tc.tile_pool(name="held", bufs=1))
+        ring = ctx.enter_context(tc.tile_pool(name="ring", bufs=1))
+        psum = ctx.enter_context(tc.psum_pool(name="psum", bufs=8))
+
+        idx = held.tile([P, S // 16], U16, name="idx")
+        idx2 = held.tile([P, S // 16], U16, name="idx2")
+        tab_w = [held.tile([P, T], I32, name="tab_w%d" % a, align_bytes=64) for a in range(2)]
+        tab_s = held.tile([P, T], U8, name="tab_s", align_bytes=64)
+        v_w = [[held.tile([P, BANK], U32, name="v_w%d%d" % (a, e), align_bytes=64) for e in range(2)] for a in range(2)]
+        v_s = [held.tile([P, BANK], U8, name="v_s%d" % e, align_bytes=64) for e in range(2)]
+        w1_c = [[held.tile([P, KP], U32, name="w1_c%d%d" % (a, b), align_bytes=64) for b in range(2)] for a in range(2)]
+        w1_s = [[held.tile([P, KP], U8, name="w1_s%d%d" % (a, b), align_bytes=64) for b in range(2)] for a in range(2)]
+        wg = [held.tile([P, S], F32, name="wg%d" % t) for t in range(PACK)]
+        b1_t = held.tile([P, 2, 8], F32, name="b1_t")
+        b4_t = held.tile([P, 4, 8], F32, name="b4_t")
+        w4_w = held.tile([P, 2, 2 * N], U8, name="w4_w", align_bytes=64)
+        w4_s = held.tile([P, 2, N], U8, name="w4_s", align_bytes=64)
+        page = [held.tile([P, T2], F32, name="page%d" % t) for t in range(PACK)]
+        z0 = held.tile([P, PACK, T2], BF16, name="z0")
+        nch = T2 // BANK
+        z_c = [[held.tile([P, BANK], U32, name="z_c%d%d" % (b, c), align_bytes=64) for c in range(nch)] for b in range(2)]
+        z_s = [[held.tile([P, BANK], U8, name="z_s%d%d" % (b, c), align_bytes=64) for c in range(nch)] for b in range(2)]
+
+        def big(name):
+            return ring.tile([P, T2], F32, name=name, tag="big", bufs=7)
+
+        def load_w1(a, b):
+            raw = big("w1_raw")
+            nc.sync.dma_start(
+                raw[:].rearrange("p (j c) -> p j c", j=PACK),
+                w1[a * KP : (a + 1) * KP, b * KP : (b + 1) * KP].rearrange("(p j) c -> p j c", j=PACK),
+            )
+            return raw
+
+        def quant_w1(a, b, raw):
+            g = ring.tile([P, PACK * KP], BF16, name="w1_g", tag="g", bufs=3, align_bytes=64)
+            nc.scalar.copy(
+                g[:].rearrange("p (t m j) -> p m j t", t=PACK, j=PACK),
+                raw[:].rearrange("p (j m t) -> p m j t", j=PACK, t=PACK),
+            )
+            nc.vector.quantize_mx(w1_c[a][b][:].bitcast(FP8X4), w1_s[a][b][:], g[:])
+
+        def load_wg(t, cols, groups=(0, 2, 1, 3)):
+            rows = wgs.rearrange("(q t) s -> t q s", t=PACK)[t]
+            for g in groups:
+                nc.sync.dma_start(wg[t][32 * g : 32 * g + 32, cols], rows[:, cols])
+
+        def load_old(b, t):
+            o = big("old_t")
+            nc.sync.dma_start(o[:], old[b * KP : (b + 1) * KP, :].rearrange("(p t) c -> t p c", t=PACK)[t])
+            return o
+
+        nc.gpsimd.memset(tab_s[:].bitcast(I32), 0)
+        nc.gpsimd.memset(page[0][:], 0.0)
+        nc.gpsimd.memset(page[1][:], 0.0)
+        nc.gpsimd.memset(w4_s[:].rearrange("p a n -> p (a n)").bitcast(I32), 0)
+        nc.gpsimd.memset(page[2][:], 0.0)
+        nc.gpsimd.memset(page[3][:], 0.0)
+        nc.sync.dma_start(idx[:], offs)
+        for q in range(4):
+            nc.scalar.dma_start(
+                tab_s[32 * q : 32 * q + 8, :].bitcast(I32),
+                tab_scales[:, 4 * q : 4 * q + 4, :].bitcast(I32),
+            )
+        tab_words_i = tab_words.rearrange("a p t i -> a p (t i)").bitcast(I32)
+        nc.sync.dma_start(b1_t[:, :, 0:PACK], b1.rearrange("(b p t) -> p b t", b=2, t=PACK))
+        nc.sync.dma_start(idx2[:], offs2)
+        load_wg(0, slice(0, BANK), (0,))
+        nc.sync.dma_start(tab_w[0][:], tab_words_i[0])
+        raw00 = load_w1(0, 0)
+        load_wg(0, slice(0, BANK), (2, 1))
+        nc.sync.dma_start(tab_w[1][:], tab_words_i[1])
+        raw10 = []
+        for e in range(2):
+            rawh = ring.tile([P, PACK, KP // 2], F32, name="rawh", tag="rawh", bufs=2)
+            nc.sync.dma_start(
+                rawh[:],
+                w1[KP : 2 * KP, e * 256 : (e + 1) * 256].rearrange("(p j) c -> p j c", j=PACK),
+            )
+            raw10.append(rawh)
+        load_wg(0, slice(0, BANK), (3,))
+
+        def half(lst, e):
+            return lst[:, e * 32 : (e + 1) * 32]
+
+        for e in range(2):
+            nc.vector.tensor_copy(v_w[0][e][:], tab_w[0][:].bitcast(U32).indirect(half(idx, e)))
+        for e in range(2):
+            nc.vector.tensor_copy(v_s[e][:], tab_s[:].indirect(half(idx, e)))
+        nc.vector.tensor_copy(v_w[1][0][:], tab_w[1][:].bitcast(U32).indirect(half(idx, 0)))
+        quant_w1(0, 0, raw00)
+        g10 = ring.tile([P, PACK * KP], BF16, name="w1_g", tag="g", bufs=3, align_bytes=64)
+        g10v = g10[:].rearrange("p (t m j) -> p m j t", t=PACK, j=PACK)
+        nc.scalar.copy(g10v[:, 0:64], raw10[0][:].rearrange("p j (m t) -> p m j t", t=PACK))
+        nc.vector.tensor_copy(g10v[:, 64:128], raw10[1][:].rearrange("p j (m t) -> p m j t", t=PACK))
+        nc.vector.quantize_mx(w1_c[1][0][:, 0:P].bitcast(FP8X4), w1_s[1][0][:, 0:P], g10[:, 0:KP])
+        nc.vector.tensor_copy(v_w[1][1][:], tab_w[1][:].bitcast(U32).indirect(half(idx, 1)))
+        nc.vector.quantize_mx(w1_c[1][0][:, P : 2 * P].bitcast(FP8X4), w1_s[1][0][:, P : 2 * P], g10[:, KP : 2 * KP])
+        nc.vector.quantize_mx(w1_c[1][0][:, 2 * P :].bitcast(FP8X4), w1_s[1][0][:, 2 * P :], g10[:, 2 * KP :])
+
+        olds = {}
+        load_wg(0, slice(BANK, S))
+        load_wg(1, slice(0, S))
+        olds[0, 0] = load_old(0, 0)
+        raw01 = load_w1(0, 1)
+        load_wg(2, slice(0, S))
+        raw11 = load_w1(1, 1)
+        olds[0, 1] = load_old(0, 1)
+        load_wg(3, slice(0, S))
+        olds[0, 2] = load_old(0, 2)
+        olds[0, 3] = load_old(0, 3)
+        nc.sync.dma_start(
+            w4_w[:].bitcast(I32), w4_words.rearrange("a p n -> p a n").bitcast(I32)
+        )
+        for q in range(4):
+            nc.sync.dma_start(
+                w4_s[32 * q : 32 * q + 4, :, :].bitcast(I32),
+                w4_scales[:, 4 * q : 4 * q + 4, :].rearrange("a r n -> r a n").bitcast(I32),
+            )
+        with nc.allow_non_contiguous_dma(reason="one bias value a partition"):
+            nc.sync.dma_start(b4_t[:, :, 0:1], b4.rearrange("(i p o) -> p i o", p=P, o=1))
+
+        def stage1(b, t):
+            h = ring.tile([P, S], F32, name="h", tag="h", bufs=2)
+            for e in range(2):
+                acc = psum.tile([P, BANK], F32, name="acc", tag="bank")
+                order = (0, 1) if (b, t) == (0, 0) else (1, 0)
+                for a in order:
+                    nc.tensor.matmul_mx(
+                        acc[:],
+                        lhsT=w1_c[a][b][:, t * P : (t + 1) * P].bitcast(FP8X4),
+                        lhsT_scale=w1_s[a][b][:, t * P : (t + 1) * P],
+                        rhs=v_w[a][e][:].bitcast(FP8X4),
+                        rhs_scale=v_s[e][4 * a :, :],
+                        start=(a == order[0]),
+                        stop=(a == order[1]),
+                    )
+                nc.scalar.activation(h[:, e * BANK : (e + 1) * BANK], acc[:], ACT.Abs, bias=b1_t[:, b, t : t + 1])
+            return h
+
+        def scatter(b, t, h):
+            if (b, t) == (0, 0):
+                for e in range(2):
+                    cols = slice(e * BANK, (e + 1) * BANK)
+                    nc.vector.tensor_tensor(page[t][:].indirect(half(idx2, e)), h[:, cols], wg[t][:, cols], ALU.mult)
+            else:
+                nc.vector.tensor_tensor(page[t][:].indirect(idx2[:]), h[:], wg[t][:], ALU.mult)
+
+        def interleave(planes, split):
+            zi = ring.tile([P, PACK * BANK], BF16, name="zi", tag="g", bufs=3, align_bytes=64)
+            dst = zi[:].rearrange("p (c i t) -> p c t i", i=4, t=PACK)
+            src = planes.rearrange("p t (c i) -> p c t i", i=4)
+            if split < P:
+                nc.scalar.copy(dst[:, split:], src[:, split:])
+            if split > 0:
+                nc.vector.tensor_copy(dst[:, :split], src[:, :split])
+            return zi
+
+        def quant_z(b, c, zi):
+            nc.vector.quantize_mx(z_c[b][c][:].bitcast(FP8X4), z_s[b][c][:], zi[:])
+
+        for t in range(PACK):
+            h = stage1(0, t)
+            scatter(0, t, h)
+            if t > 0:
+                nc.vector.tensor_tensor(z0[:, t - 1, :], page[t - 1][:], olds[0, t - 1][:], ALU.max)
+            if t == 1:
+                quant_w1(0, 1, raw01)
+            if t == 2:
+                quant_w1(1, 1, raw11)
+        for c in range(nch):
+            o = big("old_c")
+            olds[1, c] = o[:].rearrange("p (t c) -> p t c", t=PACK)
+            nc.sync.dma_start(
+                olds[1, c], old[KP:, c * BANK : (c + 1) * BANK].rearrange("(p t) c -> p t c", t=PACK)
+            )
+        for t in range(PACK):
+            h = stage1(1, t)
+            scatter(1, t, h)
+            if t == 0:
+                nc.vector.tensor_tensor(z0[:, PACK - 1, :], page[PACK - 1][:], olds[0, PACK - 1][:], ALU.max)
+            zi = interleave(z0[:, :, t * BANK : (t + 1) * BANK], 0)
+            quant_z(0, t, zi)
+
+        def mm2(acc, b, c, n):
+            nc.tensor.matmul_mx(
+                acc[:],
+                lhsT=w4_w[:, b, 2 * n * P : 2 * (n + 1) * P].bitcast(FP4X4),
+                lhsT_scale=w4_s[:, b, n * P : (n + 1) * P],
+                rhs=z_c[b][c][:].bitcast(FP8X4),
+                rhs_scale=z_s[b][c][:],
+                start=(b == 0),
+                stop=(b == 1),
+            )
+
+        def open_chunk(c):
+            accs = []
+            for n in range(N // P):
+                acc = psum.tile([P, BANK], F32, name="acc2", tag="bank")
+                mm2(acc, 0, c, n)
+                accs.append(acc)
+            return accs
+
+        def max_chunk(c):
+            cols = slice(c * BANK, (c + 1) * BANK)
+            zf = ring.tile([P, S], F32, name="z1", tag="h", bufs=2)
+            planes = zf[:].bitcast(BF16).rearrange("p (t c) -> p t c", t=PACK)
+            for t in range(PACK):
+                nc.vector.tensor_tensor(planes[:, t, :], page[t][:, cols], olds[1, c][:, t, :], ALU.max)
+            return planes
+
+        def close_chunk(c, accs):
+            cols = slice(c * BANK, (c + 1) * BANK)
+            for n in range(N // P):
+                mm2(accs[n], 1, c, n)
+            for n in range(N // P):
+                y = ring.tile([P, BANK], F32, name="y", tag="y", bufs=6)
+                if c == nch - 1 and n % 2 == 1:
+                    nc.vector.tensor_scalar(y[:], accs[n][:], b4_t[:, n, 0:1], None, ALU.add)
+                else:
+                    nc.scalar.activation(y[:], accs[n][:], ACT.Identity, bias=b4_t[:, n, 0:1])
+                nc.sync.dma_start(out[n * P : (n + 1) * P, cols], y[:])
+
+        accs = {0: open_chunk(0), 1: open_chunk(1)}
+        zi = interleave(max_chunk(0), 48)
+        for c in range(nch):
+            if c + 1 < nch:
+                planes = max_chunk(c + 1)
+            quant_z(1, c, zi)
+            if c + 1 < nch:
+                zi = interleave(planes, 48 if c + 2 < nch else P)
+            close_chunk(c, accs[c])
+            if c + 2 < nch:
+                accs[c + 2] = open_chunk(c + 2)

@@ -34,7 +34,8 @@ def tile_list_recommender_slot_memory_kernel(
         idx2 = held.tile([P, S // 16], U16, name="idx2")
         tab_w = [held.tile([P, T], I32, name="tab_w%d" % a, align_bytes=64) for a in range(2)]
         tab_s = held.tile([P, T], U8, name="tab_s", align_bytes=64)
-        v_w = [[held.tile([P, BANK], U32, name="v_w%d%d" % (a, e), align_bytes=64) for e in range(2)] for a in range(2)]
+        v_w = [[held.tile([P, BANK], U32, name="v_w%d%d" % (a, e), align_bytes=64) for e in range(2 - a)] for a in range(2)]
+        v_w[1].append(None)
         v_s = [held.tile([P, BANK], U8, name="v_s%d" % e, align_bytes=64) for e in range(2)]
         w1_c = [[held.tile([P, KP], U32, name="w1_c%d%d" % (a, b), align_bytes=64) for b in range(2)] for a in range(2)]
         w1_s = [[held.tile([P, KP], U8, name="w1_s%d%d" % (a, b), align_bytes=64) for b in range(2)] for a in range(2)]
@@ -43,7 +44,7 @@ def tile_list_recommender_slot_memory_kernel(
         b4_t = held.tile([P, 4, 8], F32, name="b4_t")
         w4_w = held.tile([P, 2, 2 * N], U8, name="w4_w", align_bytes=64)
         w4_s = held.tile([P, 2, N], U8, name="w4_s", align_bytes=64)
-        page = [held.tile([P, T2], F32, name="page%d" % t) for t in range(PACK)]
+        page = []
         z0 = held.tile([P, PACK, T2], BF16, name="z0")
         nch = T2 // BANK
         z_c = [[held.tile([P, BANK], U32, name="z_c%d%d" % (b, c), align_bytes=64) for c in range(nch)] for b in range(2)]
@@ -63,8 +64,8 @@ def tile_list_recommender_slot_memory_kernel(
         def quant_w1(a, b, raw):
             g = ring.tile([P, PACK * KP], BF16, name="w1_g", tag="g", bufs=3, align_bytes=64)
             nc.scalar.copy(
-                g[:].rearrange("p (t m j) -> p m j t", t=PACK, j=PACK),
-                raw[:].rearrange("p (j m t) -> p m j t", j=PACK, t=PACK),
+                g[:].rearrange("p (u e m j) -> p u m j e", u=2, e=2, j=PACK),
+                raw[:].rearrange("p (j m u e) -> p u m j e", j=PACK, u=2, e=2),
             )
             nc.vector.quantize_mx(w1_c[a][b][:].bitcast(FP8X4), w1_s[a][b][:], g[:])
 
@@ -79,11 +80,10 @@ def tile_list_recommender_slot_memory_kernel(
             return o
 
         nc.gpsimd.memset(tab_s[:].bitcast(I32), 0)
-        nc.gpsimd.memset(page[0][:], 0.0)
-        nc.gpsimd.memset(page[1][:], 0.0)
-        nc.gpsimd.memset(w4_s[:].rearrange("p a n -> p (a n)").bitcast(I32), 0)
-        nc.gpsimd.memset(page[2][:], 0.0)
-        nc.gpsimd.memset(page[3][:], 0.0)
+        for t in range(2):
+            page.append(held.tile([P, T2], F32, name="page%d" % t))
+            nc.vector.memset(page[t][:], 0.0)
+        nc.vector.memset(w4_s[:].rearrange("p a n -> p (a n)").bitcast(I32), 0)
         nc.sync.dma_start(idx[:], offs)
         for q in range(4):
             nc.scalar.dma_start(
@@ -96,7 +96,6 @@ def tile_list_recommender_slot_memory_kernel(
         load_wg(0, slice(0, BANK), (0,))
         nc.sync.dma_start(tab_w[0][:], tab_words_i[0])
         raw00 = load_w1(0, 0)
-        load_wg(0, slice(0, BANK), (2, 1))
         nc.sync.dma_start(tab_w[1][:], tab_words_i[1])
         raw10 = []
         for e in range(2):
@@ -106,7 +105,7 @@ def tile_list_recommender_slot_memory_kernel(
                 w1[KP : 2 * KP, e * 256 : (e + 1) * 256].rearrange("(p j) c -> p j c", j=PACK),
             )
             raw10.append(rawh)
-        load_wg(0, slice(0, BANK), (3,))
+        load_wg(0, slice(0, BANK), (2, 1, 3))
 
         def half(lst, e):
             return lst[:, e * 32 : (e + 1) * 32]
@@ -117,14 +116,24 @@ def tile_list_recommender_slot_memory_kernel(
             nc.vector.tensor_copy(v_s[e][:], tab_s[:].indirect(half(idx, e)))
         nc.vector.tensor_copy(v_w[1][0][:], tab_w[1][:].bitcast(U32).indirect(half(idx, 0)))
         quant_w1(0, 0, raw00)
-        g10 = ring.tile([P, PACK * KP], BF16, name="w1_g", tag="g", bufs=3, align_bytes=64)
-        g10v = g10[:].rearrange("p (t m j) -> p m j t", t=PACK, j=PACK)
-        nc.scalar.copy(g10v[:, 0:64], raw10[0][:].rearrange("p j (m t) -> p m j t", t=PACK))
-        nc.vector.tensor_copy(g10v[:, 64:128], raw10[1][:].rearrange("p j (m t) -> p m j t", t=PACK))
-        nc.vector.quantize_mx(w1_c[1][0][:, 0:P].bitcast(FP8X4), w1_s[1][0][:, 0:P], g10[:, 0:KP])
+        g10a = ring.tile([P, KP], BF16, name="w1_ga", tag="ga", bufs=1, align_bytes=64)
+        g10b = ring.tile([P, PACK * KP], BF16, name="w1_g", tag="g", bufs=3, align_bytes=64)
+        ga = g10a[:].rearrange("p (m j) -> p m j", j=PACK)
+        gb = g10b[:].rearrange("p (t m j) -> p t m j", t=PACK, j=PACK)
+        halves = [r[:].rearrange("p j (m t) -> p t m j", t=PACK) for r in raw10]
+        nc.scalar.copy(ga[:, 0:64], halves[0][:, 0])
+        nc.vector.tensor_copy(ga[:, 64:128], halves[1][:, 0])
+        nc.vector.quantize_mx(w1_c[1][0][:, 0:P].bitcast(FP8X4), w1_s[1][0][:, 0:P], g10a[:])
+        v_w[1][1] = ring.tile([P, BANK], U32, name="v_w11", tag="ga", bufs=1, align_bytes=64)
         nc.vector.tensor_copy(v_w[1][1][:], tab_w[1][:].bitcast(U32).indirect(half(idx, 1)))
-        nc.vector.quantize_mx(w1_c[1][0][:, P : 2 * P].bitcast(FP8X4), w1_s[1][0][:, P : 2 * P], g10[:, KP : 2 * KP])
-        nc.vector.quantize_mx(w1_c[1][0][:, 2 * P :].bitcast(FP8X4), w1_s[1][0][:, 2 * P :], g10[:, 2 * KP :])
+        for e in range(2):
+            m = slice(64 * e, 64 * (e + 1))
+            nc.scalar.copy(gb[:, 1, m], halves[e][:, 1])
+            nc.scalar.copy(
+                gb[:, 2:4, m].rearrange("p t m j -> p m j t"), halves[e][:, 2:4].rearrange("p t m j -> p m j t")
+            )
+        nc.vector.quantize_mx(w1_c[1][0][:, P : 2 * P].bitcast(FP8X4), w1_s[1][0][:, P : 2 * P], g10b[:, KP : 2 * KP])
+        nc.vector.quantize_mx(w1_c[1][0][:, 2 * P :].bitcast(FP8X4), w1_s[1][0][:, 2 * P :], g10b[:, 2 * KP :])
 
         olds = {}
         load_wg(0, slice(BANK, S))
@@ -149,7 +158,10 @@ def tile_list_recommender_slot_memory_kernel(
             nc.sync.dma_start(b4_t[:, :, 0:1], b4.rearrange("(i p o) -> p i o", p=P, o=1))
 
         def stage1(b, t):
-            h = ring.tile([P, S], F32, name="h", tag="h", bufs=2)
+            if b == 0 and t < 2:
+                h = ring.tile([P, S], F32, name="h_early", tag="late_page%d" % t, bufs=1)
+            else:
+                h = ring.tile([P, S], F32, name="h", tag="h", bufs=2)
             for e in range(2):
                 acc = psum.tile([P, BANK], F32, name="acc", tag="bank")
                 order = (0, 1) if (b, t) == (0, 0) else (1, 0)
@@ -175,21 +187,25 @@ def tile_list_recommender_slot_memory_kernel(
                 nc.vector.tensor_tensor(page[t][:].indirect(idx2[:]), h[:], wg[t][:], ALU.mult)
 
         def interleave(planes, split):
+            width = planes.shape[2]
             zi = ring.tile([P, PACK * BANK], BF16, name="zi", tag="g", bufs=3, align_bytes=64)
-            dst = zi[:].rearrange("p (c i t) -> p c t i", i=4, t=PACK)
+            dst = zi[:, : PACK * width].rearrange("p (c i t) -> p c t i", i=4, t=PACK)
             src = planes.rearrange("p t (c i) -> p c t i", i=4)
-            if split < P:
+            if split < width // 4:
                 nc.scalar.copy(dst[:, split:], src[:, split:])
             if split > 0:
                 nc.vector.tensor_copy(dst[:, :split], src[:, :split])
-            return zi
+            return zi[:, : PACK * width]
 
-        def quant_z(b, c, zi):
-            nc.vector.quantize_mx(z_c[b][c][:].bitcast(FP8X4), z_s[b][c][:], zi[:])
+        def quant_z(b, c, zi, lo=0, width=BANK):
+            nc.vector.quantize_mx(z_c[b][c][:, lo : lo + width].bitcast(FP8X4), z_s[b][c][:, lo : lo + width], zi)
 
         for t in range(PACK):
             h = stage1(0, t)
             scatter(0, t, h)
+            if t < 2:
+                page.append(ring.tile([P, T2], F32, name="page%d" % (t + 2), tag="late_page%d" % t, bufs=1))
+                nc.gpsimd.memset(page[t + 2][:], 0.0)
             if t > 0:
                 nc.vector.tensor_tensor(z0[:, t - 1, :], page[t - 1][:], olds[0, t - 1][:], ALU.max)
             if t == 1:
@@ -210,53 +226,74 @@ def tile_list_recommender_slot_memory_kernel(
             zi = interleave(z0[:, :, t * BANK : (t + 1) * BANK], 0)
             quant_z(0, t, zi)
 
-        def mm2(acc, b, c, n):
+        def mm2(acc, b, c, n, lo, width, start, stop):
             nc.tensor.matmul_mx(
-                acc[:],
+                acc,
                 lhsT=w4_w[:, b, 2 * n * P : 2 * (n + 1) * P].bitcast(FP4X4),
                 lhsT_scale=w4_s[:, b, n * P : (n + 1) * P],
-                rhs=z_c[b][c][:].bitcast(FP8X4),
-                rhs_scale=z_s[b][c][:],
-                start=(b == 0),
-                stop=(b == 1),
+                rhs=z_c[b][c][:, lo : lo + width].bitcast(FP8X4),
+                rhs_scale=z_s[b][c][:, lo : lo + width],
+                start=start,
+                stop=stop,
             )
 
-        def open_chunk(c):
-            accs = []
-            for n in range(N // P):
-                acc = psum.tile([P, BANK], F32, name="acc2", tag="bank")
-                mm2(acc, 0, c, n)
-                accs.append(acc)
+        def run_pass(b, c, lo, width, accs):
+            if width == BANK:
+                for n in range(N // P):
+                    mm2(accs[n][:], b, c, n, 0, BANK, b == 0, b == 1)
+            else:
+                for n in range(N // P):
+                    for i in range(2):
+                        at = (n % 2) * 256 + i * P
+                        mm2(accs[n // 2][:, at : at + P], b, c, n, lo + i * P, P, b == 0 and at == 0, b == 1 and at == 3 * P)
+
+        def open_piece(c, lo, width):
+            accs = [psum.tile([P, BANK], F32, name="acc2", tag="bank") for n in range(width // P)]
+            run_pass(0, c, lo, width, accs)
             return accs
 
-        def max_chunk(c):
-            cols = slice(c * BANK, (c + 1) * BANK)
+        def max_piece(c, lo, width):
+            cols = slice(c * BANK + lo, c * BANK + lo + width)
             zf = ring.tile([P, S], F32, name="z1", tag="h", bufs=2)
-            planes = zf[:].bitcast(BF16).rearrange("p (t c) -> p t c", t=PACK)
+            planes = zf[:].bitcast(BF16)[:, : PACK * width].rearrange("p (t c) -> p t c", t=PACK)
             for t in range(PACK):
-                nc.vector.tensor_tensor(planes[:, t, :], page[t][:, cols], olds[1, c][:, t, :], ALU.max)
+                nc.vector.tensor_tensor(planes[:, t, :], page[t][:, cols], olds[1, c][:, t, lo : lo + width], ALU.max)
             return planes
 
-        def close_chunk(c, accs):
-            cols = slice(c * BANK, (c + 1) * BANK)
-            for n in range(N // P):
-                mm2(accs[n], 1, c, n)
-            for n in range(N // P):
+        def close_piece(c, lo, width, accs):
+            cols = slice(c * BANK + lo, c * BANK + lo + width)
+            run_pass(1, c, lo, width, accs)
+            for k in range(len(accs)):
                 y = ring.tile([P, BANK], F32, name="y", tag="y", bufs=6)
-                if c == nch - 1 and n % 2 == 1:
-                    nc.vector.tensor_scalar(y[:], accs[n][:], b4_t[:, n, 0:1], None, ALU.add)
+                if width == BANK:
+                    nc.scalar.activation(y[:], accs[k][:], ACT.Identity, bias=b4_t[:, k, 0:1])
+                    nc.sync.dma_start(out[k * P : (k + 1) * P, cols], y[:])
                 else:
-                    nc.scalar.activation(y[:], accs[n][:], ACT.Identity, bias=b4_t[:, n, 0:1])
-                nc.sync.dma_start(out[n * P : (n + 1) * P, cols], y[:])
+                    for i in range(2):
+                        n = 2 * k + i
+                        part = slice(i * width, (i + 1) * width)
+                        if k == 0:
+                            nc.scalar.activation(y[:, part], accs[k][:, part], ACT.Identity, bias=b4_t[:, n, 0:1])
+                        else:
+                            nc.vector.tensor_scalar(y[:, part], accs[k][:, part], b4_t[:, n, 0:1], None, ALU.add)
+                    nc.sync.dma_start(
+                        out[2 * k * P : 2 * (k + 1) * P, cols].rearrange("(i p) c -> p i c", i=2),
+                        y[:].rearrange("p (i c) -> p i c", i=2),
+                    )
 
-        accs = {0: open_chunk(0), 1: open_chunk(1)}
-        zi = interleave(max_chunk(0), 48)
-        for c in range(nch):
-            if c + 1 < nch:
-                planes = max_chunk(c + 1)
-            quant_z(1, c, zi)
-            if c + 1 < nch:
-                zi = interleave(planes, 48 if c + 2 < nch else P)
-            close_chunk(c, accs[c])
-            if c + 2 < nch:
-                accs[c + 2] = open_chunk(c + 2)
+        pieces = [(0, 0, BANK), (1, 0, BANK), (2, 0, BANK), (3, 0, 256), (3, 256, 256)]
+        splits = [32, 32, 32, 64, 64]
+        accs = {0: open_piece(*pieces[0]), 1: open_piece(*pieces[1])}
+        zi = interleave(max_piece(*pieces[0]), splits[0])
+        for k, (c, lo, width) in enumerate(pieces):
+            if k + 1 < len(pieces):
+                planes = max_piece(*pieces[k + 1])
+            quant_z(1, c, zi, lo, width)
+            if k + 1 < len(pieces):
+                zi = interleave(planes, splits[k + 1])
+            close_piece(c, lo, width, accs[k])
+            if k == 0:
+                accs[2] = open_piece(*pieces[2])
+            if k == 1:
+                accs[3] = open_piece(*pieces[3])
+                accs[4] = open_piece(*pieces[4])

@@ -1,12 +1,15 @@
 from contextlib import ExitStack
 
 import concourse.mybir as mybir
+from concourse.masks import make_identity
 
 K, T, S, T2, H, N = 1024, 2048, 1024, 2048, 1024, 512
 P = 128
 PACK = 4
 KP = P * PACK
 BANK = 512
+CHUNKS = T2 // BANK
+TURNED = 2
 FLOPS = 2 * K * H * S + 2 * H * N * T2
 
 F32 = mybir.dt.float32
@@ -27,128 +30,105 @@ def tile_list_recommender_slot_memory_kernel(
     nc = tc.nc
     with ExitStack() as ctx:
         held = ctx.enter_context(tc.tile_pool(name="held", bufs=1))
-        ring = ctx.enter_context(tc.tile_pool(name="ring", bufs=1))
-        psum = ctx.enter_context(tc.psum_pool(name="psum", bufs=8))
+        sb = ctx.enter_context(tc.tile_pool(name="sb", bufs=1))
+        psum = ctx.enter_context(tc.psum_pool(name="psum", bufs=1))
+
+        def tenant(slot, name, shape, dtype, bufs=1):
+            return sb.tile(shape, dtype, name=name, tag=slot, bufs=bufs, align_bytes=64)
 
         idx = held.tile([P, S // 16], U16, name="idx")
         idx2 = held.tile([P, S // 16], U16, name="idx2")
-        tab_w = [held.tile([P, T], I32, name="tab_w%d" % a, align_bytes=64) for a in range(2)]
-        tab_s = held.tile([P, T], U8, name="tab_s", align_bytes=64)
-        v_w = [[held.tile([P, BANK], U32, name="v_w%d%d" % (a, e), align_bytes=64) for e in range(2 - a)] for a in range(2)]
-        v_w[1].append(None)
-        v_s = [held.tile([P, BANK], U8, name="v_s%d" % e, align_bytes=64) for e in range(2)]
-        w1_c = [[held.tile([P, KP], U32, name="w1_c%d%d" % (a, b), align_bytes=64) for b in range(2)] for a in range(2)]
-        w1_s = [[held.tile([P, KP], U8, name="w1_s%d%d" % (a, b), align_bytes=64) for b in range(2)] for a in range(2)]
-        wg = [held.tile([P, S], F32, name="wg%d" % t) for t in range(PACK)]
+        v_w0 = held.tile([P, S], U32, name="v_w0", align_bytes=64)
+        w1_c = held.tile([P, 2, 2, KP], U32, name="w1_c", align_bytes=64)
+        v_s = held.tile([P, S], U8, name="v_s", align_bytes=64)
+        w1_s = {(a, 1): held.tile([P, KP], U8, name="w1_s%d1" % a, align_bytes=64) for a in range(2)}
         b1_t = held.tile([P, 2, 8], F32, name="b1_t")
         b4_t = held.tile([P, 4, 8], F32, name="b4_t")
         w4_w = held.tile([P, 2, 2 * N], U8, name="w4_w", align_bytes=64)
         w4_s = held.tile([P, 2, N], U8, name="w4_s", align_bytes=64)
-        page = []
-        z0 = held.tile([P, PACK, T2], BF16, name="z0")
-        nch = T2 // BANK
-        z_c = [[held.tile([P, BANK], U32, name="z_c%d%d" % (b, c), align_bytes=64) for c in range(nch)] for b in range(2)]
-        z_s = [[held.tile([P, BANK], U8, name="z_s%d%d" % (b, c), align_bytes=64) for c in range(nch)] for b in range(2)]
-
-        def big(name):
-            return ring.tile([P, T2], F32, name=name, tag="big", bufs=7)
+        ident = held.tile([P, P], F32, name="ident")
+        z_s = [[held.tile([P, BANK], U8, name="z_s%d%d" % (b, c), align_bytes=64) for c in range(CHUNKS)] for b in range(2)]
+        z0 = held.tile([P, CHUNKS - TURNED, PACK, BANK], BF16, name="z0")
+        page = [held.tile([P, T2], F32, name="page%d" % t) for t in range(2)]
+        wg = [tenant("wg%d" % t, "wg%d" % t, [P, S], F32) for t in range(PACK)]
+        tab_w = [tenant("tab_w%d" % a, "tab_w%d" % a, [P, T], I32) for a in range(2)]
+        tab_s = tenant("tab_s", "tab_s", [P, T], U8)
 
         def load_w1(a, b):
-            raw = big("w1_raw")
+            raw = tenant("raw", "w1_raw", [P, PACK, KP], F32, bufs=2)
             nc.sync.dma_start(
-                raw[:].rearrange("p (j c) -> p j c", j=PACK),
-                w1[a * KP : (a + 1) * KP, b * KP : (b + 1) * KP].rearrange("(p j) c -> p j c", j=PACK),
+                raw[:], w1[a * KP : (a + 1) * KP, b * KP : (b + 1) * KP].rearrange("(p j) c -> p j c", j=PACK)
             )
-            return raw
+            return raw[:].rearrange("p j (m u e) -> p u m j e", u=2, e=2)
 
-        def quant_w1(a, b, raw):
-            g = ring.tile([P, PACK * KP], BF16, name="w1_g", tag="g", bufs=3, align_bytes=64)
-            nc.scalar.copy(
-                g[:].rearrange("p (u e m j) -> p u m j e", u=2, e=2, j=PACK),
-                raw[:].rearrange("p (j m u e) -> p u m j e", j=PACK, u=2, e=2),
-            )
-            nc.vector.quantize_mx(w1_c[a][b][:].bitcast(FP8X4), w1_s[a][b][:], g[:])
-
-        def load_wg(t, cols, groups=(0, 2, 1, 3)):
+        def load_wg(t, cols):
             rows = wgs.rearrange("(q t) s -> t q s", t=PACK)[t]
-            for g in groups:
+            for g in (0, 2, 1, 3):
                 nc.sync.dma_start(wg[t][32 * g : 32 * g + 32, cols], rows[:, cols])
 
-        def load_old(b, t):
-            o = big("old_t")
-            nc.sync.dma_start(o[:], old[b * KP : (b + 1) * KP, :].rearrange("(p t) c -> t p c", t=PACK)[t])
+        def load_old(t, slot, cols):
+            o = tenant(slot, "old_rows", [P, cols.stop - cols.start], F32)
+            nc.sync.dma_start(o[:], old[:KP, cols].rearrange("(p t) c -> t p c", t=PACK)[t])
             return o
 
         nc.gpsimd.memset(tab_s[:].bitcast(I32), 0)
-        for t in range(2):
-            page.append(held.tile([P, T2], F32, name="page%d" % t))
-            nc.vector.memset(page[t][:], 0.0)
-        nc.vector.memset(w4_s[:].rearrange("p a n -> p (a n)").bitcast(I32), 0)
-        nc.sync.dma_start(idx[:], offs)
         for q in range(4):
-            nc.scalar.dma_start(
+            queue = nc.gpsimd if q < 2 else nc.scalar
+            queue.dma_start(
                 tab_s[32 * q : 32 * q + 8, :].bitcast(I32),
                 tab_scales[:, 4 * q : 4 * q + 4, :].bitcast(I32),
             )
-        tab_words_i = tab_words.rearrange("a p t i -> a p (t i)").bitcast(I32)
+        for t in range(2):
+            nc.vector.memset(page[t][:], 0.0)
+        nc.vector.memset(w4_s[:].rearrange("p a n -> p (a n)").bitcast(I32), 0)
+        nc.sync.dma_start(idx[:], offs)
         nc.sync.dma_start(b1_t[:, :, 0:PACK], b1.rearrange("(b p t) -> p b t", b=2, t=PACK))
         nc.sync.dma_start(idx2[:], offs2)
-        load_wg(0, slice(0, BANK), (0,))
+        tab_words_i = tab_words.rearrange("a p t i -> a p (t i)").bitcast(I32)
         nc.sync.dma_start(tab_w[0][:], tab_words_i[0])
         raw00 = load_w1(0, 0)
         nc.sync.dma_start(tab_w[1][:], tab_words_i[1])
-        raw10 = []
-        for e in range(2):
-            rawh = ring.tile([P, PACK, KP // 2], F32, name="rawh", tag="rawh", bufs=2)
-            nc.sync.dma_start(
-                rawh[:],
-                w1[KP : 2 * KP, e * 256 : (e + 1) * 256].rearrange("(p j) c -> p j c", j=PACK),
-            )
-            raw10.append(rawh)
-        load_wg(0, slice(0, BANK), (2, 1, 3))
+        raw10 = load_w1(1, 0)
+        load_wg(0, slice(0, BANK))
 
-        def half(lst, e):
-            return lst[:, e * 32 : (e + 1) * 32]
+        def quant_w1(a, b, raw, slot):
+            g = tenant(slot, "w1_g", [P, PACK * KP], BF16)
+            nc.scalar.copy(g[:].rearrange("p (u e m j) -> p u m j e", u=2, e=2, j=PACK), raw)
+            nc.vector.quantize_mx(w1_c[:, a, b, :].bitcast(FP8X4), w1_s[a, b][:], g[:])
 
-        for e in range(2):
-            nc.vector.tensor_copy(v_w[0][e][:], tab_w[0][:].bitcast(U32).indirect(half(idx, e)))
-        for e in range(2):
-            nc.vector.tensor_copy(v_s[e][:], tab_s[:].indirect(half(idx, e)))
-        nc.vector.tensor_copy(v_w[1][0][:], tab_w[1][:].bitcast(U32).indirect(half(idx, 0)))
-        quant_w1(0, 0, raw00)
-        g10a = ring.tile([P, KP], BF16, name="w1_ga", tag="ga", bufs=1, align_bytes=64)
-        g10b = ring.tile([P, PACK * KP], BF16, name="w1_g", tag="g", bufs=3, align_bytes=64)
-        ga = g10a[:].rearrange("p (m j) -> p m j", j=PACK)
-        gb = g10b[:].rearrange("p (t m j) -> p t m j", t=PACK, j=PACK)
-        halves = [r[:].rearrange("p j (m t) -> p t m j", t=PACK) for r in raw10]
-        nc.scalar.copy(ga[:, 0:64], halves[0][:, 0])
-        nc.vector.tensor_copy(ga[:, 64:128], halves[1][:, 0])
-        nc.vector.quantize_mx(w1_c[1][0][:, 0:P].bitcast(FP8X4), w1_s[1][0][:, 0:P], g10a[:])
-        v_w[1][1] = ring.tile([P, BANK], U32, name="v_w11", tag="ga", bufs=1, align_bytes=64)
-        nc.vector.tensor_copy(v_w[1][1][:], tab_w[1][:].bitcast(U32).indirect(half(idx, 1)))
-        for e in range(2):
-            m = slice(64 * e, 64 * (e + 1))
-            nc.scalar.copy(gb[:, 1, m], halves[e][:, 1])
-            nc.scalar.copy(
-                gb[:, 2:4, m].rearrange("p t m j -> p m j t"), halves[e][:, 2:4].rearrange("p t m j -> p m j t")
-            )
-        nc.vector.quantize_mx(w1_c[1][0][:, P : 2 * P].bitcast(FP8X4), w1_s[1][0][:, P : 2 * P], g10b[:, KP : 2 * KP])
-        nc.vector.quantize_mx(w1_c[1][0][:, 2 * P :].bitcast(FP8X4), w1_s[1][0][:, 2 * P :], g10b[:, 2 * KP :])
+        nc.vector.tensor_copy(v_w0[:], tab_w[0][:].bitcast(U32).indirect(idx[:]))
+        nc.vector.tensor_copy(v_s[:], tab_s[:].indirect(idx[:]))
+        w1_s[0, 0] = tenant("tab_s", "w1_s00", [P, KP], U8)
+        quant_w1(0, 0, raw00, "first")
+        v_w1 = tenant("first", "v_w1", [P, S], U32)
+        nc.vector.tensor_copy(v_w1[:], tab_w[1][:].bitcast(U32).indirect(idx[:]))
+        v_w = [v_w0, v_w1]
+        g10 = [tenant("tab_w1", "w1_ga", [P, 2 * KP], BF16), tenant("g", "w1_gb", [P, 2 * KP], BF16, 4)]
+        nc.vector.tensor_copy(g10[0][:].rearrange("p (e m j) -> p m j e", e=2, j=PACK), raw10[:, 0])
+        nc.scalar.copy(g10[1][:].rearrange("p (e m j) -> p m j e", e=2, j=PACK), raw10[:, 1])
+        w1_s10 = []
+        for u, slot in enumerate(("chain0", "tab_w1")):
+            w1_s10.append(tenant(slot, "w1_s10", [P, 2 * P], U8))
+            nc.vector.quantize_mx(w1_c[:, 1, 0, 2 * u * P : 2 * (u + 1) * P].bitcast(FP8X4), w1_s10[u][:], g10[u][:])
+        make_identity(nc, ident[:])
 
-        olds = {}
+        left, right = slice(0, TURNED * BANK), slice(TURNED * BANK, T2)
+        old_a, old_b = {}, {}
         load_wg(0, slice(BANK, S))
+        old_b[0] = load_old(0, "chain1", right)
         load_wg(1, slice(0, S))
-        olds[0, 0] = load_old(0, 0)
+        old_a[0] = load_old(0, "left0", left)
         raw01 = load_w1(0, 1)
+        old_a[1] = load_old(1, "left1", left)
+        old_b[1] = load_old(1, "chain2", right)
         load_wg(2, slice(0, S))
         raw11 = load_w1(1, 1)
-        olds[0, 1] = load_old(0, 1)
+        old_a[2] = load_old(2, "left2", left)
+        old_b[2] = load_old(2, "chain3", right)
         load_wg(3, slice(0, S))
-        olds[0, 2] = load_old(0, 2)
-        olds[0, 3] = load_old(0, 3)
-        nc.sync.dma_start(
-            w4_w[:].bitcast(I32), w4_words.rearrange("a p n -> p a n").bitcast(I32)
-        )
+        old_a[3] = load_old(3, "left3", left)
+        old_b[3] = load_old(3, "chain4", right)
+        nc.sync.dma_start(w4_w[:].bitcast(I32), w4_words.rearrange("a p n -> p a n").bitcast(I32))
         for q in range(4):
             nc.sync.dma_start(
                 w4_s[32 * q : 32 * q + 4, :, :].bitcast(I32),
@@ -157,38 +137,51 @@ def tile_list_recommender_slot_memory_kernel(
         with nc.allow_non_contiguous_dma(reason="one bias value a partition"):
             nc.sync.dma_start(b4_t[:, :, 0:1], b4.rearrange("(i p o) -> p i o", p=P, o=1))
 
-        def stage1(b, t):
-            if b == 0 and t < 2:
-                h = ring.tile([P, S], F32, name="h_early", tag="late_page%d" % t, bufs=1)
-            else:
-                h = ring.tile([P, S], F32, name="h", tag="h", bufs=2)
+        def w1_scale(a, b, t):
+            if (a, b) == (1, 0):
+                return w1_s10[t // 2][:, (t % 2) * P : (t % 2 + 1) * P]
+            return w1_s[a, b][:, t * P : (t + 1) * P]
+
+        def first_product(s):
+            b, t = divmod(s, PACK)
+            accs = []
             for e in range(2):
-                acc = psum.tile([P, BANK], F32, name="acc", tag="bank")
-                order = (0, 1) if (b, t) == (0, 0) else (1, 0)
+                acc = psum.tile([P, BANK], F32, name="acc", tag="product", bufs=2)
+                order = (0, 1) if s == 0 else (1, 0)
+                cols = slice(e * BANK, (e + 1) * BANK)
                 for a in order:
                     nc.tensor.matmul_mx(
                         acc[:],
-                        lhsT=w1_c[a][b][:, t * P : (t + 1) * P].bitcast(FP8X4),
-                        lhsT_scale=w1_s[a][b][:, t * P : (t + 1) * P],
-                        rhs=v_w[a][e][:].bitcast(FP8X4),
-                        rhs_scale=v_s[e][4 * a :, :],
+                        lhsT=w1_c[:, a, b, t * P : (t + 1) * P].bitcast(FP8X4),
+                        lhsT_scale=w1_scale(a, b, t),
+                        rhs=v_w[a][:, cols].bitcast(FP8X4),
+                        rhs_scale=v_s[4 * a :, cols],
                         start=(a == order[0]),
                         stop=(a == order[1]),
                     )
-                nc.scalar.activation(h[:, e * BANK : (e + 1) * BANK], acc[:], ACT.Abs, bias=b1_t[:, b, t : t + 1])
+                accs.append(acc)
+            return accs
+
+        def magnitude(s, accs, slot):
+            b, t = divmod(s, PACK)
+            h = tenant(slot, "h", [P, S], F32)
+            for e in range(2):
+                nc.scalar.activation(h[:, e * BANK : (e + 1) * BANK], accs[e][:], ACT.Abs, bias=b1_t[:, b, t : t + 1])
             return h
 
-        def scatter(b, t, h):
-            if (b, t) == (0, 0):
+        def scatter(s, h):
+            t = s % PACK
+            if s == 0:
                 for e in range(2):
                     cols = slice(e * BANK, (e + 1) * BANK)
-                    nc.vector.tensor_tensor(page[t][:].indirect(half(idx2, e)), h[:, cols], wg[t][:, cols], ALU.mult)
+                    entries = idx2[:, e * 32 : (e + 1) * 32]
+                    nc.vector.tensor_tensor(page[t][:].indirect(entries), h[:, cols], wg[t][:, cols], ALU.mult)
             else:
                 nc.vector.tensor_tensor(page[t][:].indirect(idx2[:]), h[:], wg[t][:], ALU.mult)
 
         def interleave(planes, split):
             width = planes.shape[2]
-            zi = ring.tile([P, PACK * BANK], BF16, name="zi", tag="g", bufs=3, align_bytes=64)
+            zi = tenant("g", "zi", [P, PACK * BANK], BF16, 4)
             dst = zi[:, : PACK * width].rearrange("p (c i t) -> p c t i", i=4, t=PACK)
             src = planes.rearrange("p t (c i) -> p c t i", i=4)
             if split < width // 4:
@@ -197,103 +190,188 @@ def tile_list_recommender_slot_memory_kernel(
                 nc.vector.tensor_copy(dst[:, :split], src[:, :split])
             return zi[:, : PACK * width]
 
+        z_c = {}
+
         def quant_z(b, c, zi, lo=0, width=BANK):
-            nc.vector.quantize_mx(z_c[b][c][:, lo : lo + width].bitcast(FP8X4), z_s[b][c][:, lo : lo + width], zi)
+            nc.vector.quantize_mx(z_c[b, c][:, lo : lo + width].bitcast(FP8X4), z_s[b][c][:, lo : lo + width], zi)
 
-        for t in range(PACK):
-            h = stage1(0, t)
-            scatter(0, t, h)
-            if t < 2:
-                page.append(ring.tile([P, T2], F32, name="page%d" % (t + 2), tag="late_page%d" % t, bufs=1))
-                nc.gpsimd.memset(page[t + 2][:], 0.0)
-            if t > 0:
-                nc.vector.tensor_tensor(z0[:, t - 1, :], page[t - 1][:], olds[0, t - 1][:], ALU.max)
-            if t == 1:
-                quant_w1(0, 1, raw01)
-            if t == 2:
-                quant_w1(1, 1, raw11)
-        for c in range(nch):
-            o = big("old_c")
-            olds[1, c] = o[:].rearrange("p (t c) -> p t c", t=PACK)
-            nc.sync.dma_start(
-                olds[1, c], old[KP:, c * BANK : (c + 1) * BANK].rearrange("(p t) c -> p t c", t=PACK)
-            )
-        for t in range(PACK):
-            h = stage1(1, t)
-            scatter(1, t, h)
-            if t == 0:
-                nc.vector.tensor_tensor(z0[:, PACK - 1, :], page[PACK - 1][:], olds[0, PACK - 1][:], ALU.max)
-            zi = interleave(z0[:, :, t * BANK : (t + 1) * BANK], 0)
-            quant_z(0, t, zi)
+        def add_turned(dst, first, second):
+            nc.tensor.matmul(dst, first, ident[:], start=True, stop=False, is_transpose=True)
+            nc.tensor.matmul(dst, second, ident[:], start=False, stop=True, is_transpose=True)
 
-        def mm2(acc, b, c, n, lo, width, start, stop):
-            nc.tensor.matmul_mx(
-                acc,
-                lhsT=w4_w[:, b, 2 * n * P : 2 * (n + 1) * P].bitcast(FP4X4),
-                lhsT_scale=w4_s[:, b, n * P : (n + 1) * P],
-                rhs=z_c[b][c][:, lo : lo + width].bitcast(FP8X4),
-                rhs_scale=z_s[b][c][:, lo : lo + width],
-                start=start,
-                stop=stop,
+        turned = [tenant("turned%d" % c, "turned", [P, PACK, 2, BANK], F32) for c in range(TURNED)]
+
+        minus_old = {}
+
+        def negate_old(t):
+            minus_old[t] = tenant("chain%d" % t, "minus_old", [P, TURNED * BANK], F32)
+            nc.scalar.activation(minus_old[t][:], old_a[t][:], ACT.Copy, scale=-1.0)
+
+        def keep_larger(t):
+            nc.vector.tensor_tensor(
+                z0[:, :, t, :],
+                page[t][:, right].rearrange("p (c w) -> p c w", w=BANK),
+                old_b[t][:].rearrange("p (c w) -> p c w", w=BANK),
+                ALU.max,
             )
 
-        def run_pass(b, c, lo, width, accs):
-            if width == BANK:
-                for n in range(N // P):
-                    mm2(accs[n][:], b, c, n, 0, BANK, b == 0, b == 1)
-            else:
-                for n in range(N // P):
-                    for i in range(2):
-                        at = (n % 2) * 256 + i * P
-                        mm2(accs[n // 2][:, at : at + P], b, c, n, lo + i * P, P, b == 0 and at == 0, b == 1 and at == 3 * P)
+        def turn_slice(t):
+            o = minus_old[t]
+            for c in range(TURNED):
+                d_bank = psum.tile([P, BANK], F32, name="d_bank", tag="turn", bufs=4)
+                a_bank = psum.tile([P, BANK], F32, name="a_bank", tag="turn", bufs=4)
+                for i in range(4):
+                    cols = slice(c * BANK + i * P, c * BANK + (i + 1) * P)
+                    add_turned(d_bank[:, i * P : (i + 1) * P], o[:, cols], page[t][:, cols])
+                for i in range(4):
+                    cols = slice(c * BANK + i * P, c * BANK + (i + 1) * P)
+                    nc.tensor.transpose(a_bank[:, i * P : (i + 1) * P], page[t][:, cols], ident[:])
+                nc.scalar.activation(turned[c][:, t, 0, :], d_bank[:], ACT.Relu, scale=-1.0)
+                nc.scalar.copy(turned[c][:, t, 1, :], a_bank[:])
+
+        def turn_back(c):
+            zi = tenant("g", "zi", [P, PACK * BANK], BF16, 4)
+            for i in range(4):
+                z_bank = psum.tile([P, BANK], F32, name="z_bank", tag="turn", bufs=4)
+                blk = slice(i * P, (i + 1) * P)
+                for t in range(PACK):
+                    add_turned(z_bank[:, t * P : (t + 1) * P], turned[c][:, t, 1, blk], turned[c][:, t, 0, blk])
+                nc.scalar.copy(
+                    zi[:, i * BANK : (i + 1) * BANK].rearrange("p (c t) -> p c t", t=PACK),
+                    z_bank[:].rearrange("p (t c) -> p c t", t=PACK),
+                )
+            return zi[:]
+
+        def load_old_chunk(c):
+            o = tenant("chain%d" % c, "old_cols", [P, PACK, BANK], F32)
+            nc.sync.dma_start(o[:], old[KP:, c * BANK : (c + 1) * BANK].rearrange("(p t) c -> p t c", t=PACK))
+            return o
+
+        z_late = held.tile([P, 2, BANK], U32, name="z_late", align_bytes=64)
+        z_c[0, 2], z_c[0, 3] = z_late[:, 0, :], z_late[:, 1, :]
+        slices = 2 * PACK
+        acc1 = {s: first_product(s) for s in range(2)}
+        hs = {s: magnitude(s, acc1[s], "page%d" % (s + 2)) for s in range(2)}
+        negate_old(0)
+        old1, zi0 = {}, {}
+        for s in range(slices):
+            scatter(s, hs[s])
+            if s < 2:
+                page.append(tenant("page%d" % (s + 2), "late_page", [P, T2], F32))
+                nc.gpsimd.memset(page[s + 2][:], 0.0)
+            if s + 2 < slices:
+                acc1[s + 2] = first_product(s + 2)
+            if s < PACK:
+                keep_larger(s)
+                turn_slice(s)
+                hs[s + 2] = magnitude(s + 2, acc1[s + 2], "chain%d" % s)
+                if s + 1 < PACK:
+                    negate_old(s + 1)
+                if s < 2:
+                    quant_w1(s, 1, (raw01, raw11)[s], "left%d" % s)
+            elif s + 2 < slices:
+                c = s - PACK
+                quant_z(0, c + TURNED, interleave(z0[:, c], 0))
+                zi0[c] = turn_back(c)
+                hs[s + 2] = magnitude(s + 2, acc1[s + 2], "turned%d" % c)
+            if s == slices - 2 and TURNED == 3:
+                quant_z(0, 2, turn_back(2))
+            if 2 <= s < 2 + CHUNKS:
+                old1[s - 2] = load_old_chunk(s - 2)
+
+        z1 = tenant("turned1", "z1", [P, PACK * T2], BF16)
+        z_early = tenant("wg3", "z_early", [P, 2, BANK], U32)
+        z_c[0, 0], z_c[0, 1] = z_early[:, 0, :], z_early[:, 1, :]
+        z_second = tenant("tab_w0", "z_second", [P, CHUNKS, BANK], U32)
+        for c in range(CHUNKS):
+            z_c[1, c] = z_second[:, c, :]
+
+        def second_product(b, c, lo, width, accs):
+            for n in range(N // P):
+                steps = [(accs[n][:], 0, BANK, True, True)] if width == BANK else [
+                    (accs[n // 2][:, at : at + P], lo + at % 256, P, at == 0, at == 3 * P)
+                    for at in ((n % 2) * 256, (n % 2) * 256 + P)
+                ]
+                for acc, at, cols, first, last in steps:
+                    nc.tensor.matmul_mx(
+                        acc,
+                        lhsT=w4_w[:, b, 2 * n * P : 2 * (n + 1) * P].bitcast(FP4X4),
+                        lhsT_scale=w4_s[:, b, n * P : (n + 1) * P],
+                        rhs=z_c[b, c][:, at : at + cols].bitcast(FP8X4),
+                        rhs_scale=z_s[b][c][:, at : at + cols],
+                        start=(b == 0 and first),
+                        stop=(b == 1 and last),
+                    )
 
         def open_piece(c, lo, width):
-            accs = [psum.tile([P, BANK], F32, name="acc2", tag="bank") for n in range(width // P)]
-            run_pass(0, c, lo, width, accs)
+            accs = []
+            for n in range(width // P):
+                if (c, lo) == (3, 256) or (c == 1 and n >= 2):
+                    accs.append(psum.tile([P, BANK], F32, name="score", tag="product", bufs=2))
+                elif c % 2 == 1:
+                    accs.append(psum.tile([P, BANK], F32, name="score", tag="spare", bufs=2))
+                else:
+                    accs.append(psum.tile([P, BANK], F32, name="score", tag="turn", bufs=4))
+            second_product(0, c, lo, width, accs)
             return accs
 
         def max_piece(c, lo, width):
             cols = slice(c * BANK + lo, c * BANK + lo + width)
-            zf = ring.tile([P, S], F32, name="z1", tag="h", bufs=2)
-            planes = zf[:].bitcast(BF16)[:, : PACK * width].rearrange("p (t c) -> p t c", t=PACK)
+            planes = z1[:, PACK * cols.start : PACK * cols.stop].rearrange("p (t c) -> p t c", t=PACK)
             for t in range(PACK):
-                nc.vector.tensor_tensor(planes[:, t, :], page[t][:, cols], olds[1, c][:, t, lo : lo + width], ALU.max)
+                nc.vector.tensor_tensor(planes[:, t, :], page[t][:, cols], old1[c][:, t, lo : lo + width], ALU.max)
             return planes
 
-        def close_piece(c, lo, width, accs):
+        staged = {}
+
+        def close_piece(c, lo, width, accs, on_vector):
             cols = slice(c * BANK + lo, c * BANK + lo + width)
-            run_pass(1, c, lo, width, accs)
-            for k in range(len(accs)):
-                y = ring.tile([P, BANK], F32, name="y", tag="y", bufs=6)
+            second_product(1, c, lo, width, accs)
+            if lo == 0:
+                staged[c] = tenant("chain%d" % c, "y", [P, N // P * BANK], F32)
+            y = staged[c][:, 4 * lo : 4 * (lo + width)].rearrange("p (n c) -> p n c", n=N // P)
+            for k, acc in enumerate(accs):
                 if width == BANK:
-                    nc.scalar.activation(y[:], accs[k][:], ACT.Identity, bias=b4_t[:, k, 0:1])
-                    nc.sync.dma_start(out[k * P : (k + 1) * P, cols], y[:])
+                    if k in on_vector:
+                        nc.vector.tensor_scalar(y[:, k, :], acc[:], b4_t[:, k, 0:1], None, ALU.add)
+                    else:
+                        nc.scalar.activation(y[:, k, :], acc[:], ACT.Identity, bias=b4_t[:, k, 0:1])
+                    nc.sync.dma_start(out[k * P : (k + 1) * P, cols], y[:, k, :])
                 else:
                     for i in range(2):
                         n = 2 * k + i
-                        part = slice(i * width, (i + 1) * width)
-                        if k == 0:
-                            nc.scalar.activation(y[:, part], accs[k][:, part], ACT.Identity, bias=b4_t[:, n, 0:1])
+                        part = acc[:, i * width : (i + 1) * width]
+                        if k not in on_vector:
+                            nc.scalar.activation(y[:, n, :], part, ACT.Identity, bias=b4_t[:, n, 0:1])
                         else:
-                            nc.vector.tensor_scalar(y[:, part], accs[k][:, part], b4_t[:, n, 0:1], None, ALU.add)
+                            nc.vector.tensor_scalar(y[:, n, :], part, b4_t[:, n, 0:1], None, ALU.add)
                     nc.sync.dma_start(
-                        out[2 * k * P : 2 * (k + 1) * P, cols].rearrange("(i p) c -> p i c", i=2),
-                        y[:].rearrange("p (i c) -> p i c", i=2),
+                        out[2 * k * P : 2 * (k + 1) * P, cols].rearrange("(i p) c -> p i c", i=2), y[:, 2 * k : 2 * k + 2, :]
                     )
 
-        pieces = [(0, 0, BANK), (1, 0, BANK), (2, 0, BANK), (3, 0, 256), (3, 256, 256)]
-        splits = [32, 32, 32, 64, 64]
-        accs = {0: open_piece(*pieces[0]), 1: open_piece(*pieces[1])}
-        zi = interleave(max_piece(*pieces[0]), splits[0])
-        for k, (c, lo, width) in enumerate(pieces):
-            if k + 1 < len(pieces):
-                planes = max_piece(*pieces[k + 1])
-            quant_z(1, c, zi, lo, width)
-            if k + 1 < len(pieces):
-                zi = interleave(planes, splits[k + 1])
-            close_piece(c, lo, width, accs[k])
-            if k == 0:
-                accs[2] = open_piece(*pieces[2])
-            if k == 1:
-                accs[3] = open_piece(*pieces[3])
-                accs[4] = open_piece(*pieces[4])
+        pieces = [(0, 0, 512), (1, 0, 512), (2, 0, 512), (3, 0, 256), (3, 256, 256)]
+        splits = [56,56,56,64,64]
+        on_vector = [[],[],[],[1],[1]]
+        accs, zis = {}, {}
+        quant_z(0, 0, zi0[0])
+        accs[0] = open_piece(*pieces[0])
+        zis[0] = interleave(max_piece(*pieces[0]), splits[0])
+        quant_z(0, 1, zi0[1])
+        accs[1] = open_piece(*pieces[1])
+        quant_z(1, pieces[0][0], zis[0], pieces[0][1], pieces[0][2])
+        zis[1] = interleave(max_piece(*pieces[1]), splits[1])
+        close_piece(*pieces[0], accs[0], on_vector[0])
+        accs[2] = open_piece(*pieces[2])
+        quant_z(1, pieces[1][0], zis[1], pieces[1][1], pieces[1][2])
+        zis[2] = interleave(max_piece(*pieces[2]), splits[2])
+        close_piece(*pieces[1], accs[1], on_vector[1])
+        accs[3] = open_piece(*pieces[3])
+        accs[4] = open_piece(*pieces[4])
+        quant_z(1, pieces[2][0], zis[2], pieces[2][1], pieces[2][2])
+        zis[3] = interleave(max_piece(*pieces[3]), splits[3])
+        close_piece(*pieces[2], accs[2], on_vector[2])
+        quant_z(1, pieces[3][0], zis[3], pieces[3][1], pieces[3][2])
+        zis[4] = interleave(max_piece(*pieces[4]), splits[4])
+        close_piece(*pieces[3], accs[3], on_vector[3])
+        quant_z(1, pieces[4][0], zis[4], pieces[4][1], pieces[4][2])
+        close_piece(*pieces[4], accs[4], on_vector[4])

@@ -9,7 +9,7 @@ PACK = 4
 KP = P * PACK
 BANK = 512
 CHUNKS = T2 // BANK
-TURNED = 2
+TURNED = 1
 FLOPS = 2 * K * H * S + 2 * H * N * T2
 
 F32 = mybir.dt.float32
@@ -38,10 +38,10 @@ def tile_list_recommender_slot_memory_kernel(
 
         idx = held.tile([P, S // 16], U16, name="idx")
         idx2 = held.tile([P, S // 16], U16, name="idx2")
-        v_w0 = held.tile([P, S], U32, name="v_w0", align_bytes=64)
+        v_w = {ae: held.tile([P, BANK], U32, name="v_w%d%d" % ae, align_bytes=64) for ae in ((0, 0), (0, 1), (1, 0))}
         w1_c = held.tile([P, 2, 2, KP], U32, name="w1_c", align_bytes=64)
-        v_s = held.tile([P, S], U8, name="v_s", align_bytes=64)
-        w1_s = {(a, 1): held.tile([P, KP], U8, name="w1_s%d1" % a, align_bytes=64) for a in range(2)}
+        v_s = [held.tile([P, BANK], U8, name="v_s%d" % e, align_bytes=64) for e in range(2)]
+        w1_s = {(a, b): held.tile([P, KP], U8, name="w1_s%d%d" % (a, b), align_bytes=64) for a in range(2) for b in range(2)}
         b1_t = held.tile([P, 2, 8], F32, name="b1_t")
         b4_t = held.tile([P, 4, 8], F32, name="b4_t")
         w4_w = held.tile([P, 2, 2 * N], U8, name="w4_w", align_bytes=64)
@@ -61,9 +61,9 @@ def tile_list_recommender_slot_memory_kernel(
             )
             return raw[:].rearrange("p j (m u e) -> p u m j e", u=2, e=2)
 
-        def load_wg(t, cols):
+        def load_wg(t, cols, groups=(0, 2, 1, 3)):
             rows = wgs.rearrange("(q t) s -> t q s", t=PACK)[t]
-            for g in (0, 2, 1, 3):
+            for g in groups:
                 nc.sync.dma_start(wg[t][32 * g : 32 * g + 32, cols], rows[:, cols])
 
         def load_old(t, slot, cols):
@@ -72,60 +72,79 @@ def tile_list_recommender_slot_memory_kernel(
             return o
 
         nc.gpsimd.memset(tab_s[:].bitcast(I32), 0)
-        for q in range(4):
-            queue = nc.gpsimd if q < 2 else nc.scalar
-            queue.dma_start(
-                tab_s[32 * q : 32 * q + 8, :].bitcast(I32),
-                tab_scales[:, 4 * q : 4 * q + 4, :].bitcast(I32),
-            )
         for t in range(2):
             nc.vector.memset(page[t][:], 0.0)
         nc.vector.memset(w4_s[:].rearrange("p a n -> p (a n)").bitcast(I32), 0)
         nc.sync.dma_start(idx[:], offs)
+        for q in range(4):
+            nc.scalar.dma_start(
+                tab_s[32 * q : 32 * q + 8, :].bitcast(I32),
+                tab_scales[:, 4 * q : 4 * q + 4, :].bitcast(I32),
+            )
+        tab_words_i = tab_words.rearrange("a p t i -> a p (t i)").bitcast(I32)
         nc.sync.dma_start(b1_t[:, :, 0:PACK], b1.rearrange("(b p t) -> p b t", b=2, t=PACK))
         nc.sync.dma_start(idx2[:], offs2)
-        tab_words_i = tab_words.rearrange("a p t i -> a p (t i)").bitcast(I32)
+        load_wg(0, slice(0, BANK), (0,))
         nc.sync.dma_start(tab_w[0][:], tab_words_i[0])
         raw00 = load_w1(0, 0)
         nc.sync.dma_start(tab_w[1][:], tab_words_i[1])
-        raw10 = load_w1(1, 0)
-        load_wg(0, slice(0, BANK))
+        raw10 = []
+        for e in range(2):
+            rawh = held.tile([P, PACK, KP // 2], F32, name="rawh%d" % e)
+            nc.sync.dma_start(
+                rawh[:], w1[KP : 2 * KP, e * 256 : (e + 1) * 256].rearrange("(p j) c -> p j c", j=PACK)
+            )
+            raw10.append(rawh[:].rearrange("p j (m t) -> p t m j", t=PACK))
+        load_wg(0, slice(0, BANK), (2, 1, 3))
 
-        def quant_w1(a, b, raw, slot):
-            g = tenant(slot, "w1_g", [P, PACK * KP], BF16)
+        def quant_w1(a, b, raw, slot, bufs):
+            g = tenant(slot, "w1_g", [P, PACK * KP], BF16, bufs)
             nc.scalar.copy(g[:].rearrange("p (u e m j) -> p u m j e", u=2, e=2, j=PACK), raw)
             nc.vector.quantize_mx(w1_c[:, a, b, :].bitcast(FP8X4), w1_s[a, b][:], g[:])
 
-        nc.vector.tensor_copy(v_w0[:], tab_w[0][:].bitcast(U32).indirect(idx[:]))
-        nc.vector.tensor_copy(v_s[:], tab_s[:].indirect(idx[:]))
-        w1_s[0, 0] = tenant("tab_s", "w1_s00", [P, KP], U8)
-        quant_w1(0, 0, raw00, "first")
-        v_w1 = tenant("first", "v_w1", [P, S], U32)
-        nc.vector.tensor_copy(v_w1[:], tab_w[1][:].bitcast(U32).indirect(idx[:]))
-        v_w = [v_w0, v_w1]
-        g10 = [tenant("tab_w1", "w1_ga", [P, 2 * KP], BF16), tenant("g", "w1_gb", [P, 2 * KP], BF16, 4)]
-        nc.vector.tensor_copy(g10[0][:].rearrange("p (e m j) -> p m j e", e=2, j=PACK), raw10[:, 0])
-        nc.scalar.copy(g10[1][:].rearrange("p (e m j) -> p m j e", e=2, j=PACK), raw10[:, 1])
-        w1_s10 = []
-        for u, slot in enumerate(("chain0", "tab_w1")):
-            w1_s10.append(tenant(slot, "w1_s10", [P, 2 * P], U8))
-            nc.vector.quantize_mx(w1_c[:, 1, 0, 2 * u * P : 2 * (u + 1) * P].bitcast(FP8X4), w1_s10[u][:], g10[u][:])
+        def half(lst, e):
+            return lst[:, e * 32 : (e + 1) * 32]
+
+        for e in range(2):
+            nc.vector.tensor_copy(v_w[0, e][:], tab_w[0][:].bitcast(U32).indirect(half(idx, e)))
+        for e in range(2):
+            nc.vector.tensor_copy(v_s[e][:], tab_s[:].indirect(half(idx, e)))
+        nc.vector.tensor_copy(v_w[1, 0][:], tab_w[1][:].bitcast(U32).indirect(half(idx, 0)))
+        quant_w1(0, 0, raw00, "g", 4)
+        g10a = tenant("first", "w1_ga", [P, KP], BF16)
+        g10b = tenant("g", "w1_gb", [P, PACK * KP], BF16, 4)
+        ga = g10a[:].rearrange("p (m j) -> p m j", j=PACK)
+        gb = g10b[:].rearrange("p (t m j) -> p t m j", t=PACK, j=PACK)
+        nc.scalar.copy(ga[:, 0:64], raw10[0][:, 0])
+        nc.vector.tensor_copy(ga[:, 64:128], raw10[1][:, 0])
+        nc.vector.quantize_mx(w1_c[:, 1, 0, :P].bitcast(FP8X4), w1_s[1, 0][:, :P], g10a[:])
+        v_w[1, 1] = tenant("first", "v_w11", [P, BANK], U32)
+        nc.vector.tensor_copy(v_w[1, 1][:], tab_w[1][:].bitcast(U32).indirect(half(idx, 1)))
+        for e in range(2):
+            m = slice(64 * e, 64 * (e + 1))
+            nc.scalar.copy(gb[:, 1, m], raw10[e][:, 1])
+            nc.scalar.copy(
+                gb[:, 2:4, m].rearrange("p t m j -> p m j t"), raw10[e][:, 2:4].rearrange("p t m j -> p m j t")
+            )
+        w1_s101 = tenant("chain0", "w1_s101", [P, P], U8)
+        nc.vector.quantize_mx(w1_c[:, 1, 0, P : 2 * P].bitcast(FP8X4), w1_s101[:], g10b[:, KP : 2 * KP])
+        nc.vector.quantize_mx(w1_c[:, 1, 0, 2 * P :].bitcast(FP8X4), w1_s[1, 0][:, 2 * P :], g10b[:, 2 * KP :])
         make_identity(nc, ident[:])
 
         left, right = slice(0, TURNED * BANK), slice(TURNED * BANK, T2)
         old_a, old_b = {}, {}
         load_wg(0, slice(BANK, S))
-        old_b[0] = load_old(0, "chain1", right)
         load_wg(1, slice(0, S))
+        old_b[0] = load_old(0, "chain1", right)
         old_a[0] = load_old(0, "left0", left)
         raw01 = load_w1(0, 1)
+        load_wg(2, slice(0, S))
         old_a[1] = load_old(1, "left1", left)
         old_b[1] = load_old(1, "chain2", right)
-        load_wg(2, slice(0, S))
         raw11 = load_w1(1, 1)
+        load_wg(3, slice(0, S))
         old_a[2] = load_old(2, "left2", left)
         old_b[2] = load_old(2, "chain3", right)
-        load_wg(3, slice(0, S))
         old_a[3] = load_old(3, "left3", left)
         old_b[3] = load_old(3, "chain4", right)
         nc.sync.dma_start(w4_w[:].bitcast(I32), w4_words.rearrange("a p n -> p a n").bitcast(I32))
@@ -138,8 +157,8 @@ def tile_list_recommender_slot_memory_kernel(
             nc.sync.dma_start(b4_t[:, :, 0:1], b4.rearrange("(i p o) -> p i o", p=P, o=1))
 
         def w1_scale(a, b, t):
-            if (a, b) == (1, 0):
-                return w1_s10[t // 2][:, (t % 2) * P : (t % 2 + 1) * P]
+            if (a, b, t) == (1, 0, 1):
+                return w1_s101[:]
             return w1_s[a, b][:, t * P : (t + 1) * P]
 
         def first_product(s):
@@ -148,14 +167,13 @@ def tile_list_recommender_slot_memory_kernel(
             for e in range(2):
                 acc = psum.tile([P, BANK], F32, name="acc", tag="product", bufs=2)
                 order = (0, 1) if s == 0 else (1, 0)
-                cols = slice(e * BANK, (e + 1) * BANK)
                 for a in order:
                     nc.tensor.matmul_mx(
                         acc[:],
                         lhsT=w1_c[:, a, b, t * P : (t + 1) * P].bitcast(FP8X4),
                         lhsT_scale=w1_scale(a, b, t),
-                        rhs=v_w[a][:, cols].bitcast(FP8X4),
-                        rhs_scale=v_s[4 * a :, cols],
+                        rhs=v_w[a, e][:].bitcast(FP8X4),
+                        rhs_scale=v_s[e][4 * a :, :],
                         start=(a == order[0]),
                         stop=(a == order[1]),
                     )
@@ -268,18 +286,20 @@ def tile_list_recommender_slot_memory_kernel(
                 if s + 1 < PACK:
                     negate_old(s + 1)
                 if s < 2:
-                    quant_w1(s, 1, (raw01, raw11)[s], "left%d" % s)
+                    quant_w1(s, 1, (raw01, raw11)[s], "left%d" % s, 1)
             elif s + 2 < slices:
-                c = s - PACK
-                quant_z(0, c + TURNED, interleave(z0[:, c], 0))
-                zi0[c] = turn_back(c)
-                hs[s + 2] = magnitude(s + 2, acc1[s + 2], "turned%d" % c)
-            if s == slices - 2 and TURNED == 3:
-                quant_z(0, 2, turn_back(2))
+                if s == PACK:
+                    hs[s + 2] = magnitude(s + 2, acc1[s + 2], "sixth")
+                    zi0[0] = turn_back(0)
+                    for c in (2, 3):
+                        quant_z(0, c, interleave(z0[:, c - TURNED], 0))
+                else:
+                    hs[s + 2] = magnitude(s + 2, acc1[s + 2], "turned0")
+                    zi0[1] = interleave(z0[:, 0], 0)
             if 2 <= s < 2 + CHUNKS:
                 old1[s - 2] = load_old_chunk(s - 2)
 
-        z1 = tenant("turned1", "z1", [P, PACK * T2], BF16)
+        z1 = tenant("turned0", "z1", [P, PACK * T2], BF16)
         z_early = tenant("wg3", "z_early", [P, 2, BANK], U32)
         z_c[0, 0], z_c[0, 1] = z_early[:, 0, :], z_early[:, 1, :]
         z_second = tenant("tab_w0", "z_second", [P, CHUNKS, BANK], U32)
@@ -350,7 +370,7 @@ def tile_list_recommender_slot_memory_kernel(
                     )
 
         pieces = [(0, 0, 512), (1, 0, 512), (2, 0, 512), (3, 0, 256), (3, 256, 256)]
-        splits = [56,56,56,64,64]
+        splits = [48,48,48,64,64]
         on_vector = [[],[],[],[1],[1]]
         accs, zis = {}, {}
         quant_z(0, 0, zi0[0])

@@ -4,13 +4,17 @@ import concourse.mybir as mybir
 from concourse.masks import make_identity
 
 K, T, S, T2, H, N = 1024, 2048, 1024, 2048, 1024, 512
+FLOPS = 2 * K * H * S + 2 * H * N * T2
+
 P = 128
 PACK = 4
 KP = P * PACK
 BANK = 512
+HALF = BANK // 2
+SLICES = H // P
 CHUNKS = T2 // BANK
-TURNED = 1
-FLOPS = 2 * K * H * S + 2 * H * N * T2
+TURNED = 2
+VECTOR_SHARE = 48
 
 F32 = mybir.dt.float32
 BF16 = mybir.dt.bfloat16
@@ -30,24 +34,34 @@ def tile_list_recommender_slot_memory_kernel(
     nc = tc.nc
     with ExitStack() as ctx:
         held = ctx.enter_context(tc.tile_pool(name="held", bufs=1))
-        sb = ctx.enter_context(tc.tile_pool(name="sb", bufs=1))
+        rooms = ctx.enter_context(tc.tile_pool(name="rooms", bufs=1))
         psum = ctx.enter_context(tc.psum_pool(name="psum", bufs=1))
 
-        def tenant(slot, name, shape, dtype, bufs=1):
-            return sb.tile(shape, dtype, name=name, tag=slot, bufs=bufs, align_bytes=64)
+        def tenant(room, name, shape, dtype, bufs=1):
+            return rooms.tile(shape, dtype, name=name, tag=room, bufs=bufs, align_bytes=64)
+
+        def quantiser_input(name):
+            return tenant("ring", name, [P, PACK * BANK], BF16, bufs=4)
+
+        def bank(group, name):
+            return psum.tile([P, BANK], F32, name=name, tag=group, bufs=4 if group == "turn" else 2)
 
         idx = held.tile([P, S // 16], U16, name="idx")
         idx2 = held.tile([P, S // 16], U16, name="idx2")
         v_w = {ae: held.tile([P, BANK], U32, name="v_w%d%d" % ae, align_bytes=64) for ae in ((0, 0), (0, 1), (1, 0))}
         w1_c = held.tile([P, 2, 2, KP], U32, name="w1_c", align_bytes=64)
         v_s = [held.tile([P, BANK], U8, name="v_s%d" % e, align_bytes=64) for e in range(2)]
-        w1_s = {(a, b): held.tile([P, KP], U8, name="w1_s%d%d" % (a, b), align_bytes=64) for a in range(2) for b in range(2)}
+        w1_s = {
+            (a, b): held.tile([P, KP], U8, name="w1_s%d%d" % (a, b), align_bytes=64) for a in range(2) for b in range(2)
+        }
         b1_t = held.tile([P, 2, 8], F32, name="b1_t")
-        b4_t = held.tile([P, 4, 8], F32, name="b4_t")
+        b4_t = held.tile([P, N // P, 8], F32, name="b4_t")
         w4_w = held.tile([P, 2, 2 * N], U8, name="w4_w", align_bytes=64)
         w4_s = held.tile([P, 2, N], U8, name="w4_s", align_bytes=64)
         ident = held.tile([P, P], F32, name="ident")
-        z_s = [[held.tile([P, BANK], U8, name="z_s%d%d" % (b, c), align_bytes=64) for c in range(CHUNKS)] for b in range(2)]
+        z_s = [
+            [held.tile([P, BANK], U8, name="z_s%d%d" % (b, c), align_bytes=64) for c in range(CHUNKS)] for b in range(2)
+        ]
         z0 = held.tile([P, CHUNKS - TURNED, PACK, BANK], BF16, name="z0")
         page = [held.tile([P, T2], F32, name="page%d" % t) for t in range(2)]
         wg = [tenant("wg%d" % t, "wg%d" % t, [P, S], F32) for t in range(PACK)]
@@ -61,15 +75,15 @@ def tile_list_recommender_slot_memory_kernel(
             )
             return raw[:].rearrange("p j (m u e) -> p u m j e", u=2, e=2)
 
-        def load_wg(t, cols, groups=(0, 2, 1, 3)):
+        def load_wg(t, cols, quadrants=(0, 2, 1, 3)):
             rows = wgs.rearrange("(q t) s -> t q s", t=PACK)[t]
-            for g in groups:
+            for g in quadrants:
                 nc.sync.dma_start(wg[t][32 * g : 32 * g + 32, cols], rows[:, cols])
 
-        def load_old(t, slot, cols):
-            o = tenant(slot, "old_rows", [P, cols.stop - cols.start], F32)
-            nc.sync.dma_start(o[:], old[:KP, cols].rearrange("(p t) c -> t p c", t=PACK)[t])
-            return o
+        def load_old_slice(t, room, cols):
+            rows = tenant(room, "old_rows", [P, cols.stop - cols.start], F32)
+            nc.sync.dma_start(rows[:], old[:KP, cols].rearrange("(p t) c -> t p c", t=PACK)[t])
+            return rows
 
         nc.gpsimd.memset(tab_s[:].bitcast(I32), 0)
         for t in range(2):
@@ -90,63 +104,57 @@ def tile_list_recommender_slot_memory_kernel(
         nc.sync.dma_start(tab_w[1][:], tab_words_i[1])
         raw10 = []
         for e in range(2):
-            rawh = held.tile([P, PACK, KP // 2], F32, name="rawh%d" % e)
+            raw_half = tenant("right%d" % (e + 2), "raw_half", [P, PACK, HALF], F32)
             nc.sync.dma_start(
-                rawh[:], w1[KP : 2 * KP, e * 256 : (e + 1) * 256].rearrange("(p j) c -> p j c", j=PACK)
+                raw_half[:], w1[KP : 2 * KP, e * HALF : (e + 1) * HALF].rearrange("(p j) c -> p j c", j=PACK)
             )
-            raw10.append(rawh[:].rearrange("p j (m t) -> p t m j", t=PACK))
+            raw10.append(raw_half[:].rearrange("p j (m t) -> p t m j", t=PACK))
         load_wg(0, slice(0, BANK), (2, 1, 3))
 
-        def quant_w1(a, b, raw, slot, bufs):
-            g = tenant(slot, "w1_g", [P, PACK * KP], BF16, bufs)
-            nc.scalar.copy(g[:].rearrange("p (u e m j) -> p u m j e", u=2, e=2, j=PACK), raw)
-            nc.vector.quantize_mx(w1_c[:, a, b, :].bitcast(FP8X4), w1_s[a, b][:], g[:])
+        def quantise_w1(a, b, raw):
+            grouped = quantiser_input("w1_grouped")
+            nc.scalar.copy(grouped[:].rearrange("p (u e m j) -> p u m j e", u=2, e=2, j=PACK), raw)
+            nc.vector.quantize_mx(w1_c[:, a, b, :].bitcast(FP8X4), w1_s[a, b][:], grouped[:])
 
-        def half(lst, e):
-            return lst[:, e * 32 : (e + 1) * 32]
+        def half(entries, e):
+            return entries[:, e * BANK // 16 : (e + 1) * BANK // 16]
 
         for e in range(2):
             nc.vector.tensor_copy(v_w[0, e][:], tab_w[0][:].bitcast(U32).indirect(half(idx, e)))
         for e in range(2):
             nc.vector.tensor_copy(v_s[e][:], tab_s[:].indirect(half(idx, e)))
         nc.vector.tensor_copy(v_w[1, 0][:], tab_w[1][:].bitcast(U32).indirect(half(idx, 0)))
-        quant_w1(0, 0, raw00, "g", 4)
-        g10a = tenant("first", "w1_ga", [P, KP], BF16)
-        g10b = tenant("g", "w1_gb", [P, PACK * KP], BF16, 4)
-        ga = g10a[:].rearrange("p (m j) -> p m j", j=PACK)
-        gb = g10b[:].rearrange("p (t m j) -> p t m j", t=PACK, j=PACK)
-        nc.scalar.copy(ga[:, 0:64], raw10[0][:, 0])
-        nc.vector.tensor_copy(ga[:, 64:128], raw10[1][:, 0])
-        nc.vector.quantize_mx(w1_c[:, 1, 0, :P].bitcast(FP8X4), w1_s[1, 0][:, :P], g10a[:])
+        quantise_w1(0, 0, raw00)
+        first_cols = tenant("first", "first_cols", [P, KP], BF16)
+        other_cols = quantiser_input("other_cols")
+        first_view = first_cols[:].rearrange("p (m j) -> p m j", j=PACK)
+        other_view = other_cols[:].rearrange("p (t m j) -> p t m j", t=PACK, j=PACK)
+        nc.scalar.copy(first_view[:, : P // 2], raw10[0][:, 0])
+        nc.vector.tensor_copy(first_view[:, P // 2 :], raw10[1][:, 0])
+        nc.vector.quantize_mx(w1_c[:, 1, 0, :P].bitcast(FP8X4), w1_s[1, 0][:, :P], first_cols[:])
         v_w[1, 1] = tenant("first", "v_w11", [P, BANK], U32)
         nc.vector.tensor_copy(v_w[1, 1][:], tab_w[1][:].bitcast(U32).indirect(half(idx, 1)))
         for e in range(2):
-            m = slice(64 * e, 64 * (e + 1))
-            nc.scalar.copy(gb[:, 1, m], raw10[e][:, 1])
+            m = slice(e * P // 2, (e + 1) * P // 2)
+            nc.scalar.copy(other_view[:, 1, m], raw10[e][:, 1])
             nc.scalar.copy(
-                gb[:, 2:4, m].rearrange("p t m j -> p m j t"), raw10[e][:, 2:4].rearrange("p t m j -> p m j t")
+                other_view[:, 2:4, m].rearrange("p t m j -> p m j t"), raw10[e][:, 2:4].rearrange("p t m j -> p m j t")
             )
-        w1_s101 = tenant("chain0", "w1_s101", [P, P], U8)
-        nc.vector.quantize_mx(w1_c[:, 1, 0, P : 2 * P].bitcast(FP8X4), w1_s101[:], g10b[:, KP : 2 * KP])
-        nc.vector.quantize_mx(w1_c[:, 1, 0, 2 * P :].bitcast(FP8X4), w1_s[1, 0][:, 2 * P :], g10b[:, 2 * KP :])
+        w1_s_slice1 = tenant("chain0", "w1_s_slice1", [P, P], U8)
+        nc.vector.quantize_mx(w1_c[:, 1, 0, P : 2 * P].bitcast(FP8X4), w1_s_slice1[:], other_cols[:, KP : 2 * KP])
+        nc.vector.quantize_mx(w1_c[:, 1, 0, 2 * P :].bitcast(FP8X4), w1_s[1, 0][:, 2 * P :], other_cols[:, 2 * KP :])
         make_identity(nc, ident[:])
 
         left, right = slice(0, TURNED * BANK), slice(TURNED * BANK, T2)
-        old_a, old_b = {}, {}
+        old_left, old_right, raw_second = [], [], []
         load_wg(0, slice(BANK, S))
-        load_wg(1, slice(0, S))
-        old_b[0] = load_old(0, "chain1", right)
-        old_a[0] = load_old(0, "left0", left)
-        raw01 = load_w1(0, 1)
-        load_wg(2, slice(0, S))
-        old_a[1] = load_old(1, "left1", left)
-        old_b[1] = load_old(1, "chain2", right)
-        raw11 = load_w1(1, 1)
-        load_wg(3, slice(0, S))
-        old_a[2] = load_old(2, "left2", left)
-        old_b[2] = load_old(2, "chain3", right)
-        old_a[3] = load_old(3, "left3", left)
-        old_b[3] = load_old(3, "chain4", right)
+        for t in range(PACK):
+            if t + 1 < PACK:
+                load_wg(t + 1, slice(0, S))
+            old_left.append(load_old_slice(t, "left%d" % t, left))
+            if t < 2:
+                raw_second.append(load_w1(t, 1))
+            old_right.append(load_old_slice(t, "right%d" % t, right))
         nc.sync.dma_start(w4_w[:].bitcast(I32), w4_words.rearrange("a p n -> p a n").bitcast(I32))
         for q in range(4):
             nc.sync.dma_start(
@@ -158,15 +166,15 @@ def tile_list_recommender_slot_memory_kernel(
 
         def w1_scale(a, b, t):
             if (a, b, t) == (1, 0, 1):
-                return w1_s101[:]
+                return w1_s_slice1[:]
             return w1_s[a, b][:, t * P : (t + 1) * P]
 
         def first_product(s):
             b, t = divmod(s, PACK)
+            order = (0, 1) if s == 0 else (1, 0)
             accs = []
             for e in range(2):
-                acc = psum.tile([P, BANK], F32, name="acc", tag="product", bufs=2)
-                order = (0, 1) if s == 0 else (1, 0)
+                acc = bank("product", "acc")
                 for a in order:
                     nc.tensor.matmul_mx(
                         acc[:],
@@ -180,9 +188,9 @@ def tile_list_recommender_slot_memory_kernel(
                 accs.append(acc)
             return accs
 
-        def magnitude(s, accs, slot):
+        def magnitude(s, accs, room):
             b, t = divmod(s, PACK)
-            h = tenant(slot, "h", [P, S], F32)
+            h = tenant(room, "h", [P, S], F32)
             for e in range(2):
                 nc.scalar.activation(h[:, e * BANK : (e + 1) * BANK], accs[e][:], ACT.Abs, bias=b1_t[:, b, t : t + 1])
             return h
@@ -192,206 +200,192 @@ def tile_list_recommender_slot_memory_kernel(
             if s == 0:
                 for e in range(2):
                     cols = slice(e * BANK, (e + 1) * BANK)
-                    entries = idx2[:, e * 32 : (e + 1) * 32]
-                    nc.vector.tensor_tensor(page[t][:].indirect(entries), h[:, cols], wg[t][:, cols], ALU.mult)
+                    nc.vector.tensor_tensor(page[t][:].indirect(half(idx2, e)), h[:, cols], wg[t][:, cols], ALU.mult)
             else:
                 nc.vector.tensor_tensor(page[t][:].indirect(idx2[:]), h[:], wg[t][:], ALU.mult)
 
-        def interleave(planes, split):
-            width = planes.shape[2]
-            zi = tenant("g", "zi", [P, PACK * BANK], BF16, 4)
-            dst = zi[:, : PACK * width].rearrange("p (c i t) -> p c t i", i=4, t=PACK)
-            src = planes.rearrange("p t (c i) -> p c t i", i=4)
-            if split < width // 4:
-                nc.scalar.copy(dst[:, split:], src[:, split:])
-            if split > 0:
-                nc.vector.tensor_copy(dst[:, :split], src[:, :split])
-            return zi[:, : PACK * width]
+        def side_by_side(slices, on_vector):
+            width = slices.shape[2]
+            words = quantiser_input("z_words")
+            dst = words[:, : PACK * width].rearrange("p (c i t) -> p c t i", i=4, t=PACK)
+            src = slices.rearrange("p t (c i) -> p c t i", i=4)
+            if on_vector < width // 4:
+                nc.scalar.copy(dst[:, on_vector:], src[:, on_vector:])
+            if on_vector > 0:
+                nc.vector.tensor_copy(dst[:, :on_vector], src[:, :on_vector])
+            return words[:, : PACK * width]
 
         z_c = {}
 
-        def quant_z(b, c, zi, lo=0, width=BANK):
-            nc.vector.quantize_mx(z_c[b, c][:, lo : lo + width].bitcast(FP8X4), z_s[b][c][:, lo : lo + width], zi)
+        def quantise_z(b, c, words, lo=0, width=BANK):
+            nc.vector.quantize_mx(z_c[b, c][:, lo : lo + width].bitcast(FP8X4), z_s[b][c][:, lo : lo + width], words)
 
-        def add_turned(dst, first, second):
-            nc.tensor.matmul(dst, first, ident[:], start=True, stop=False, is_transpose=True)
-            nc.tensor.matmul(dst, second, ident[:], start=False, stop=True, is_transpose=True)
-
-        turned = [tenant("turned%d" % c, "turned", [P, PACK, 2, BANK], F32) for c in range(TURNED)]
-
-        minus_old = {}
-
-        def negate_old(t):
-            minus_old[t] = tenant("chain%d" % t, "minus_old", [P, TURNED * BANK], F32)
-            nc.scalar.activation(minus_old[t][:], old_a[t][:], ACT.Copy, scale=-1.0)
-
-        def keep_larger(t):
+        def larger_on_vector(t):
             nc.vector.tensor_tensor(
                 z0[:, :, t, :],
                 page[t][:, right].rearrange("p (c w) -> p c w", w=BANK),
-                old_b[t][:].rearrange("p (c w) -> p c w", w=BANK),
+                old_right[t][:].rearrange("p (c w) -> p c w", w=BANK),
                 ALU.max,
             )
 
-        def turn_slice(t):
-            o = minus_old[t]
+        turned = [tenant("turned%d" % c, "turned", [P, PACK, 2, BANK], F32) for c in range(TURNED)]
+        minus_old = {}
+
+        def add_transposed(dst, first, second):
+            nc.tensor.matmul(dst, first, ident[:], start=True, stop=False, is_transpose=True)
+            nc.tensor.matmul(dst, second, ident[:], start=False, stop=True, is_transpose=True)
+
+        def negate_old(t):
+            chunk0 = tenant("chain%d" % t, "minus_old", [P, BANK], F32)
+            minus_old[t] = [chunk0[:], old_left[t][:, BANK:]]
             for c in range(TURNED):
-                d_bank = psum.tile([P, BANK], F32, name="d_bank", tag="turn", bufs=4)
-                a_bank = psum.tile([P, BANK], F32, name="a_bank", tag="turn", bufs=4)
-                for i in range(4):
-                    cols = slice(c * BANK + i * P, c * BANK + (i + 1) * P)
-                    add_turned(d_bank[:, i * P : (i + 1) * P], o[:, cols], page[t][:, cols])
-                for i in range(4):
-                    cols = slice(c * BANK + i * P, c * BANK + (i + 1) * P)
-                    nc.tensor.transpose(a_bank[:, i * P : (i + 1) * P], page[t][:, cols], ident[:])
-                nc.scalar.activation(turned[c][:, t, 0, :], d_bank[:], ACT.Relu, scale=-1.0)
-                nc.scalar.copy(turned[c][:, t, 1, :], a_bank[:])
+                nc.scalar.activation(minus_old[t][c], old_left[t][:, c * BANK : (c + 1) * BANK], ACT.Copy, scale=-1.0)
+
+        def turn_excess(t, c):
+            difference = bank("turn", "difference")
+            for i in range(BANK // P):
+                blk = slice(i * P, (i + 1) * P)
+                add_transposed(difference[:, blk], minus_old[t][c][:, blk], page[t][:, c * BANK :][:, blk])
+            nc.scalar.activation(turned[c][:, t, 0, :], difference[:], ACT.Relu, scale=-1.0)
+
+        def turn_page(t, c):
+            copied = bank("turn", "copied")
+            for i in range(BANK // P):
+                blk = slice(i * P, (i + 1) * P)
+                nc.tensor.transpose(copied[:, blk], page[t][:, c * BANK :][:, blk], ident[:])
+            nc.scalar.copy(turned[c][:, t, 1, :], copied[:])
 
         def turn_back(c):
-            zi = tenant("g", "zi", [P, PACK * BANK], BF16, 4)
-            for i in range(4):
-                z_bank = psum.tile([P, BANK], F32, name="z_bank", tag="turn", bufs=4)
+            words = quantiser_input("z_words")
+            for i in range(BANK // P):
+                larger = bank("turn", "larger")
                 blk = slice(i * P, (i + 1) * P)
                 for t in range(PACK):
-                    add_turned(z_bank[:, t * P : (t + 1) * P], turned[c][:, t, 1, blk], turned[c][:, t, 0, blk])
+                    add_transposed(larger[:, t * P : (t + 1) * P], turned[c][:, t, 1, blk], turned[c][:, t, 0, blk])
                 nc.scalar.copy(
-                    zi[:, i * BANK : (i + 1) * BANK].rearrange("p (c t) -> p c t", t=PACK),
-                    z_bank[:].rearrange("p (t c) -> p c t", t=PACK),
+                    words[:, i * BANK : (i + 1) * BANK].rearrange("p (c t) -> p c t", t=PACK),
+                    larger[:].rearrange("p (t c) -> p c t", t=PACK),
                 )
-            return zi[:]
+            return words[:]
 
         def load_old_chunk(c):
-            o = tenant("chain%d" % c, "old_cols", [P, PACK, BANK], F32)
-            nc.sync.dma_start(o[:], old[KP:, c * BANK : (c + 1) * BANK].rearrange("(p t) c -> p t c", t=PACK))
-            return o
+            cols = tenant("chain%d" % c, "old_cols", [P, PACK, BANK], F32)
+            nc.sync.dma_start(cols[:], old[KP:, c * BANK : (c + 1) * BANK].rearrange("(p t) c -> p t c", t=PACK))
+            return cols
 
-        z_late = held.tile([P, 2, BANK], U32, name="z_late", align_bytes=64)
-        z_c[0, 2], z_c[0, 3] = z_late[:, 0, :], z_late[:, 1, :]
-        slices = 2 * PACK
-        acc1 = {s: first_product(s) for s in range(2)}
-        hs = {s: magnitude(s, acc1[s], "page%d" % (s + 2)) for s in range(2)}
+        z_right = held.tile([P, CHUNKS - TURNED, BANK], U32, name="z_right", align_bytes=64)
+        for c in range(TURNED, CHUNKS):
+            z_c[0, c] = z_right[:, c - TURNED, :]
+        products = {s: first_product(s) for s in range(2)}
+        hs = {s: magnitude(s, products[s], "page%d" % (s + 2)) for s in range(2)}
         negate_old(0)
-        old1, zi0 = {}, {}
-        for s in range(slices):
+        old_chunk, left_words = {}, {}
+        for s in range(SLICES):
             scatter(s, hs[s])
             if s < 2:
                 page.append(tenant("page%d" % (s + 2), "late_page", [P, T2], F32))
                 nc.gpsimd.memset(page[s + 2][:], 0.0)
-            if s + 2 < slices:
-                acc1[s + 2] = first_product(s + 2)
+            if s + 2 < SLICES:
+                products[s + 2] = first_product(s + 2)
             if s < PACK:
-                keep_larger(s)
-                turn_slice(s)
-                hs[s + 2] = magnitude(s + 2, acc1[s + 2], "chain%d" % s)
+                larger_on_vector(s)
+                turn_excess(s, 0)
+                hs[s + 2] = magnitude(s + 2, products[s + 2], "chain%d" % s)
+                turn_excess(s, 1)
+                for c in range(TURNED):
+                    turn_page(s, c)
                 if s + 1 < PACK:
                     negate_old(s + 1)
                 if s < 2:
-                    quant_w1(s, 1, (raw01, raw11)[s], "left%d" % s, 1)
-            elif s + 2 < slices:
-                if s == PACK:
-                    hs[s + 2] = magnitude(s + 2, acc1[s + 2], "sixth")
-                    zi0[0] = turn_back(0)
-                    for c in (2, 3):
-                        quant_z(0, c, interleave(z0[:, c - TURNED], 0))
-                else:
-                    hs[s + 2] = magnitude(s + 2, acc1[s + 2], "turned0")
-                    zi0[1] = interleave(z0[:, 0], 0)
+                    quantise_w1(s, 1, raw_second[s])
+            elif s == PACK:
+                hs[s + 2] = magnitude(s + 2, products[s + 2], "tab_w1")
+                left_words[0] = turn_back(0)
+                for c in range(TURNED, CHUNKS):
+                    quantise_z(0, c, side_by_side(z0[:, c - TURNED], 0))
+            elif s == PACK + 1:
+                hs[s + 2] = magnitude(s + 2, products[s + 2], "turned0")
+                left_words[1] = turn_back(1)
             if 2 <= s < 2 + CHUNKS:
-                old1[s - 2] = load_old_chunk(s - 2)
+                old_chunk[s - 2] = load_old_chunk(s - 2)
 
         z1 = tenant("turned0", "z1", [P, PACK * T2], BF16)
-        z_early = tenant("wg3", "z_early", [P, 2, BANK], U32)
-        z_c[0, 0], z_c[0, 1] = z_early[:, 0, :], z_early[:, 1, :]
+        z_left = tenant("wg3", "z_left", [P, TURNED, BANK], U32)
+        for c in range(TURNED):
+            z_c[0, c] = z_left[:, c, :]
         z_second = tenant("tab_w0", "z_second", [P, CHUNKS, BANK], U32)
         for c in range(CHUNKS):
             z_c[1, c] = z_second[:, c, :]
 
         def second_product(b, c, lo, width, accs):
             for n in range(N // P):
-                steps = [(accs[n][:], 0, BANK, True, True)] if width == BANK else [
-                    (accs[n // 2][:, at : at + P], lo + at % 256, P, at == 0, at == 3 * P)
-                    for at in ((n % 2) * 256, (n % 2) * 256 + P)
-                ]
-                for acc, at, cols, first, last in steps:
+                if width == BANK:
+                    steps = [(accs[n][:], 0, BANK, True, True)]
+                else:
+                    steps = [
+                        (accs[n // 2][:, at : at + P], lo + at % HALF, P, at == 0, at == BANK - P)
+                        for at in ((n % 2) * HALF, (n % 2) * HALF + P)
+                    ]
+                for acc, col, cols, first, last in steps:
                     nc.tensor.matmul_mx(
                         acc,
                         lhsT=w4_w[:, b, 2 * n * P : 2 * (n + 1) * P].bitcast(FP4X4),
                         lhsT_scale=w4_s[:, b, n * P : (n + 1) * P],
-                        rhs=z_c[b, c][:, at : at + cols].bitcast(FP8X4),
-                        rhs_scale=z_s[b][c][:, at : at + cols],
+                        rhs=z_c[b, c][:, col : col + cols].bitcast(FP8X4),
+                        rhs_scale=z_s[b][c][:, col : col + cols],
                         start=(b == 0 and first),
                         stop=(b == 1 and last),
                     )
 
         def open_piece(c, lo, width):
-            accs = []
-            for n in range(width // P):
-                if (c, lo) == (3, 256) or (c == 1 and n >= 2):
-                    accs.append(psum.tile([P, BANK], F32, name="score", tag="product", bufs=2))
-                elif c % 2 == 1:
-                    accs.append(psum.tile([P, BANK], F32, name="score", tag="spare", bufs=2))
-                else:
-                    accs.append(psum.tile([P, BANK], F32, name="score", tag="turn", bufs=4))
+            groups = ["turn"] * 4 if c % 2 == 0 else ["spare", "spare", "product", "product"]
+            accs = [bank(group, "score") for group in groups[lo // P : (lo + width) // P]]
             second_product(0, c, lo, width, accs)
             return accs
 
-        def max_piece(c, lo, width):
+        def piece_words(c, lo, width):
             cols = slice(c * BANK + lo, c * BANK + lo + width)
-            planes = z1[:, PACK * cols.start : PACK * cols.stop].rearrange("p (t c) -> p t c", t=PACK)
+            slices = z1[:, PACK * cols.start : PACK * cols.stop].rearrange("p (t c) -> p t c", t=PACK)
             for t in range(PACK):
-                nc.vector.tensor_tensor(planes[:, t, :], page[t][:, cols], old1[c][:, t, lo : lo + width], ALU.max)
-            return planes
+                nc.vector.tensor_tensor(slices[:, t, :], page[t][:, cols], old_chunk[c][:, t, lo : lo + width], ALU.max)
+            return side_by_side(slices, VECTOR_SHARE if width == BANK else width // 4)
 
         staged = {}
 
-        def close_piece(c, lo, width, accs, on_vector):
+        def close_piece(c, lo, width, accs):
             cols = slice(c * BANK + lo, c * BANK + lo + width)
             second_product(1, c, lo, width, accs)
             if lo == 0:
                 staged[c] = tenant("chain%d" % c, "y", [P, N // P * BANK], F32)
-            y = staged[c][:, 4 * lo : 4 * (lo + width)].rearrange("p (n c) -> p n c", n=N // P)
+            y = staged[c][:, N // P * lo : N // P * (lo + width)].rearrange("p (n c) -> p n c", n=N // P)
             for k, acc in enumerate(accs):
                 if width == BANK:
-                    if k in on_vector:
-                        nc.vector.tensor_scalar(y[:, k, :], acc[:], b4_t[:, k, 0:1], None, ALU.add)
-                    else:
-                        nc.scalar.activation(y[:, k, :], acc[:], ACT.Identity, bias=b4_t[:, k, 0:1])
+                    nc.scalar.activation(y[:, k, :], acc[:], ACT.Identity, bias=b4_t[:, k, 0:1])
                     nc.sync.dma_start(out[k * P : (k + 1) * P, cols], y[:, k, :])
                 else:
                     for i in range(2):
                         n = 2 * k + i
                         part = acc[:, i * width : (i + 1) * width]
-                        if k not in on_vector:
+                        if k == 0:
                             nc.scalar.activation(y[:, n, :], part, ACT.Identity, bias=b4_t[:, n, 0:1])
                         else:
                             nc.vector.tensor_scalar(y[:, n, :], part, b4_t[:, n, 0:1], None, ALU.add)
                     nc.sync.dma_start(
-                        out[2 * k * P : 2 * (k + 1) * P, cols].rearrange("(i p) c -> p i c", i=2), y[:, 2 * k : 2 * k + 2, :]
+                        out[2 * k * P : 2 * (k + 1) * P, cols].rearrange("(i p) c -> p i c", i=2),
+                        y[:, 2 * k : 2 * k + 2, :],
                     )
 
-        pieces = [(0, 0, 512), (1, 0, 512), (2, 0, 512), (3, 0, 256), (3, 256, 256)]
-        splits = [48,48,48,64,64]
-        on_vector = [[],[],[],[1],[1]]
-        accs, zis = {}, {}
-        quant_z(0, 0, zi0[0])
-        accs[0] = open_piece(*pieces[0])
-        zis[0] = interleave(max_piece(*pieces[0]), splits[0])
-        quant_z(0, 1, zi0[1])
-        accs[1] = open_piece(*pieces[1])
-        quant_z(1, pieces[0][0], zis[0], pieces[0][1], pieces[0][2])
-        zis[1] = interleave(max_piece(*pieces[1]), splits[1])
-        close_piece(*pieces[0], accs[0], on_vector[0])
-        accs[2] = open_piece(*pieces[2])
-        quant_z(1, pieces[1][0], zis[1], pieces[1][1], pieces[1][2])
-        zis[2] = interleave(max_piece(*pieces[2]), splits[2])
-        close_piece(*pieces[1], accs[1], on_vector[1])
-        accs[3] = open_piece(*pieces[3])
-        accs[4] = open_piece(*pieces[4])
-        quant_z(1, pieces[2][0], zis[2], pieces[2][1], pieces[2][2])
-        zis[3] = interleave(max_piece(*pieces[3]), splits[3])
-        close_piece(*pieces[2], accs[2], on_vector[2])
-        quant_z(1, pieces[3][0], zis[3], pieces[3][1], pieces[3][2])
-        zis[4] = interleave(max_piece(*pieces[4]), splits[4])
-        close_piece(*pieces[3], accs[3], on_vector[3])
-        quant_z(1, pieces[4][0], zis[4], pieces[4][1], pieces[4][2])
-        close_piece(*pieces[4], accs[4], on_vector[4])
+        pieces = [(c, 0, BANK) for c in range(CHUNKS - 1)] + [(CHUNKS - 1, lo, HALF) for lo in (0, HALF)]
+        quantise_z(0, 0, left_words[0])
+        accs = {pieces[0]: open_piece(*pieces[0])}
+        words = piece_words(*pieces[0])
+        quantise_z(0, 1, left_words[1])
+        accs[pieces[1]] = open_piece(*pieces[1])
+        for k, (c, lo, width) in enumerate(pieces):
+            quantise_z(1, c, words, lo, width)
+            if k + 1 < len(pieces):
+                words = piece_words(*pieces[k + 1])
+            close_piece(c, lo, width, accs[c, lo, width])
+            for piece in pieces:
+                if piece[0] == c + 2:
+                    accs[piece] = open_piece(*piece)

@@ -13,8 +13,8 @@ BANK = 512
 HALF = BANK // 2
 SLICES = H // P
 CHUNKS = T2 // BANK
-TURNED = 2
-VECTOR_SHARE = 48
+BLOCKS = BANK // P
+VECTOR_SHARE = (32, 24, 64, 128, 64, 64)
 
 F32 = mybir.dt.float32
 BF16 = mybir.dt.bfloat16
@@ -37,58 +37,48 @@ def tile_list_recommender_slot_memory_kernel(
         rooms = ctx.enter_context(tc.tile_pool(name="rooms", bufs=1))
         psum = ctx.enter_context(tc.psum_pool(name="psum", bufs=1))
 
-        def tenant(room, name, shape, dtype, bufs=1):
-            return rooms.tile(shape, dtype, name=name, tag=room, bufs=bufs, align_bytes=64)
+        def tenant(room, name, shape, dtype):
+            return rooms.tile(shape, dtype, name=name, tag=room, align_bytes=64)
 
-        def quantiser_input(name):
-            return tenant("ring", name, [P, PACK * BANK], BF16, bufs=4)
+        def quantiser_input(room):
+            return tenant(room, "grouped", [P, PACK * BANK], BF16)
 
-        def bank(group, name):
-            return psum.tile([P, BANK], F32, name=name, tag=group, bufs=4 if group == "turn" else 2)
+        def bank(k, name):
+            return psum.tile([P, BANK], F32, name=name, tag="bank%d" % k)
 
         idx = held.tile([P, S // 16], U16, name="idx")
         idx2 = held.tile([P, S // 16], U16, name="idx2")
-        v_w = {ae: held.tile([P, BANK], U32, name="v_w%d%d" % ae, align_bytes=64) for ae in ((0, 0), (0, 1), (1, 0))}
-        w1_c = held.tile([P, 2, 2, KP], U32, name="w1_c", align_bytes=64)
-        v_s = [held.tile([P, BANK], U8, name="v_s%d" % e, align_bytes=64) for e in range(2)]
-        w1_s = {
-            (a, b): held.tile([P, KP], U8, name="w1_s%d%d" % (a, b), align_bytes=64) for a in range(2) for b in range(2)
+        v_w = {
+            (a, e): held.tile([P, BANK], U32, name="v_w%d%d" % (a, e), align_bytes=64)
+            for a in range(2)
+            for e in range(2)
         }
-        b1_t = held.tile([P, 2, 8], F32, name="b1_t")
+        v_s = [held.tile([P, BANK], U8, name="v_s%d" % e, align_bytes=64) for e in range(2)]
+        b1_rows = held.tile([P, PACK, 8], F32, name="b1_rows")
+        b1_dealt = held.tile([P, PACK], F32, name="b1_dealt")
         b4_t = held.tile([P, N // P, 8], F32, name="b4_t")
-        w4_w = held.tile([P, 2, 2 * N], U8, name="w4_w", align_bytes=64)
         w4_s = held.tile([P, 2, N], U8, name="w4_s", align_bytes=64)
         ident = held.tile([P, P], F32, name="ident")
         z_s = [
             [held.tile([P, BANK], U8, name="z_s%d%d" % (b, c), align_bytes=64) for c in range(CHUNKS)] for b in range(2)
         ]
-        z0 = held.tile([P, CHUNKS - TURNED, PACK, BANK], BF16, name="z0")
-        page = [held.tile([P, T2], F32, name="page%d" % t) for t in range(2)]
-        wg = [tenant("wg%d" % t, "wg%d" % t, [P, S], F32) for t in range(PACK)]
-        tab_w = [tenant("tab_w%d" % a, "tab_w%d" % a, [P, T], I32) for a in range(2)]
-        tab_s = tenant("tab_s", "tab_s", [P, T], U8)
-
-        def load_w1(a, b):
-            raw = tenant("raw", "w1_raw", [P, PACK, KP], F32, bufs=2)
-            nc.sync.dma_start(
-                raw[:], w1[a * KP : (a + 1) * KP, b * KP : (b + 1) * KP].rearrange("(p j) c -> p j c", j=PACK)
-            )
-            return raw[:].rearrange("p j (m u e) -> p u m j e", u=2, e=2)
-
-        def load_wg(t, cols, quadrants=(0, 2, 1, 3)):
-            rows = wgs.rearrange("(q t) s -> t q s", t=PACK)[t]
-            for g in quadrants:
-                nc.sync.dma_start(wg[t][32 * g : 32 * g + 32, cols], rows[:, cols])
-
-        def load_old_slice(t, room, cols):
-            rows = tenant(room, "old_rows", [P, cols.stop - cols.start], F32)
-            nc.sync.dma_start(rows[:], old[:KP, cols].rearrange("(p t) c -> t p c", t=PACK)[t])
-            return rows
+        z_c = {(1, c): held.tile([P, BANK], U32, name="z_c%d" % c, align_bytes=64)[:] for c in range(CHUNKS)}
+        z1 = held.tile([P, PACK * T2], BF16, name="z1", align_bytes=64)
+        pages = [held.tile([P, T2], F32, name="page%d" % k) for k in range(3)]
+        page = [pages[k] for k in (0, 1, 2, 0, 1, 2, 0, 0)]
+        wg_rows = tenant("h2", "wg_rows", [P, S], F32)
+        minus_first = held.tile([P, BANK], F32, name="minus_first")
+        w4_w = held.tile([P, 2, 2 * N], U8, name="w4_w", align_bytes=64)
+        wg_dealt = held.tile([P, PACK, S], F32, name="wg_dealt")
+        tab_s = held.tile([P, T], U8, name="tab_s")
+        tab_w = [tenant("big0%d" % a, "tab_w%d" % a, [P, T], I32) for a in range(2)]
 
         nc.gpsimd.memset(tab_s[:].bitcast(I32), 0)
-        for t in range(2):
-            nc.vector.memset(page[t][:], 0.0)
+        for k in range(2):
+            nc.vector.memset(pages[k][:], 0.0)
         nc.vector.memset(w4_s[:].rearrange("p a n -> p (a n)").bitcast(I32), 0)
+        nc.gpsimd.memset(pages[2][:], 0.0)
+        make_identity(nc, ident[:])
         nc.sync.dma_start(idx[:], offs)
         for q in range(4):
             nc.scalar.dma_start(
@@ -96,65 +86,42 @@ def tile_list_recommender_slot_memory_kernel(
                 tab_scales[:, 4 * q : 4 * q + 4, :].bitcast(I32),
             )
         tab_words_i = tab_words.rearrange("a p t i -> a p (t i)").bitcast(I32)
-        nc.sync.dma_start(b1_t[:, :, 0:PACK], b1.rearrange("(b p t) -> p b t", b=2, t=PACK))
+        with nc.allow_non_contiguous_dma(reason="one bias value a partition"):
+            nc.sync.dma_start(b1_rows[:, :, 0:1], b1[:KP].rearrange("(s p o) -> p s o", p=P, o=1))
         nc.sync.dma_start(idx2[:], offs2)
-        load_wg(0, slice(0, BANK), (0,))
+        nc.sync.dma_start(b1_dealt[:], b1[KP:].rearrange("(p t) -> p t", t=PACK))
+
+        def load_w1(room, a, cols):
+            raw = tenant(room, "w1_raw", [P, PACK, cols.stop - cols.start], F32)
+            nc.sync.dma_start(raw[:], w1[a * KP : (a + 1) * KP, cols].rearrange("(p j) c -> p j c", j=PACK))
+            return raw
+
+        def load_old(s):
+            rows = tenant("big31" if s == SLICES - 1 else "old%d" % (s % 3), "old_rows", [P, T2], F32)
+            if s < PACK:
+                nc.sync.dma_start(rows[:], old[s * P : (s + 1) * P, :])
+            else:
+                nc.sync.dma_start(rows[:], old[KP:, :].rearrange("(p t) c -> t p c", t=PACK)[s - PACK])
+            return rows
+
         nc.sync.dma_start(tab_w[0][:], tab_words_i[0])
-        raw00 = load_w1(0, 0)
+        raw_first = [load_w1("first%d" % a, a, slice(0, P)) for a in range(2)]
         nc.sync.dma_start(tab_w[1][:], tab_words_i[1])
-        raw10 = []
-        for e in range(2):
-            raw_half = tenant("right%d" % (e + 2), "raw_half", [P, PACK, HALF], F32)
+        nc.sync.dma_start(wg_rows[:, :BANK], wgs[:, :BANK])
+        raw_rest = [load_w1("big1%d" % a, a, slice(P, KP)) for a in range(2)]
+        nc.sync.dma_start(wg_rows[:, BANK:], wgs[:, BANK:])
+        olds = {0: load_old(0)}
+        raw_dealt = {
+            (a, e): load_w1(("big20", "big21", "big30", "h3")[2 * a + e], a, slice(KP + e * HALF, KP + (e + 1) * HALF))
+            for a in range(2)
+            for e in range(2)
+        }
+        for s in (1, 2):
+            olds[s] = load_old(s)
+        for g in (0, 2, 1, 3):
             nc.sync.dma_start(
-                raw_half[:], w1[KP : 2 * KP, e * HALF : (e + 1) * HALF].rearrange("(p j) c -> p j c", j=PACK)
+                wg_dealt[32 * g : 32 * g + 32].rearrange("p t s -> p (t s)"), wgs.rearrange("(q t) s -> q (t s)", t=PACK)
             )
-            raw10.append(raw_half[:].rearrange("p j (m t) -> p t m j", t=PACK))
-        load_wg(0, slice(0, BANK), (2, 1, 3))
-
-        def quantise_w1(a, b, raw):
-            grouped = quantiser_input("w1_grouped")
-            nc.scalar.copy(grouped[:].rearrange("p (u e m j) -> p u m j e", u=2, e=2, j=PACK), raw)
-            nc.vector.quantize_mx(w1_c[:, a, b, :].bitcast(FP8X4), w1_s[a, b][:], grouped[:])
-
-        def half(entries, e):
-            return entries[:, e * BANK // 16 : (e + 1) * BANK // 16]
-
-        for e in range(2):
-            nc.vector.tensor_copy(v_w[0, e][:], tab_w[0][:].bitcast(U32).indirect(half(idx, e)))
-        for e in range(2):
-            nc.vector.tensor_copy(v_s[e][:], tab_s[:].indirect(half(idx, e)))
-        nc.vector.tensor_copy(v_w[1, 0][:], tab_w[1][:].bitcast(U32).indirect(half(idx, 0)))
-        quantise_w1(0, 0, raw00)
-        first_cols = tenant("first", "first_cols", [P, KP], BF16)
-        other_cols = quantiser_input("other_cols")
-        first_view = first_cols[:].rearrange("p (m j) -> p m j", j=PACK)
-        other_view = other_cols[:].rearrange("p (t m j) -> p t m j", t=PACK, j=PACK)
-        nc.scalar.copy(first_view[:, : P // 2], raw10[0][:, 0])
-        nc.vector.tensor_copy(first_view[:, P // 2 :], raw10[1][:, 0])
-        nc.vector.quantize_mx(w1_c[:, 1, 0, :P].bitcast(FP8X4), w1_s[1, 0][:, :P], first_cols[:])
-        v_w[1, 1] = tenant("first", "v_w11", [P, BANK], U32)
-        nc.vector.tensor_copy(v_w[1, 1][:], tab_w[1][:].bitcast(U32).indirect(half(idx, 1)))
-        for e in range(2):
-            m = slice(e * P // 2, (e + 1) * P // 2)
-            nc.scalar.copy(other_view[:, 1, m], raw10[e][:, 1])
-            nc.scalar.copy(
-                other_view[:, 2:4, m].rearrange("p t m j -> p m j t"), raw10[e][:, 2:4].rearrange("p t m j -> p m j t")
-            )
-        w1_s_slice1 = tenant("chain0", "w1_s_slice1", [P, P], U8)
-        nc.vector.quantize_mx(w1_c[:, 1, 0, P : 2 * P].bitcast(FP8X4), w1_s_slice1[:], other_cols[:, KP : 2 * KP])
-        nc.vector.quantize_mx(w1_c[:, 1, 0, 2 * P :].bitcast(FP8X4), w1_s[1, 0][:, 2 * P :], other_cols[:, 2 * KP :])
-        make_identity(nc, ident[:])
-
-        left, right = slice(0, TURNED * BANK), slice(TURNED * BANK, T2)
-        old_left, old_right, raw_second = [], [], []
-        load_wg(0, slice(BANK, S))
-        for t in range(PACK):
-            if t + 1 < PACK:
-                load_wg(t + 1, slice(0, S))
-            old_left.append(load_old_slice(t, "left%d" % t, left))
-            if t < 2:
-                raw_second.append(load_w1(t, 1))
-            old_right.append(load_old_slice(t, "right%d" % t, right))
         nc.sync.dma_start(w4_w[:].bitcast(I32), w4_words.rearrange("a p n -> p a n").bitcast(I32))
         for q in range(4):
             nc.sync.dma_start(
@@ -164,49 +131,135 @@ def tile_list_recommender_slot_memory_kernel(
         with nc.allow_non_contiguous_dma(reason="one bias value a partition"):
             nc.sync.dma_start(b4_t[:, :, 0:1], b4.rearrange("(i p o) -> p i o", p=P, o=1))
 
-        def w1_scale(a, b, t):
-            if (a, b, t) == (1, 0, 1):
-                return w1_s_slice1[:]
-            return w1_s[a, b][:, t * P : (t + 1) * P]
+        w1_c, w1_s = {}, {}
+
+        def quantise_w1(slices, grouped):
+            n = len(slices)
+            codes = held.tile([P, 2 * n * P], U32, name="w1_c%d" % slices[0], align_bytes=64)
+            scales = held.tile([P, 2 * n * P], U8, name="w1_s%d" % slices[0], align_bytes=64)
+            nc.vector.quantize_mx(codes[:].bitcast(FP8X4), scales[:], grouped[:, : 2 * n * KP])
+            for a in range(2):
+                for k, s in enumerate(slices):
+                    at = (a * n + k) * P
+                    w1_c[a, s] = codes[:, at : at + P]
+                    w1_s[a, s] = scales[:, at : at + P]
+
+        def cast_rows(raws, lo, width, grouped):
+            for a in range(2):
+                nc.scalar.copy(
+                    grouped[:, a * width * PACK : (a + 1) * width * PACK].rearrange("p (c i j) -> p c j i", i=4, j=PACK),
+                    raws[a][:, :, lo : lo + width].rearrange("p j (c i) -> p c j i", i=4),
+                )
+            return grouped
+
+        def half(entries, e):
+            return entries[:, e * BANK // 16 : (e + 1) * BANK // 16]
+
+        for e in range(2):
+            nc.vector.tensor_copy(v_s[e][:], tab_s[:].indirect(half(idx, e)))
+        for e in range(2):
+            nc.vector.tensor_copy(v_w[0, e][:], tab_w[0][:].bitcast(U32).indirect(half(idx, e)))
+        quantise_w1([0], cast_rows(raw_first, 0, P, quantiser_input("ring0")))
+        for e in range(2):
+            nc.vector.tensor_copy(v_w[1, e][:], tab_w[1][:].bitcast(U32).indirect(half(idx, e)))
+        nc.vector.tensor_scalar(minus_first[:], wg_rows[:, :BANK], -1.0, None, ALU.mult)
+
+        hs = {}
 
         def first_product(s):
-            b, t = divmod(s, PACK)
-            order = (0, 1) if s == 0 else (1, 0)
-            accs = []
+            h = tenant("h%d" % (s % PACK), "h", [P, S], F32)
+            bias = b1_rows[:, s, 0:1] if s < PACK else b1_dealt[:, s - PACK : s - PACK + 1]
             for e in range(2):
-                acc = bank("product", "acc")
-                for a in order:
+                acc = bank(e, "acc")
+                for a in range(2):
                     nc.tensor.matmul_mx(
                         acc[:],
-                        lhsT=w1_c[:, a, b, t * P : (t + 1) * P].bitcast(FP8X4),
-                        lhsT_scale=w1_scale(a, b, t),
+                        lhsT=w1_c[a, s].bitcast(FP8X4),
+                        lhsT_scale=w1_s[a, s],
                         rhs=v_w[a, e][:].bitcast(FP8X4),
                         rhs_scale=v_s[e][4 * a :, :],
-                        start=(a == order[0]),
-                        stop=(a == order[1]),
+                        start=(a == 0),
+                        stop=(a == 1),
                     )
-                accs.append(acc)
-            return accs
+                nc.scalar.activation(h[:, e * BANK : (e + 1) * BANK], acc[:], ACT.Abs, bias=bias)
+            hs[s] = h
 
-        def magnitude(s, accs, room):
-            b, t = divmod(s, PACK)
-            h = tenant(room, "h", [P, S], F32)
+        def scatter_half(e, weights):
+            cols = slice(e * BANK, (e + 1) * BANK)
+            nc.vector.tensor_tensor(page[0][:].indirect(half(idx2, e)), hs[0][:, cols], weights, ALU.mult)
+
+        first_product(0)
+        scatter_half(0, minus_first[:])
+        quantise_w1([1, 2], cast_rows(raw_rest, 0, 2 * P, quantiser_input("ring1")))
+        quantise_w1([3], cast_rows(raw_rest, 2 * P, P, tenant("weights", "w1_grouped", [P, 2 * KP], BF16)))
+        minus_wg = tenant("weights", "minus_wg", [P, S], F32)
+        nc.vector.tensor_scalar(minus_wg[:], wg_rows[:], -1.0, None, ALU.mult)
+        first_product(1)
+        scatter_half(1, minus_wg[:, BANK:])
+        first_product(2)
+
+        def scatter(s):
+            weights = minus_wg[:] if s < PACK else wg_dealt[:, s - PACK, :]
+            nc.vector.tensor_tensor(page[s][:].indirect(idx2[:]), hs[s][:], weights, ALU.mult)
+
+        dealt_grouped = []
+        for a in range(2):
+            grouped = quantiser_input(("ring2", "ring0")[a])
             for e in range(2):
-                nc.scalar.activation(h[:, e * BANK : (e + 1) * BANK], accs[e][:], ACT.Abs, bias=b1_t[:, b, t : t + 1])
-            return h
+                nc.scalar.copy(
+                    grouped[:].rearrange("p (u i m j) -> p u m j i", u=2, i=2, j=PACK)[:, :, e * P // 2 : (e + 1) * P // 2],
+                    raw_dealt[a, e][:].rearrange("p j (m u i) -> p u m j i", u=2, i=2),
+                )
+            dealt_grouped.append(grouped)
 
-        def scatter(s, h):
-            t = s % PACK
-            if s == 0:
-                for e in range(2):
-                    cols = slice(e * BANK, (e + 1) * BANK)
-                    nc.vector.tensor_tensor(page[t][:].indirect(half(idx2, e)), h[:, cols], wg[t][:, cols], ALU.mult)
-            else:
-                nc.vector.tensor_tensor(page[t][:].indirect(idx2[:]), h[:], wg[t][:], ALU.mult)
+        def quantise_dealt(a):
+            codes = held.tile([P, KP], U32, name="w1_cd%d" % a, align_bytes=64)
+            scales = held.tile([P, KP], U8, name="w1_sd%d" % a, align_bytes=64)
+            nc.vector.quantize_mx(codes[:].bitcast(FP8X4), scales[:], dealt_grouped[a][:])
+            for t in range(PACK):
+                w1_c[a, PACK + t] = codes[:, t * P : (t + 1) * P]
+                w1_s[a, PACK + t] = scales[:, t * P : (t + 1) * P]
 
-        def side_by_side(slices, on_vector):
+        turned = [
+            [tenant("big%d%d" % (c, k), "turned", [P, BLOCKS, PACK, P], F32) for k in range(2)] for c in range(CHUNKS)
+        ]
+
+        def add_transposed(dst, first, second):
+            nc.tensor.matmul(dst, first, ident[:], start=True, stop=False, is_transpose=True)
+            nc.tensor.matmul(dst, second, ident[:], start=False, stop=True, is_transpose=True)
+
+        def turned_out(dst, src, scale):
+            nc.scalar.activation(dst, src.rearrange("p (i m t) -> p i t m", i=BLOCKS, t=PACK), ACT.Relu, scale=scale)
+
+        def turn(s):
+            quarter = slice(32 * s, 32 * s + 32)
+            for c in range(CHUNKS):
+                difference = bank(c, "difference")
+                for i in range(BLOCKS):
+                    cols = slice(c * BANK + i * P, c * BANK + (i + 1) * P)
+                    add_transposed(difference[:, i * P : (i + 1) * P], olds[s][:, cols], page[s][:, cols])
+                turned_out(turned[c][0][:, :, :, quarter], difference[:], 1.0)
+            for c in range(CHUNKS):
+                copied = bank(c, "copied")
+                for i in range(BLOCKS):
+                    cols = slice(c * BANK + i * P, c * BANK + (i + 1) * P)
+                    nc.tensor.transpose(copied[:, i * P : (i + 1) * P], page[s][:, cols], ident[:])
+                turned_out(turned[c][1][:, :, :, quarter], copied[:], -1.0)
+
+        def turn_back(c, banks, room):
+            words = quantiser_input(room)
+            for i in range(BLOCKS):
+                larger = bank(banks[i], "larger")
+                for t in range(PACK):
+                    add_transposed(larger[:, t * P : (t + 1) * P], turned[c][1][:, i, t, :], turned[c][0][:, i, t, :])
+                nc.scalar.copy(
+                    words[:, i * BANK : (i + 1) * BANK].rearrange("p (c t) -> p c t", t=PACK),
+                    larger[:].rearrange("p (t c) -> p c t", t=PACK),
+                )
+            return words[:]
+
+        def side_by_side(slices, on_vector, words):
             width = slices.shape[2]
-            words = quantiser_input("z_words")
             dst = words[:, : PACK * width].rearrange("p (c i t) -> p c t i", i=4, t=PACK)
             src = slices.rearrange("p t (c i) -> p c t i", i=4)
             if on_vector < width // 4:
@@ -215,107 +268,41 @@ def tile_list_recommender_slot_memory_kernel(
                 nc.vector.tensor_copy(dst[:, :on_vector], src[:, :on_vector])
             return words[:, : PACK * width]
 
-        z_c = {}
-
         def quantise_z(b, c, words, lo=0, width=BANK):
             nc.vector.quantize_mx(z_c[b, c][:, lo : lo + width].bitcast(FP8X4), z_s[b][c][:, lo : lo + width], words)
 
-        def larger_on_vector(t):
+        z1_chunks = z1[:].rearrange("p (c t w) -> p c t w", c=CHUNKS, t=PACK)
+
+        def larger_on_vector(s):
             nc.vector.tensor_tensor(
-                z0[:, :, t, :],
-                page[t][:, right].rearrange("p (c w) -> p c w", w=BANK),
-                old_right[t][:].rearrange("p (c w) -> p c w", w=BANK),
+                z1_chunks[:, :, s - PACK, :],
+                page[s][:].rearrange("p (c w) -> p c w", w=BANK),
+                olds[s][:].rearrange("p (c w) -> p c w", w=BANK),
                 ALU.max,
             )
 
-        turned = [tenant("turned%d" % c, "turned", [P, PACK, 2, BANK], F32) for c in range(TURNED)]
-        minus_old = {}
-
-        def add_transposed(dst, first, second):
-            nc.tensor.matmul(dst, first, ident[:], start=True, stop=False, is_transpose=True)
-            nc.tensor.matmul(dst, second, ident[:], start=False, stop=True, is_transpose=True)
-
-        def negate_old(t):
-            chunk0 = tenant("chain%d" % t, "minus_old", [P, BANK], F32)
-            minus_old[t] = [chunk0[:], old_left[t][:, BANK:]]
-            for c in range(TURNED):
-                nc.scalar.activation(minus_old[t][c], old_left[t][:, c * BANK : (c + 1) * BANK], ACT.Copy, scale=-1.0)
-
-        def turn_excess(t, c):
-            difference = bank("turn", "difference")
-            for i in range(BANK // P):
-                blk = slice(i * P, (i + 1) * P)
-                add_transposed(difference[:, blk], minus_old[t][c][:, blk], page[t][:, c * BANK :][:, blk])
-            nc.scalar.activation(turned[c][:, t, 0, :], difference[:], ACT.Relu, scale=-1.0)
-
-        def turn_page(t, c):
-            copied = bank("turn", "copied")
-            for i in range(BANK // P):
-                blk = slice(i * P, (i + 1) * P)
-                nc.tensor.transpose(copied[:, blk], page[t][:, c * BANK :][:, blk], ident[:])
-            nc.scalar.copy(turned[c][:, t, 1, :], copied[:])
-
-        def turn_back(c):
-            words = quantiser_input("z_words")
-            for i in range(BANK // P):
-                larger = bank("turn", "larger")
-                blk = slice(i * P, (i + 1) * P)
-                for t in range(PACK):
-                    add_transposed(larger[:, t * P : (t + 1) * P], turned[c][:, t, 1, blk], turned[c][:, t, 0, blk])
-                nc.scalar.copy(
-                    words[:, i * BANK : (i + 1) * BANK].rearrange("p (c t) -> p c t", t=PACK),
-                    larger[:].rearrange("p (t c) -> p c t", t=PACK),
-                )
-            return words[:]
-
-        def load_old_chunk(c):
-            cols = tenant("chain%d" % c, "old_cols", [P, PACK, BANK], F32)
-            nc.sync.dma_start(cols[:], old[KP:, c * BANK : (c + 1) * BANK].rearrange("(p t) c -> p t c", t=PACK))
-            return cols
-
-        z_right = held.tile([P, CHUNKS - TURNED, BANK], U32, name="z_right", align_bytes=64)
-        for c in range(TURNED, CHUNKS):
-            z_c[0, c] = z_right[:, c - TURNED, :]
-        products = {s: first_product(s) for s in range(2)}
-        hs = {s: magnitude(s, products[s], "page%d" % (s + 2)) for s in range(2)}
-        negate_old(0)
-        old_chunk, left_words = {}, {}
-        for s in range(SLICES):
-            scatter(s, hs[s])
-            if s < 2:
-                page.append(tenant("page%d" % (s + 2), "late_page", [P, T2], F32))
-                nc.gpsimd.memset(page[s + 2][:], 0.0)
+        for s in range(PACK):
+            scatter(s + 1)
+            if s == 1:
+                for a in range(2):
+                    quantise_dealt(a)
+            turn(s)
+            first_product(s + 3)
+            olds[s + 3] = load_old(s + 3)
+        for s in range(PACK, SLICES - 1):
+            larger_on_vector(s)
             if s + 2 < SLICES:
-                products[s + 2] = first_product(s + 2)
-            if s < PACK:
-                larger_on_vector(s)
-                turn_excess(s, 0)
-                hs[s + 2] = magnitude(s + 2, products[s + 2], "chain%d" % s)
-                turn_excess(s, 1)
-                for c in range(TURNED):
-                    turn_page(s, c)
-                if s + 1 < PACK:
-                    negate_old(s + 1)
-                if s < 2:
-                    quantise_w1(s, 1, raw_second[s])
-            elif s == PACK:
-                hs[s + 2] = magnitude(s + 2, products[s + 2], "tab_w1")
-                left_words[0] = turn_back(0)
-                for c in range(TURNED, CHUNKS):
-                    quantise_z(0, c, side_by_side(z0[:, c - TURNED], 0))
-            elif s == PACK + 1:
-                hs[s + 2] = magnitude(s + 2, products[s + 2], "turned0")
-                left_words[1] = turn_back(1)
-            if 2 <= s < 2 + CHUNKS:
-                old_chunk[s - 2] = load_old_chunk(s - 2)
-
-        z1 = tenant("turned0", "z1", [P, PACK * T2], BF16)
-        z_left = tenant("wg3", "z_left", [P, TURNED, BANK], U32)
-        for c in range(TURNED):
-            z_c[0, c] = z_left[:, c, :]
-        z_second = tenant("tab_w0", "z_second", [P, CHUNKS, BANK], U32)
+                scatter(s + 1)
+        left_words = {}
         for c in range(CHUNKS):
-            z_c[1, c] = z_second[:, c, :]
+            left_words[c] = turn_back(c, ((4, 5, 6, 7), (2, 3, 0, 1))[c % 2], ("ring1", "ring2", "ring0", "big00")[c])
+            if c < 2:
+                z_c[0, c] = held.tile([P, BANK], U32, name="z_first%d" % c, align_bytes=64)[:]
+                quantise_z(0, c, left_words[c])
+            if c == 1:
+                first_product(7)
+                scatter(7)
+        olds[7] = load_old(7)
 
         def second_product(b, c, lo, width, accs):
             for n in range(N // P):
@@ -338,17 +325,18 @@ def tile_list_recommender_slot_memory_kernel(
                     )
 
         def open_piece(c, lo, width):
-            groups = ["turn"] * 4 if c % 2 == 0 else ["spare", "spare", "product", "product"]
-            accs = [bank(group, "score") for group in groups[lo // P : (lo + width) // P]]
+            ks = [PACK * (c % 2) + k for k in range(PACK)]
+            accs = [bank(k, "score") for k in ks[lo // P : (lo + width) // P]]
             second_product(0, c, lo, width, accs)
             return accs
 
         def piece_words(c, lo, width):
             cols = slice(c * BANK + lo, c * BANK + lo + width)
-            slices = z1[:, PACK * cols.start : PACK * cols.stop].rearrange("p (t c) -> p t c", t=PACK)
-            for t in range(PACK):
-                nc.vector.tensor_tensor(slices[:, t, :], page[t][:, cols], old_chunk[c][:, t, lo : lo + width], ALU.max)
-            return side_by_side(slices, VECTOR_SHARE if width == BANK else width // 4)
+            slices = z1_chunks[:, c, :, lo : lo + width]
+            nc.vector.tensor_tensor(slices[:, PACK - 1, :], page[7][:, cols], olds[7][:, cols], ALU.max)
+            k = pieces.index((c, lo, width))
+            words = tenant(("first0", "first1", "h0", "h1", "h2", "weights")[k], "words", [P, PACK * width], BF16)
+            return side_by_side(slices, VECTOR_SHARE[k], words)
 
         staged = {}
 
@@ -356,7 +344,7 @@ def tile_list_recommender_slot_memory_kernel(
             cols = slice(c * BANK + lo, c * BANK + lo + width)
             second_product(1, c, lo, width, accs)
             if lo == 0:
-                staged[c] = tenant("chain%d" % c, "y", [P, N // P * BANK], F32)
+                staged[c] = tenant(("big01", "big10", "big11", "big20")[c], "y", [P, N // P * BANK], F32)
             y = staged[c][:, N // P * lo : N // P * (lo + width)].rearrange("p (n c) -> p n c", n=N // P)
             for k, acc in enumerate(accs):
                 if width == BANK:
@@ -366,7 +354,7 @@ def tile_list_recommender_slot_memory_kernel(
                     for i in range(2):
                         n = 2 * k + i
                         part = acc[:, i * width : (i + 1) * width]
-                        if k == 0:
+                        if k == 0 or c == 0:
                             nc.scalar.activation(y[:, n, :], part, ACT.Identity, bias=b4_t[:, n, 0:1])
                         else:
                             nc.vector.tensor_scalar(y[:, n, :], part, b4_t[:, n, 0:1], None, ALU.add)
@@ -375,17 +363,23 @@ def tile_list_recommender_slot_memory_kernel(
                         y[:, 2 * k : 2 * k + 2, :],
                     )
 
-        pieces = [(c, 0, BANK) for c in range(CHUNKS - 1)] + [(CHUNKS - 1, lo, HALF) for lo in (0, HALF)]
-        quantise_z(0, 0, left_words[0])
-        accs = {pieces[0]: open_piece(*pieces[0])}
-        words = piece_words(*pieces[0])
-        quantise_z(0, 1, left_words[1])
-        accs[pieces[1]] = open_piece(*pieces[1])
-        for k, (c, lo, width) in enumerate(pieces):
-            quantise_z(1, c, words, lo, width)
-            if k + 1 < len(pieces):
-                words = piece_words(*pieces[k + 1])
-            close_piece(c, lo, width, accs[c, lo, width])
+        pieces = [(0, 0, HALF), (0, HALF, HALF), (1, 0, BANK), (2, 0, BANK), (3, 0, HALF), (3, HALF, HALF)]
+        accs = {}
+
+        def open_chunk(c):
+            if c > 1:
+                z_c[0, c] = tenant("first%d" % (c - 2), "codes", [P, BANK], U32)[:]
+                quantise_z(0, c, left_words[c])
             for piece in pieces:
-                if piece[0] == c + 2:
+                if piece[0] == c:
                     accs[piece] = open_piece(*piece)
+
+        open_chunk(0)
+        words = piece_words(*pieces[0])
+        for k, (c, lo, width) in enumerate(pieces):
+            following = piece_words(*pieces[k + 1]) if k + 1 < len(pieces) else None
+            quantise_z(1, c, words, lo, width)
+            words = following
+            close_piece(c, lo, width, accs[c, lo, width])
+            if k + 1 < CHUNKS:
+                open_chunk(k + 1)

@@ -14,6 +14,7 @@ HALF = BANK // 2
 SLICES = H // P
 CHUNKS = T2 // BANK
 BLOCKS = BANK // P
+TURNED_LATE = {4: (2, 3), 5: (2, 3), 6: ()}
 VECTOR_SHARE = (32, 24, 64, 128, 64, 64)
 
 F32 = mybir.dt.float32
@@ -64,32 +65,25 @@ def tile_list_recommender_slot_memory_kernel(
         ]
         z_c = {(1, c): held.tile([P, BANK], U32, name="z_c%d" % c, align_bytes=64)[:] for c in range(CHUNKS)}
         z1 = held.tile([P, PACK * T2], BF16, name="z1", align_bytes=64)
-        pages = [held.tile([P, T2], F32, name="page%d" % k) for k in range(3)]
-        page = [pages[k] for k in (0, 1, 2, 0, 1, 2, 0, 0)]
-        wg_rows = tenant("h2", "wg_rows", [P, S], F32)
-        minus_first = held.tile([P, BANK], F32, name="minus_first")
+        pages = [held.tile([P, T2], F32, name="page%d" % k) for k in range(1)]
+        minus_wg = tenant("weights", "minus_wg", [P, S], F32)
         w4_w = held.tile([P, 2, 2 * N], U8, name="w4_w", align_bytes=64)
         wg_dealt = held.tile([P, PACK, S], F32, name="wg_dealt")
-        tab_s = held.tile([P, T], U8, name="tab_s")
+        tab_s = tenant("page2", "tab_s", [P, T], U8)
+        scale_rows = tenant("page1", "scale_rows", [P, T // 4], I32)
         tab_w = [tenant("big0%d" % a, "tab_w%d" % a, [P, T], I32) for a in range(2)]
 
-        nc.gpsimd.memset(tab_s[:].bitcast(I32), 0)
-        for k in range(2):
-            nc.vector.memset(pages[k][:], 0.0)
-        nc.vector.memset(w4_s[:].rearrange("p a n -> p (a n)").bitcast(I32), 0)
-        nc.gpsimd.memset(pages[2][:], 0.0)
         make_identity(nc, ident[:])
+        nc.vector.memset(tab_s[:].bitcast(I32), 0)
+        nc.vector.memset(pages[0][:].bitcast(I32), 0)
         nc.sync.dma_start(idx[:], offs)
         for q in range(4):
-            nc.scalar.dma_start(
-                tab_s[32 * q : 32 * q + 8, :].bitcast(I32),
-                tab_scales[:, 4 * q : 4 * q + 4, :].bitcast(I32),
-            )
+            nc.sync.dma_start(scale_rows[32 * q : 32 * q + 8, :], tab_scales[:, 4 * q : 4 * q + 4, :].bitcast(I32))
+        for q in range(4):
+            rows = slice(32 * q, 32 * q + 8)
+            nc.vector.tensor_copy(tab_s[rows, :].bitcast(I32), scale_rows[rows, :])
+        nc.gpsimd.memset(w4_s[:].rearrange("p a n -> p (a n)").bitcast(I32), 0)
         tab_words_i = tab_words.rearrange("a p t i -> a p (t i)").bitcast(I32)
-        with nc.allow_non_contiguous_dma(reason="one bias value a partition"):
-            nc.sync.dma_start(b1_rows[:, :, 0:1], b1[:KP].rearrange("(s p o) -> p s o", p=P, o=1))
-        nc.sync.dma_start(idx2[:], offs2)
-        nc.sync.dma_start(b1_dealt[:], b1[KP:].rearrange("(p t) -> p t", t=PACK))
 
         def load_w1(room, a, cols):
             raw = tenant(room, "w1_raw", [P, PACK, cols.stop - cols.start], F32)
@@ -107,21 +101,21 @@ def tile_list_recommender_slot_memory_kernel(
         nc.sync.dma_start(tab_w[0][:], tab_words_i[0])
         raw_first = [load_w1("first%d" % a, a, slice(0, P)) for a in range(2)]
         nc.sync.dma_start(tab_w[1][:], tab_words_i[1])
-        nc.sync.dma_start(wg_rows[:, :BANK], wgs[:, :BANK])
-        raw_rest = [load_w1("big1%d" % a, a, slice(P, KP)) for a in range(2)]
-        nc.sync.dma_start(wg_rows[:, BANK:], wgs[:, BANK:])
-        olds = {0: load_old(0)}
+        nc.sync.dma_start(minus_wg[:], wgs)
+        with nc.allow_non_contiguous_dma(reason="one bias value a partition"):
+            nc.sync.dma_start(b1_rows[:, 0, 0:1], b1[:P].rearrange("(p o) -> p o", o=1))
+        nc.sync.dma_start(idx2[:], offs2)
+        raw_second = [load_w1(room, a, slice(P, 2 * P)) for a, room in enumerate(("big10", "h0_second"))]
+        raw_rest = [load_w1(room, a, slice(2 * P, KP)) for a, room in enumerate(("big11", "h1"))]
+        with nc.allow_non_contiguous_dma(reason="one bias value a partition"):
+            nc.sync.dma_start(b1_rows[:, 1:, 0:1], b1[P:KP].rearrange("(s p o) -> p s o", p=P, o=1))
         raw_dealt = {
-            (a, e): load_w1(("big20", "big21", "big30", "h3")[2 * a + e], a, slice(KP + e * HALF, KP + (e + 1) * HALF))
+            (a, e): load_w1(("big20", "big21", "big30", "h2")[2 * a + e], a, slice(KP + e * HALF, KP + (e + 1) * HALF))
             for a in range(2)
             for e in range(2)
         }
-        for s in (1, 2):
-            olds[s] = load_old(s)
-        for g in (0, 2, 1, 3):
-            nc.sync.dma_start(
-                wg_dealt[32 * g : 32 * g + 32].rearrange("p t s -> p (t s)"), wgs.rearrange("(q t) s -> q (t s)", t=PACK)
-            )
+        olds = {s: load_old(s) for s in range(3)}
+        nc.sync.dma_start(b1_dealt[:], b1[KP:].rearrange("(p t) -> p t", t=PACK))
         nc.sync.dma_start(w4_w[:].bitcast(I32), w4_words.rearrange("a p n -> p a n").bitcast(I32))
         for q in range(4):
             nc.sync.dma_start(
@@ -157,20 +151,26 @@ def tile_list_recommender_slot_memory_kernel(
 
         for e in range(2):
             nc.vector.tensor_copy(v_s[e][:], tab_s[:].indirect(half(idx, e)))
+        for k in (1, 2):
+            pages.append(tenant("page%d" % k, "page", [P, T2], F32))
+            nc.gpsimd.memset(pages[k][:].bitcast(I32), 0)
+        page = [pages[k] for k in (0, 1, 2, 0, 1, 2, 0, 0)]
         for e in range(2):
             nc.vector.tensor_copy(v_w[0, e][:], tab_w[0][:].bitcast(U32).indirect(half(idx, e)))
         quantise_w1([0], cast_rows(raw_first, 0, P, quantiser_input("ring0")))
         for e in range(2):
             nc.vector.tensor_copy(v_w[1, e][:], tab_w[1][:].bitcast(U32).indirect(half(idx, e)))
-        nc.vector.tensor_scalar(minus_first[:], wg_rows[:, :BANK], -1.0, None, ALU.mult)
+        for e in range(2):
+            cols = slice(e * BANK, (e + 1) * BANK)
+            nc.gpsimd.tensor_scalar(minus_wg[:, cols], minus_wg[:, cols], -1.0, 0.0, ALU.mult, ALU.add)
 
         hs = {}
 
-        def first_product(s):
-            h = tenant("h%d" % (s % PACK), "h", [P, S], F32)
+        def first_product(s, halves=(0, 1), room=None, banks=(0, 1)):
+            h = tenant(room or "h%d" % (s % PACK), "h", [P, len(halves) * BANK], F32)
             bias = b1_rows[:, s, 0:1] if s < PACK else b1_dealt[:, s - PACK : s - PACK + 1]
-            for e in range(2):
-                acc = bank(e, "acc")
+            for k, e in enumerate(halves):
+                acc = bank(banks[e], "acc")
                 for a in range(2):
                     nc.tensor.matmul_mx(
                         acc[:],
@@ -181,22 +181,23 @@ def tile_list_recommender_slot_memory_kernel(
                         start=(a == 0),
                         stop=(a == 1),
                     )
-                nc.scalar.activation(h[:, e * BANK : (e + 1) * BANK], acc[:], ACT.Abs, bias=bias)
+                nc.scalar.activation(h[:, k * BANK : (k + 1) * BANK], acc[:], ACT.Abs, bias=bias)
             hs[s] = h
 
-        def scatter_half(e, weights):
-            cols = slice(e * BANK, (e + 1) * BANK)
-            nc.vector.tensor_tensor(page[0][:].indirect(half(idx2, e)), hs[0][:, cols], weights, ALU.mult)
+        def scatter_half(e):
+            weights = minus_wg[:, e * BANK : (e + 1) * BANK]
+            nc.vector.tensor_tensor(page[0][:].indirect(half(idx2, e)), hs[0][:], weights, ALU.mult)
 
-        first_product(0)
-        scatter_half(0, minus_first[:])
-        quantise_w1([1, 2], cast_rows(raw_rest, 0, 2 * P, quantiser_input("ring1")))
-        quantise_w1([3], cast_rows(raw_rest, 2 * P, P, tenant("weights", "w1_grouped", [P, 2 * KP], BF16)))
-        minus_wg = tenant("weights", "minus_wg", [P, S], F32)
-        nc.vector.tensor_scalar(minus_wg[:], wg_rows[:], -1.0, None, ALU.mult)
+        first_product(0, (0,))
+        scatter_half(0)
+        quantise_w1([1], cast_rows(raw_second, 0, P, quantiser_input("ring1")))
+        first_product(0, (1,), "h0_second")
+        scatter_half(1)
+        quantise_w1([2, 3], cast_rows(raw_rest, 0, 2 * P, quantiser_input("ring2")))
+        for t in range(PACK):
+            for g in (0, 2, 1, 3):
+                nc.sync.dma_start(wg_dealt[32 * g : 32 * g + 32, t, :], minus_wg[t:P:PACK, :])
         first_product(1)
-        scatter_half(1, minus_wg[:, BANK:])
-        first_product(2)
 
         def scatter(s):
             weights = minus_wg[:] if s < PACK else wg_dealt[:, s - PACK, :]
@@ -204,7 +205,7 @@ def tile_list_recommender_slot_memory_kernel(
 
         dealt_grouped = []
         for a in range(2):
-            grouped = quantiser_input(("ring2", "ring0")[a])
+            grouped = quantiser_input("ring%d" % a)
             for e in range(2):
                 nc.scalar.copy(
                     grouped[:].rearrange("p (u i m j) -> p u m j i", u=2, i=2, j=PACK)[:, :, e * P // 2 : (e + 1) * P // 2],
@@ -233,13 +234,15 @@ def tile_list_recommender_slot_memory_kernel(
 
         def turn(s):
             quarter = slice(32 * s, 32 * s + 32)
-            for c in range(CHUNKS):
+            order = [(c + 2 * s + 2) % CHUNKS for c in range(CHUNKS)]
+            for c in order:
                 difference = bank(c, "difference")
                 for i in range(BLOCKS):
                     cols = slice(c * BANK + i * P, c * BANK + (i + 1) * P)
                     add_transposed(difference[:, i * P : (i + 1) * P], olds[s][:, cols], page[s][:, cols])
                 turned_out(turned[c][0][:, :, :, quarter], difference[:], 1.0)
-            for c in range(CHUNKS):
+            first_product(s + 3, banks=order[:2])
+            for c in order[2:] + order[:2]:
                 copied = bank(c, "copied")
                 for i in range(BLOCKS):
                     cols = slice(c * BANK + i * P, c * BANK + (i + 1) * P)
@@ -274,20 +277,47 @@ def tile_list_recommender_slot_memory_kernel(
         z1_chunks = z1[:].rearrange("p (c t w) -> p c t w", c=CHUNKS, t=PACK)
 
         def larger_on_vector(s):
-            nc.vector.tensor_tensor(
-                z1_chunks[:, :, s - PACK, :],
-                page[s][:].rearrange("p (c w) -> p c w", w=BANK),
-                olds[s][:].rearrange("p (c w) -> p c w", w=BANK),
+            n = CHUNKS - len(TURNED_LATE[s])
+            nc.vector.scalar_tensor_tensor(
+                z1_chunks[:, :n, s - PACK, :],
+                page[s][:, : n * BANK].rearrange("p (c w) -> p c w", w=BANK),
+                -1.0,
+                olds[s][:, : n * BANK].rearrange("p (c w) -> p c w", w=BANK),
+                ALU.mult,
                 ALU.max,
             )
 
+        def turn_late(s, rooms_of_planes):
+            planes = {c: tenant(room, "planes", [P, 2, BANK], F32) for c, room in zip(TURNED_LATE[s], rooms_of_planes)}
+            for c in TURNED_LATE[s]:
+                difference = bank(c % 2, "difference")
+                for i in range(BLOCKS):
+                    cols = slice(c * BANK + i * P, c * BANK + (i + 1) * P)
+                    add_transposed(difference[:, i * P : (i + 1) * P], olds[s][:, cols], page[s][:, cols])
+                nc.scalar.activation(planes[c][:, 0, :], difference[:], ACT.Relu)
+            for c in TURNED_LATE[s]:
+                copied = bank(c % 2, "copied")
+                for i in range(BLOCKS):
+                    cols = slice(c * BANK + i * P, c * BANK + (i + 1) * P)
+                    nc.tensor.transpose(copied[:, i * P : (i + 1) * P], page[s][:, cols], ident[:])
+                nc.scalar.activation(planes[c][:, 1, :], copied[:], ACT.Relu, scale=-1.0)
+            return planes
+
+        def turn_late_back(s, planes):
+            for c in TURNED_LATE[s]:
+                larger = bank(c % 2, "larger")
+                for i in range(BLOCKS):
+                    blk = slice(i * P, (i + 1) * P)
+                    add_transposed(larger[:, blk], planes[c][:, 1, blk], planes[c][:, 0, blk])
+                nc.scalar.copy(z1_chunks[:, c, s - PACK, :], larger[:])
+
+        first_product(2)
         for s in range(PACK):
             scatter(s + 1)
-            if s == 1:
+            if s == 0:
                 for a in range(2):
                     quantise_dealt(a)
             turn(s)
-            first_product(s + 3)
             olds[s + 3] = load_old(s + 3)
         for s in range(PACK, SLICES - 1):
             larger_on_vector(s)
@@ -295,13 +325,17 @@ def tile_list_recommender_slot_memory_kernel(
                 scatter(s + 1)
         left_words = {}
         for c in range(CHUNKS):
-            left_words[c] = turn_back(c, ((4, 5, 6, 7), (2, 3, 0, 1))[c % 2], ("ring1", "ring2", "ring0", "big00")[c])
+            left_words[c] = turn_back(c, ((4, 5, 6, 7), (2, 3, 0, 1))[c % 2], ("ring2", "ring0", "ring1", "big00")[c])
             if c < 2:
                 z_c[0, c] = held.tile([P, BANK], U32, name="z_first%d" % c, align_bytes=64)[:]
                 quantise_z(0, c, left_words[c])
             if c == 1:
                 first_product(7)
                 scatter(7)
+                turn_late_back(4, turn_late(4, ("first_planes", "h0")))
+            if c == 2:
+                planes = turn_late(5, ("first_planes", "h1"))
+        turn_late_back(5, planes)
         olds[7] = load_old(7)
 
         def second_product(b, c, lo, width, accs):
@@ -333,7 +367,9 @@ def tile_list_recommender_slot_memory_kernel(
         def piece_words(c, lo, width):
             cols = slice(c * BANK + lo, c * BANK + lo + width)
             slices = z1_chunks[:, c, :, lo : lo + width]
-            nc.vector.tensor_tensor(slices[:, PACK - 1, :], page[7][:, cols], olds[7][:, cols], ALU.max)
+            nc.vector.scalar_tensor_tensor(
+                slices[:, PACK - 1, :], page[7][:, cols], -1.0, olds[7][:, cols], ALU.mult, ALU.max
+            )
             k = pieces.index((c, lo, width))
             words = tenant(("first0", "first1", "h0", "h1", "h2", "weights")[k], "words", [P, PACK * width], BF16)
             return side_by_side(slices, VECTOR_SHARE[k], words)

@@ -14,7 +14,6 @@ HALF = BANK // 2
 SLICES = H // P
 CHUNKS = T2 // BANK
 BLOCKS = BANK // P
-TURNED_LATE = {4: (2, 3), 5: (2, 3), 6: ()}
 VECTOR_SHARE = (32, 24, 64, 128, 64, 64)
 
 F32 = mybir.dt.float32
@@ -64,7 +63,7 @@ def tile_list_recommender_slot_memory_kernel(
             [held.tile([P, BANK], U8, name="z_s%d%d" % (b, c), align_bytes=64) for c in range(CHUNKS)] for b in range(2)
         ]
         z_c = {(1, c): held.tile([P, BANK], U32, name="z_c%d" % c, align_bytes=64)[:] for c in range(CHUNKS)}
-        z1 = held.tile([P, PACK * T2], BF16, name="z1", align_bytes=64)
+        z1_early = held.tile([P, CHUNKS, PACK, BANK], BF16, name="z1_early", align_bytes=64)
         pages = [held.tile([P, T2], F32, name="page%d" % k) for k in range(1)]
         minus_wg = tenant("weights", "minus_wg", [P, S], F32)
         w4_w = held.tile([P, 2, 2 * N], U8, name="w4_w", align_bytes=64)
@@ -91,7 +90,7 @@ def tile_list_recommender_slot_memory_kernel(
             return raw
 
         def load_old(s):
-            rows = tenant("big31" if s == SLICES - 1 else "old%d" % (s % 3), "old_rows", [P, T2], F32)
+            rows = tenant("big21" if s == SLICES - 1 else "old%d" % (s % 3), "old_rows", [P, T2], F32)
             if s < PACK:
                 nc.sync.dma_start(rows[:], old[s * P : (s + 1) * P, :])
             else:
@@ -105,7 +104,7 @@ def tile_list_recommender_slot_memory_kernel(
         with nc.allow_non_contiguous_dma(reason="one bias value a partition"):
             nc.sync.dma_start(b1_rows[:, 0, 0:1], b1[:P].rearrange("(p o) -> p o", o=1))
         nc.sync.dma_start(idx2[:], offs2)
-        raw_second = [load_w1(room, a, slice(P, 2 * P)) for a, room in enumerate(("big10", "h0_second"))]
+        raw_second = [load_w1(room, a, slice(P, 2 * P)) for a, room in enumerate(("page3", "h0_second"))]
         raw_rest = [load_w1(room, a, slice(2 * P, KP)) for a, room in enumerate(("big11", "h1"))]
         with nc.allow_non_contiguous_dma(reason="one bias value a partition"):
             nc.sync.dma_start(b1_rows[:, 1:, 0:1], b1[P:KP].rearrange("(s p o) -> p s o", p=P, o=1))
@@ -154,7 +153,6 @@ def tile_list_recommender_slot_memory_kernel(
         for k in (1, 2):
             pages.append(tenant("page%d" % k, "page", [P, T2], F32))
             nc.gpsimd.memset(pages[k][:].bitcast(I32), 0)
-        page = [pages[k] for k in (0, 1, 2, 0, 1, 2, 0, 0)]
         for e in range(2):
             nc.vector.tensor_copy(v_w[0, e][:], tab_w[0][:].bitcast(U32).indirect(half(idx, e)))
         quantise_w1([0], cast_rows(raw_first, 0, P, quantiser_input("ring0")))
@@ -186,11 +184,13 @@ def tile_list_recommender_slot_memory_kernel(
 
         def scatter_half(e):
             weights = minus_wg[:, e * BANK : (e + 1) * BANK]
-            nc.vector.tensor_tensor(page[0][:].indirect(half(idx2, e)), hs[0][:], weights, ALU.mult)
+            nc.vector.tensor_tensor(pages[0][:].indirect(half(idx2, e)), hs[0][:], weights, ALU.mult)
 
         first_product(0, (0,))
         scatter_half(0)
         quantise_w1([1], cast_rows(raw_second, 0, P, quantiser_input("ring1")))
+        pages.append(tenant("page3", "page", [P, T2], F32))
+        nc.gpsimd.memset(pages[3][:].bitcast(I32), 0)
         first_product(0, (1,), "h0_second")
         scatter_half(1)
         quantise_w1([2, 3], cast_rows(raw_rest, 0, 2 * P, quantiser_input("ring2")))
@@ -201,7 +201,7 @@ def tile_list_recommender_slot_memory_kernel(
 
         def scatter(s):
             weights = minus_wg[:] if s < PACK else wg_dealt[:, s - PACK, :]
-            nc.vector.tensor_tensor(page[s][:].indirect(idx2[:]), hs[s][:], weights, ALU.mult)
+            nc.vector.tensor_tensor(pages[s % PACK][:].indirect(idx2[:]), hs[s][:], weights, ALU.mult)
 
         dealt_grouped = []
         for a in range(2):
@@ -229,8 +229,8 @@ def tile_list_recommender_slot_memory_kernel(
             nc.tensor.matmul(dst, first, ident[:], start=True, stop=False, is_transpose=True)
             nc.tensor.matmul(dst, second, ident[:], start=False, stop=True, is_transpose=True)
 
-        def turned_out(dst, src, scale):
-            nc.scalar.activation(dst, src.rearrange("p (i m t) -> p i t m", i=BLOCKS, t=PACK), ACT.Relu, scale=scale)
+        def turned_out(dst, src, func, scale):
+            nc.scalar.activation(dst, src.rearrange("p (i m t) -> p i t m", i=BLOCKS, t=PACK), func, scale=scale)
 
         def turn(s):
             quarter = slice(32 * s, 32 * s + 32)
@@ -239,15 +239,15 @@ def tile_list_recommender_slot_memory_kernel(
                 difference = bank(c, "difference")
                 for i in range(BLOCKS):
                     cols = slice(c * BANK + i * P, c * BANK + (i + 1) * P)
-                    add_transposed(difference[:, i * P : (i + 1) * P], olds[s][:, cols], page[s][:, cols])
-                turned_out(turned[c][0][:, :, :, quarter], difference[:], 1.0)
+                    add_transposed(difference[:, i * P : (i + 1) * P], olds[s][:, cols], pages[s % PACK][:, cols])
+                turned_out(turned[c][0][:, :, :, quarter], difference[:], ACT.Relu, 1.0)
             first_product(s + 3, banks=order[:2])
             for c in order[2:] + order[:2]:
                 copied = bank(c, "copied")
                 for i in range(BLOCKS):
                     cols = slice(c * BANK + i * P, c * BANK + (i + 1) * P)
-                    nc.tensor.transpose(copied[:, i * P : (i + 1) * P], page[s][:, cols], ident[:])
-                turned_out(turned[c][1][:, :, :, quarter], copied[:], -1.0)
+                    nc.tensor.transpose(copied[:, i * P : (i + 1) * P], pages[s % PACK][:, cols], ident[:])
+                turned_out(turned[c][1][:, :, :, quarter], copied[:], ACT.Copy, -1.0)
 
         def turn_back(c, banks, room):
             words = quantiser_input(room)
@@ -274,42 +274,16 @@ def tile_list_recommender_slot_memory_kernel(
         def quantise_z(b, c, words, lo=0, width=BANK):
             nc.vector.quantize_mx(z_c[b, c][:, lo : lo + width].bitcast(FP8X4), z_s[b][c][:, lo : lo + width], words)
 
-        z1_chunks = z1[:].rearrange("p (c t w) -> p c t w", c=CHUNKS, t=PACK)
-
-        def larger_on_vector(s):
-            n = CHUNKS - len(TURNED_LATE[s])
+        def larger_on_vector(dst, s, lo):
+            cols = slice(lo, lo + dst.shape[1] * dst.shape[2])
             nc.vector.scalar_tensor_tensor(
-                z1_chunks[:, :n, s - PACK, :],
-                page[s][:, : n * BANK].rearrange("p (c w) -> p c w", w=BANK),
+                dst,
+                pages[s % PACK][:, cols].rearrange("p (c w) -> p c w", c=dst.shape[1]),
                 -1.0,
-                olds[s][:, : n * BANK].rearrange("p (c w) -> p c w", w=BANK),
+                olds[s][:, cols].rearrange("p (c w) -> p c w", c=dst.shape[1]),
                 ALU.mult,
                 ALU.max,
             )
-
-        def turn_late(s, rooms_of_planes):
-            planes = {c: tenant(room, "planes", [P, 2, BANK], F32) for c, room in zip(TURNED_LATE[s], rooms_of_planes)}
-            for c in TURNED_LATE[s]:
-                difference = bank(c % 2, "difference")
-                for i in range(BLOCKS):
-                    cols = slice(c * BANK + i * P, c * BANK + (i + 1) * P)
-                    add_transposed(difference[:, i * P : (i + 1) * P], olds[s][:, cols], page[s][:, cols])
-                nc.scalar.activation(planes[c][:, 0, :], difference[:], ACT.Relu)
-            for c in TURNED_LATE[s]:
-                copied = bank(c % 2, "copied")
-                for i in range(BLOCKS):
-                    cols = slice(c * BANK + i * P, c * BANK + (i + 1) * P)
-                    nc.tensor.transpose(copied[:, i * P : (i + 1) * P], page[s][:, cols], ident[:])
-                nc.scalar.activation(planes[c][:, 1, :], copied[:], ACT.Relu, scale=-1.0)
-            return planes
-
-        def turn_late_back(s, planes):
-            for c in TURNED_LATE[s]:
-                larger = bank(c % 2, "larger")
-                for i in range(BLOCKS):
-                    blk = slice(i * P, (i + 1) * P)
-                    add_transposed(larger[:, blk], planes[c][:, 1, blk], planes[c][:, 0, blk])
-                nc.scalar.copy(z1_chunks[:, c, s - PACK, :], larger[:])
 
         first_product(2)
         for s in range(PACK):
@@ -320,7 +294,8 @@ def tile_list_recommender_slot_memory_kernel(
             turn(s)
             olds[s + 3] = load_old(s + 3)
         for s in range(PACK, SLICES - 1):
-            larger_on_vector(s)
+            larger_on_vector(z1_early[:, : CHUNKS - 1, s - PACK, :], s, 0)
+            larger_on_vector(z1_early[:, CHUNKS - 1 :, s - PACK, :HALF], s, T2 - BANK)
             if s + 2 < SLICES:
                 scatter(s + 1)
         left_words = {}
@@ -332,10 +307,6 @@ def tile_list_recommender_slot_memory_kernel(
             if c == 1:
                 first_product(7)
                 scatter(7)
-                turn_late_back(4, turn_late(4, ("first_planes", "h0")))
-            if c == 2:
-                planes = turn_late(5, ("first_planes", "h1"))
-        turn_late_back(5, planes)
         olds[7] = load_old(7)
 
         def second_product(b, c, lo, width, accs):
@@ -365,11 +336,12 @@ def tile_list_recommender_slot_memory_kernel(
             return accs
 
         def piece_words(c, lo, width):
-            cols = slice(c * BANK + lo, c * BANK + lo + width)
-            slices = z1_chunks[:, c, :, lo : lo + width]
-            nc.vector.scalar_tensor_tensor(
-                slices[:, PACK - 1, :], page[7][:, cols], -1.0, olds[7][:, cols], ALU.mult, ALU.max
-            )
+            if (c, lo, width) == pieces[-1]:
+                slices, missing = tenant("h1", "z1_late", [P, PACK, HALF], BF16)[:], range(PACK, SLICES)
+            else:
+                slices, missing = z1_early[:, c, :, lo : lo + width], [SLICES - 1]
+            for s in missing:
+                larger_on_vector(slices[:, s - PACK : s - PACK + 1, :], s, c * BANK + lo)
             k = pieces.index((c, lo, width))
             words = tenant(("first0", "first1", "h0", "h1", "h2", "weights")[k], "words", [P, PACK * width], BF16)
             return side_by_side(slices, VECTOR_SHARE[k], words)

@@ -14,6 +14,7 @@ HALF = BANK // 2
 SLICES = H // P
 CHUNKS = T2 // BANK
 BLOCKS = BANK // P
+TURNED_LATE = (4, 5)
 VECTOR_SHARE = (32, 24, 64, 128, 64, 64)
 
 F32 = mybir.dt.float32
@@ -285,6 +286,27 @@ def tile_list_recommender_slot_memory_kernel(
                 ALU.max,
             )
 
+        def turn_late(s, room):
+            c = CHUNKS - 2
+            planes = tenant(room, "planes", [P, 2, BANK], F32)
+            difference, copied = bank(0, "difference"), bank(1, "copied")
+            for i in range(BLOCKS):
+                cols = slice(c * BANK + i * P, c * BANK + (i + 1) * P)
+                add_transposed(difference[:, i * P : (i + 1) * P], olds[s][:, cols], pages[s % PACK][:, cols])
+            nc.scalar.activation(planes[:, 0, :], difference[:], ACT.Relu)
+            for i in range(BLOCKS):
+                cols = slice(c * BANK + i * P, c * BANK + (i + 1) * P)
+                nc.tensor.transpose(copied[:, i * P : (i + 1) * P], pages[s % PACK][:, cols], ident[:])
+            nc.scalar.activation(planes[:, 1, :], copied[:], ACT.Copy, scale=-1.0)
+            return planes
+
+        def turn_late_back(s, planes, k):
+            larger = bank(k, "larger")
+            for i in range(BLOCKS):
+                blk = slice(i * P, (i + 1) * P)
+                add_transposed(larger[:, blk], planes[:, 1, blk], planes[:, 0, blk])
+            nc.scalar.copy(z1_early[:, CHUNKS - 2, s - PACK, :], larger[:])
+
         first_product(2)
         for s in range(PACK):
             scatter(s + 1)
@@ -294,19 +316,22 @@ def tile_list_recommender_slot_memory_kernel(
             turn(s)
             olds[s + 3] = load_old(s + 3)
         for s in range(PACK, SLICES - 1):
-            larger_on_vector(z1_early[:, : CHUNKS - 1, s - PACK, :], s, 0)
+            larger_on_vector(z1_early[:, : CHUNKS - 1 - (s in TURNED_LATE), s - PACK, :], s, 0)
             larger_on_vector(z1_early[:, CHUNKS - 1 :, s - PACK, :HALF], s, T2 - BANK)
             if s + 2 < SLICES:
                 scatter(s + 1)
         left_words = {}
         for c in range(CHUNKS):
-            left_words[c] = turn_back(c, ((4, 5, 6, 7), (2, 3, 0, 1))[c % 2], ("ring2", "ring0", "ring1", "big00")[c])
+            left_words[c] = turn_back(c, ((4, 5, 6, 7), (2, 3, 0, 1), (4, 5, 0, 1), (2, 3, 6, 7))[c], ("ring2", "ring0", "ring1", "big00")[c])
             if c < 2:
                 z_c[0, c] = held.tile([P, BANK], U32, name="z_first%d" % c, align_bytes=64)[:]
                 quantise_z(0, c, left_words[c])
             if c == 1:
                 first_product(7)
                 scatter(7)
+                planes = [turn_late(s, "h%d" % (s % PACK)) for s in TURNED_LATE]
+                for k, s in enumerate(TURNED_LATE):
+                    turn_late_back(s, planes[k], k)
         olds[7] = load_old(7)
 
         def second_product(b, c, lo, width, accs):

@@ -68,7 +68,6 @@ def tile_list_recommender_slot_memory_kernel(
         pages = [held.tile([P, T2], F32, name="page%d" % k) for k in range(1)]
         minus_wg = tenant("weights", "minus_wg", [P, S], F32)
         w4_w = held.tile([P, 2, 2 * N], U8, name="w4_w", align_bytes=64)
-        wg_dealt = held.tile([P, PACK, S], F32, name="wg_dealt")
         tab_s = tenant("page2", "tab_s", [P, T], U8)
         scale_rows = tenant("page1", "scale_rows", [P, T // 4], I32)
         tab_w = [tenant("big0%d" % a, "tab_w%d" % a, [P, T], I32) for a in range(2)]
@@ -109,12 +108,14 @@ def tile_list_recommender_slot_memory_kernel(
         raw_rest = [load_w1(room, a, slice(2 * P, KP)) for a, room in enumerate(("big11", "h1"))]
         with nc.allow_non_contiguous_dma(reason="one bias value a partition"):
             nc.sync.dma_start(b1_rows[:, 1:, 0:1], b1[P:KP].rearrange("(s p o) -> p s o", p=P, o=1))
+        olds = {0: load_old(0)}
         raw_dealt = {
-            (a, e): load_w1(("big20", "big21", "big30", "h2")[2 * a + e], a, slice(KP + e * HALF, KP + (e + 1) * HALF))
+            (a, e): load_w1(("wg0", "wg1", "wg2", "h3")[2 * a + e], a, slice(KP + e * HALF, KP + (e + 1) * HALF))
             for a in range(2)
             for e in range(2)
         }
-        olds = {s: load_old(s) for s in range(3)}
+        for s in (1, 2):
+            olds[s] = load_old(s)
         nc.sync.dma_start(b1_dealt[:], b1[KP:].rearrange("(p t) -> p t", t=PACK))
         nc.sync.dma_start(w4_w[:].bitcast(I32), w4_words.rearrange("a p n -> p a n").bitcast(I32))
         for q in range(4):
@@ -195,24 +196,11 @@ def tile_list_recommender_slot_memory_kernel(
         first_product(0, (1,), "h0_second")
         scatter_half(1)
         quantise_w1([2, 3], cast_rows(raw_rest, 0, 2 * P, quantiser_input("ring2")))
-        for t in range(PACK):
-            for g in (0, 2, 1, 3):
-                nc.sync.dma_start(wg_dealt[32 * g : 32 * g + 32, t, :], minus_wg[t:P:PACK, :])
         first_product(1)
 
         def scatter(s):
-            weights = minus_wg[:] if s < PACK else wg_dealt[:, s - PACK, :]
+            weights = minus_wg[:] if s < PACK else wg_dealt[s - PACK][:]
             nc.vector.tensor_tensor(pages[s % PACK][:].indirect(idx2[:]), hs[s][:], weights, ALU.mult)
-
-        dealt_grouped = []
-        for a in range(2):
-            grouped = quantiser_input("ring%d" % a)
-            for e in range(2):
-                nc.scalar.copy(
-                    grouped[:].rearrange("p (u i m j) -> p u m j i", u=2, i=2, j=PACK)[:, :, e * P // 2 : (e + 1) * P // 2],
-                    raw_dealt[a, e][:].rearrange("p j (m u i) -> p u m j i", u=2, i=2),
-                )
-            dealt_grouped.append(grouped)
 
         def quantise_dealt(a):
             codes = held.tile([P, KP], U32, name="w1_cd%d" % a, align_bytes=64)
@@ -233,7 +221,7 @@ def tile_list_recommender_slot_memory_kernel(
         def turned_out(dst, src, func, scale):
             nc.scalar.activation(dst, src.rearrange("p (i m t) -> p i t m", i=BLOCKS, t=PACK), func, scale=scale)
 
-        def turn(s):
+        def turn(s, product):
             quarter = slice(32 * s, 32 * s + 32)
             order = [(c + 2 * s + 2) % CHUNKS for c in range(CHUNKS)]
             for c in order:
@@ -242,7 +230,8 @@ def tile_list_recommender_slot_memory_kernel(
                     cols = slice(c * BANK + i * P, c * BANK + (i + 1) * P)
                     add_transposed(difference[:, i * P : (i + 1) * P], olds[s][:, cols], pages[s % PACK][:, cols])
                 turned_out(turned[c][0][:, :, :, quarter], difference[:], ACT.Relu, 1.0)
-            first_product(s + 3, banks=order[:2])
+            if product:
+                first_product(product, banks=order[:2])
             for c in order[2:] + order[:2]:
                 copied = bank(c, "copied")
                 for i in range(BLOCKS):
@@ -308,18 +297,38 @@ def tile_list_recommender_slot_memory_kernel(
             nc.scalar.copy(z1_early[:, CHUNKS - 2, s - PACK, :], larger[:])
 
         first_product(2)
-        for s in range(PACK):
-            scatter(s + 1)
-            if s == 0:
-                for a in range(2):
-                    quantise_dealt(a)
-            turn(s)
+        scatter(1)
+        turn(0, None)
+        olds[3] = load_old(3)
+        dealt_grouped = []
+        for a in range(2):
+            grouped = quantiser_input("ring%d" % a)
+            for e in range(2):
+                nc.scalar.copy(
+                    grouped[:].rearrange("p (u i m j) -> p u m j i", u=2, i=2, j=PACK)[:, :, e * P // 2 : (e + 1) * P // 2],
+                    raw_dealt[a, e][:].rearrange("p j (m u i) -> p u m j i", u=2, i=2),
+                )
+            dealt_grouped.append(grouped)
+
+        wg_dealt = [tenant("wg%d" % t, "wg_dealt", [P, S], F32) for t in range(PACK)]
+        for t in range(PACK):
+            for g in (0, 2, 1, 3):
+                nc.sync.dma_start(wg_dealt[t][32 * g : 32 * g + 32, :], minus_wg[t:P:PACK, :])
+        scatter(2)
+        for a in range(2):
+            quantise_dealt(a)
+        first_product(3, banks=(4, 5))
+        for s in range(1, PACK):
+            if s == 2:
+                first_product(4, banks=(0, 1))
+            turn(s, (None, 5, 6)[s - 1])
             olds[s + 3] = load_old(s + 3)
+            scatter(s + 2)
         for s in range(PACK, SLICES - 1):
             larger_on_vector(z1_early[:, : CHUNKS - 1 - (s in TURNED_LATE), s - PACK, :], s, 0)
             larger_on_vector(z1_early[:, CHUNKS - 1 :, s - PACK, :HALF], s, T2 - BANK)
-            if s + 2 < SLICES:
-                scatter(s + 1)
+            if s == PACK:
+                scatter(s + 2)
         left_words = {}
         for c in range(CHUNKS):
             left_words[c] = turn_back(c, ((4, 5, 6, 7), (2, 3, 0, 1), (4, 5, 0, 1), (2, 3, 6, 7))[c], ("ring2", "ring0", "ring1", "big00")[c])

@@ -15,7 +15,7 @@ SLICES = H // P
 CHUNKS = T2 // BANK
 BLOCKS = BANK // P
 TURNED_LATE = (4, 5)
-VECTOR_SHARE = (32, 24, 64, 128, 64, 64)
+VECTOR_SHARE = (32, 24, 64, 128, 48, 48)
 
 F32 = mybir.dt.float32
 BF16 = mybir.dt.bfloat16
@@ -326,7 +326,6 @@ def tile_list_recommender_slot_memory_kernel(
             scatter(s + 2)
         for s in range(PACK, SLICES - 1):
             larger_on_vector(z1_early[:, : CHUNKS - 1 - (s in TURNED_LATE), s - PACK, :], s, 0)
-            larger_on_vector(z1_early[:, CHUNKS - 1 :, s - PACK, :HALF], s, T2 - BANK)
             if s == PACK:
                 scatter(s + 2)
         left_words = {}
@@ -369,9 +368,13 @@ def tile_list_recommender_slot_memory_kernel(
             second_product(0, c, lo, width, accs)
             return accs
 
+        late = []
+
         def piece_words(c, lo, width):
-            if (c, lo, width) == pieces[-1]:
-                slices, missing = tenant("h1", "z1_late", [P, PACK, HALF], BF16)[:], range(PACK, SLICES)
+            if c == CHUNKS - 1:
+                if lo == 0:
+                    late.append(tenant("h1", "z1_late", [P, 2, PACK, HALF], BF16))
+                slices, missing = late[0][:, lo // HALF], range(PACK, SLICES)
             else:
                 slices, missing = z1_early[:, c, :, lo : lo + width], [SLICES - 1]
             for s in missing:
@@ -396,7 +399,7 @@ def tile_list_recommender_slot_memory_kernel(
                     for i in range(2):
                         n = 2 * k + i
                         part = acc[:, i * width : (i + 1) * width]
-                        if k == 0 or c == 0:
+                        if k == 0 or (c, lo, width) != pieces[-1]:
                             nc.scalar.activation(y[:, n, :], part, ACT.Identity, bias=b4_t[:, n, 0:1])
                         else:
                             nc.vector.tensor_scalar(y[:, n, :], part, b4_t[:, n, 0:1], None, ALU.add)
@@ -419,9 +422,10 @@ def tile_list_recommender_slot_memory_kernel(
         open_chunk(0)
         words = piece_words(*pieces[0])
         for k, (c, lo, width) in enumerate(pieces):
-            following = piece_words(*pieces[k + 1]) if k + 1 < len(pieces) else None
+            ahead = k + 1 < len(pieces) and pieces[k + 1][0] < CHUNKS - 1
+            following = piece_words(*pieces[k + 1]) if ahead else None
             quantise_z(1, c, words, lo, width)
-            words = following
+            words = piece_words(*pieces[k + 1]) if k + 1 < len(pieces) and not ahead else following
             close_piece(c, lo, width, accs[c, lo, width])
             if k + 1 < CHUNKS:
                 open_chunk(k + 1)

@@ -14,7 +14,7 @@ HALF = BANK // 2
 SLICES = H // P
 CHUNKS = T2 // BANK
 BLOCKS = BANK // P
-TURNED_LATE = (4, 5)
+TURNED_LATE = (4,)
 VECTOR_SHARE = (32, 24, 64, 128, 48, 48)
 
 F32 = mybir.dt.float32
@@ -100,9 +100,10 @@ def tile_list_recommender_slot_memory_kernel(
         nc.sync.dma_start(tab_w[0][:], tab_words_i[0])
         raw_first = [load_w1("first%d" % a, a, slice(0, P)) for a in range(2)]
         nc.sync.dma_start(tab_w[1][:], tab_words_i[1])
-        nc.sync.dma_start(minus_wg[:], wgs)
+        for e in range(2):
+            nc.sync.dma_start(minus_wg[:, e * BANK : (e + 1) * BANK], wgs[:, e * BANK : (e + 1) * BANK])
         with nc.allow_non_contiguous_dma(reason="one bias value a partition"):
-            nc.sync.dma_start(b1_rows[:, 0, 0:1], b1[:P].rearrange("(p o) -> p o", o=1))
+            nc.scalar.dma_start(b1_rows[:, 0, 0:1], b1[:P].rearrange("(p o) -> p o", o=1))
         nc.sync.dma_start(idx2[:], offs2)
         raw_second = [load_w1(room, a, slice(P, 2 * P)) for a, room in enumerate(("page3", "h0_second"))]
         raw_rest = [load_w1(room, a, slice(2 * P, KP)) for a, room in enumerate(("big11", "h1"))]

@@ -14,7 +14,7 @@ HALF = BANK // 2
 SLICES = H // P
 CHUNKS = T2 // BANK
 BLOCKS = BANK // P
-TURNED_LATE = (4,)
+TURNED_LATE = (4, 5)
 VECTOR_SHARE = (32, 24, 64, 128, 48, 48)
 
 F32 = mybir.dt.float32
@@ -64,7 +64,7 @@ def tile_list_recommender_slot_memory_kernel(
             [held.tile([P, BANK], U8, name="z_s%d%d" % (b, c), align_bytes=64) for c in range(CHUNKS)] for b in range(2)
         ]
         z_c = {(1, c): held.tile([P, BANK], U32, name="z_c%d" % c, align_bytes=64)[:] for c in range(CHUNKS)}
-        z1_early = held.tile([P, CHUNKS, PACK, BANK], BF16, name="z1_early", align_bytes=64)
+        z1_early = held.tile([P, CHUNKS - 1, PACK, BANK], BF16, name="z1_early", align_bytes=64)
         pages = [held.tile([P, T2], F32, name="page%d" % k) for k in range(1)]
         minus_wg = tenant("weights", "minus_wg", [P, S], F32)
         w4_w = held.tile([P, 2, 2 * N], U8, name="w4_w", align_bytes=64)
@@ -105,13 +105,13 @@ def tile_list_recommender_slot_memory_kernel(
         with nc.allow_non_contiguous_dma(reason="one bias value a partition"):
             nc.scalar.dma_start(b1_rows[:, 0, 0:1], b1[:P].rearrange("(p o) -> p o", o=1))
         nc.sync.dma_start(idx2[:], offs2)
-        raw_second = [load_w1(room, a, slice(P, 2 * P)) for a, room in enumerate(("page3", "h0_second"))]
-        raw_rest = [load_w1(room, a, slice(2 * P, KP)) for a, room in enumerate(("big11", "h1"))]
+        raw_second = [load_w1(room, a, slice(P, 2 * P)) for a, room in enumerate(("wg0", "h0_second"))]
+        raw_rest = [load_w1(room, a, slice(2 * P, KP)) for a, room in enumerate(("big11", "h0_third"))]
         with nc.allow_non_contiguous_dma(reason="one bias value a partition"):
             nc.sync.dma_start(b1_rows[:, 1:, 0:1], b1[P:KP].rearrange("(s p o) -> p s o", p=P, o=1))
         olds = {0: load_old(0)}
         raw_dealt = {
-            (a, e): load_w1(("wg0", "wg1", "wg2", "h3")[2 * a + e], a, slice(KP + e * HALF, KP + (e + 1) * HALF))
+            (a, e): load_w1(("page3", "wg1", "wg2", "h3")[2 * a + e], a, slice(KP + e * HALF, KP + (e + 1) * HALF))
             for a in range(2)
             for e in range(2)
         }
@@ -167,37 +167,47 @@ def tile_list_recommender_slot_memory_kernel(
 
         hs = {}
 
-        def first_product(s, halves=(0, 1), room=None, banks=(0, 1)):
-            h = tenant(room or "h%d" % (s % PACK), "h", [P, len(halves) * BANK], F32)
+        def product(s, e, k):
+            acc = bank(k, "acc")
+            for a in range(2):
+                nc.tensor.matmul_mx(
+                    acc[:],
+                    lhsT=w1_c[a, s].bitcast(FP8X4),
+                    lhsT_scale=w1_s[a, s],
+                    rhs=v_w[a, e][:].bitcast(FP8X4),
+                    rhs_scale=v_s[e][4 * a :, :],
+                    start=(a == 0),
+                    stop=(a == 1),
+                )
+            return acc
+
+        def magnitude(s, dst, acc):
             bias = b1_rows[:, s, 0:1] if s < PACK else b1_dealt[:, s - PACK : s - PACK + 1]
-            for k, e in enumerate(halves):
-                acc = bank(banks[e], "acc")
-                for a in range(2):
-                    nc.tensor.matmul_mx(
-                        acc[:],
-                        lhsT=w1_c[a, s].bitcast(FP8X4),
-                        lhsT_scale=w1_s[a, s],
-                        rhs=v_w[a, e][:].bitcast(FP8X4),
-                        rhs_scale=v_s[e][4 * a :, :],
-                        start=(a == 0),
-                        stop=(a == 1),
-                    )
-                nc.scalar.activation(h[:, k * BANK : (k + 1) * BANK], acc[:], ACT.Abs, bias=bias)
-            hs[s] = h
+            nc.scalar.activation(dst, acc, ACT.Abs, bias=bias)
 
-        def scatter_half(e):
-            weights = minus_wg[:, e * BANK : (e + 1) * BANK]
-            nc.vector.tensor_tensor(pages[0][:].indirect(half(idx2, e)), hs[0][:], weights, ALU.mult)
+        def magnitudes(s, accs):
+            hs[s] = tenant("h%d" % (s % PACK), "h", [P, S], F32)
+            for e in range(2):
+                magnitude(s, hs[s][:, e * BANK : (e + 1) * BANK], accs[e][:])
 
-        first_product(0, (0,))
-        scatter_half(0)
+        def first_product(s, banks=(0, 1), room=None):
+            hs[s] = tenant(room or "h%d" % (s % PACK), "h", [P, S], F32)
+            for e in range(2):
+                magnitude(s, hs[s][:, e * BANK : (e + 1) * BANK], product(s, e, banks[e])[:])
+
+        def scatter_part(room, acc, lo, width):
+            h = tenant(room, "h", [P, width], F32)
+            magnitude(0, h[:], acc[:, lo % BANK : lo % BANK + width])
+            entries = idx2[:, lo // 16 : (lo + width) // 16]
+            nc.vector.tensor_tensor(pages[0][:].indirect(entries), h[:], minus_wg[:, lo : lo + width], ALU.mult)
+
+        scatter_part("h0", product(0, 0, 0), 0, BANK)
+        second_half = product(0, 1, 1)
         quantise_w1([1], cast_rows(raw_second, 0, P, quantiser_input("ring1")))
-        pages.append(tenant("page3", "page", [P, T2], F32))
-        nc.gpsimd.memset(pages[3][:].bitcast(I32), 0)
-        first_product(0, (1,), "h0_second")
-        scatter_half(1)
+        scatter_part("h0_second", second_half, BANK, HALF)
         quantise_w1([2, 3], cast_rows(raw_rest, 0, 2 * P, quantiser_input("ring2")))
-        first_product(1)
+        scatter_part("h0_third", second_half, BANK + HALF, HALF)
+        first_product(1, banks=(2, 3), room="ring2")
 
         def scatter(s):
             weights = minus_wg[:] if s < PACK else wg_dealt[s - PACK][:]
@@ -222,7 +232,7 @@ def tile_list_recommender_slot_memory_kernel(
         def turned_out(dst, src, func, scale):
             nc.scalar.activation(dst, src.rearrange("p (i m t) -> p i t m", i=BLOCKS, t=PACK), func, scale=scale)
 
-        def turn(s, product):
+        def turn(s, ahead):
             quarter = slice(32 * s, 32 * s + 32)
             order = [(c + 2 * s + 2) % CHUNKS for c in range(CHUNKS)]
             for c in order:
@@ -231,8 +241,8 @@ def tile_list_recommender_slot_memory_kernel(
                     cols = slice(c * BANK + i * P, c * BANK + (i + 1) * P)
                     add_transposed(difference[:, i * P : (i + 1) * P], olds[s][:, cols], pages[s % PACK][:, cols])
                 turned_out(turned[c][0][:, :, :, quarter], difference[:], ACT.Relu, 1.0)
-            if product:
-                first_product(product, banks=order[:2])
+            if ahead:
+                first_product(ahead, banks=order[:2])
             for c in order[2:] + order[:2]:
                 copied = bank(c, "copied")
                 for i in range(BLOCKS):
@@ -298,6 +308,7 @@ def tile_list_recommender_slot_memory_kernel(
             nc.scalar.copy(z1_early[:, CHUNKS - 2, s - PACK, :], larger[:])
 
         first_product(2)
+        third_accs = [product(3, e, PACK + e) for e in range(2)]
         scatter(1)
         turn(0, None)
         olds[3] = load_old(3)
@@ -311,6 +322,8 @@ def tile_list_recommender_slot_memory_kernel(
                 )
             dealt_grouped.append(grouped)
 
+        pages.append(tenant("page3", "page", [P, T2], F32))
+        nc.gpsimd.memset(pages[3][:].bitcast(I32), 0)
         wg_dealt = [tenant("wg%d" % t, "wg_dealt", [P, S], F32) for t in range(PACK)]
         for t in range(PACK):
             for g in (0, 2, 1, 3):
@@ -318,7 +331,7 @@ def tile_list_recommender_slot_memory_kernel(
         scatter(2)
         for a in range(2):
             quantise_dealt(a)
-        first_product(3, banks=(4, 5))
+        magnitudes(3, third_accs)
         for s in range(1, PACK):
             if s == 2:
                 first_product(4, banks=(0, 1))

@@ -14,8 +14,6 @@ HALF = BANK // 2
 SLICES = H // P
 CHUNKS = T2 // BANK
 BLOCKS = BANK // P
-TURNED_LATE = (4, 5)
-VECTOR_SHARE = (32, 24, 64, 128, 48, 48)
 
 F32 = mybir.dt.float32
 BF16 = mybir.dt.bfloat16
@@ -64,8 +62,7 @@ def tile_list_recommender_slot_memory_kernel(
             [held.tile([P, BANK], U8, name="z_s%d%d" % (b, c), align_bytes=64) for c in range(CHUNKS)] for b in range(2)
         ]
         z_c = {(1, c): held.tile([P, BANK], U32, name="z_c%d" % c, align_bytes=64)[:] for c in range(CHUNKS)}
-        z1_early = held.tile([P, CHUNKS - 1, PACK, BANK], BF16, name="z1_early", align_bytes=64)
-        pages = [held.tile([P, T2], F32, name="page%d" % k) for k in range(1)]
+        pages = [tenant("page0", "page", [P, T2], F32)]
         minus_wg = tenant("weights", "minus_wg", [P, S], F32)
         w4_w = held.tile([P, 2, 2 * N], U8, name="w4_w", align_bytes=64)
         tab_s = tenant("page2", "tab_s", [P, T], U8)
@@ -90,11 +87,13 @@ def tile_list_recommender_slot_memory_kernel(
             return raw
 
         def load_old(s):
-            rows = tenant("big21" if s == SLICES - 1 else "old%d" % (s % 3), "old_rows", [P, T2], F32)
-            if s < PACK:
-                nc.sync.dma_start(rows[:], old[s * P : (s + 1) * P, :])
-            else:
-                nc.sync.dma_start(rows[:], old[KP:, :].rearrange("(p t) c -> t p c", t=PACK)[s - PACK])
+            rows = tenant("old%d" % (s % 3), "old_rows", [P, T2], F32)
+            nc.sync.dma_start(rows[:], old[s * P : (s + 1) * P, :])
+            return rows
+
+        def load_old_dealt(c):
+            rows = tenant(("old1", "old2", "old0", "old3")[c], "old_dealt", [P, PACK, BANK], F32)
+            nc.sync.dma_start(rows[:], old[KP:, c * BANK : (c + 1) * BANK].rearrange("(p t) c -> p t c", t=PACK))
             return rows
 
         nc.sync.dma_start(tab_w[0][:], tab_words_i[0])
@@ -262,50 +261,8 @@ def tile_list_recommender_slot_memory_kernel(
                 )
             return words[:]
 
-        def side_by_side(slices, on_vector, words):
-            width = slices.shape[2]
-            dst = words[:, : PACK * width].rearrange("p (c i t) -> p c t i", i=4, t=PACK)
-            src = slices.rearrange("p t (c i) -> p c t i", i=4)
-            if on_vector < width // 4:
-                nc.scalar.copy(dst[:, on_vector:], src[:, on_vector:])
-            if on_vector > 0:
-                nc.vector.tensor_copy(dst[:, :on_vector], src[:, :on_vector])
-            return words[:, : PACK * width]
-
         def quantise_z(b, c, words, lo=0, width=BANK):
             nc.vector.quantize_mx(z_c[b, c][:, lo : lo + width].bitcast(FP8X4), z_s[b][c][:, lo : lo + width], words)
-
-        def larger_on_vector(dst, s, lo):
-            cols = slice(lo, lo + dst.shape[1] * dst.shape[2])
-            nc.vector.scalar_tensor_tensor(
-                dst,
-                pages[s % PACK][:, cols].rearrange("p (c w) -> p c w", c=dst.shape[1]),
-                -1.0,
-                olds[s][:, cols].rearrange("p (c w) -> p c w", c=dst.shape[1]),
-                ALU.mult,
-                ALU.max,
-            )
-
-        def turn_late(s, room):
-            c = CHUNKS - 2
-            planes = tenant(room, "planes", [P, 2, BANK], F32)
-            difference, copied = bank(0, "difference"), bank(1, "copied")
-            for i in range(BLOCKS):
-                cols = slice(c * BANK + i * P, c * BANK + (i + 1) * P)
-                add_transposed(difference[:, i * P : (i + 1) * P], olds[s][:, cols], pages[s % PACK][:, cols])
-            nc.scalar.activation(planes[:, 0, :], difference[:], ACT.Relu)
-            for i in range(BLOCKS):
-                cols = slice(c * BANK + i * P, c * BANK + (i + 1) * P)
-                nc.tensor.transpose(copied[:, i * P : (i + 1) * P], pages[s % PACK][:, cols], ident[:])
-            nc.scalar.activation(planes[:, 1, :], copied[:], ACT.Copy, scale=-1.0)
-            return planes
-
-        def turn_late_back(s, planes, k):
-            larger = bank(k, "larger")
-            for i in range(BLOCKS):
-                blk = slice(i * P, (i + 1) * P)
-                add_transposed(larger[:, blk], planes[:, 1, blk], planes[:, 0, blk])
-            nc.scalar.copy(z1_early[:, CHUNKS - 2, s - PACK, :], larger[:])
 
         first_product(2)
         third_accs = [product(3, e, PACK + e) for e in range(2)]
@@ -327,54 +284,48 @@ def tile_list_recommender_slot_memory_kernel(
         wg_dealt = [tenant("wg%d" % t, "wg_dealt", [P, S], F32) for t in range(PACK)]
         for t in range(PACK):
             for g in (0, 2, 1, 3):
-                nc.sync.dma_start(wg_dealt[t][32 * g : 32 * g + 32, :], minus_wg[t:P:PACK, :])
+                nc.sync.dma_start(wg_dealt[t][32 * g : 32 * g + 32, :], wgs.rearrange("(q t) c -> t q c", t=PACK)[t])
         scatter(2)
         for a in range(2):
             quantise_dealt(a)
         magnitudes(3, third_accs)
+        old_dealt = {}
         for s in range(1, PACK):
             if s == 2:
                 first_product(4, banks=(0, 1))
             turn(s, (None, 5, 6)[s - 1])
-            olds[s + 3] = load_old(s + 3)
+            old_dealt[s - 1] = load_old_dealt(s - 1)
             scatter(s + 2)
-        for s in range(PACK, SLICES - 1):
-            larger_on_vector(z1_early[:, : CHUNKS - 1 - (s in TURNED_LATE), s - PACK, :], s, 0)
-            if s == PACK:
-                scatter(s + 2)
+        old_dealt[3] = load_old_dealt(3)
+        scatter(6)
         left_words = {}
         for c in range(CHUNKS):
-            left_words[c] = turn_back(c, ((4, 5, 6, 7), (2, 3, 0, 1), (4, 5, 0, 1), (2, 3, 6, 7))[c], ("ring2", "ring0", "ring1", "big00")[c])
-            if c < 2:
-                z_c[0, c] = held.tile([P, BANK], U32, name="z_first%d" % c, align_bytes=64)[:]
-                quantise_z(0, c, left_words[c])
+            left_words[c] = turn_back(c, ((4, 5, 6, 7), (2, 3, 0, 1), (4, 5, 0, 1), (2, 3, 6, 7))[c], ("ring2", "ring0", "ring1", "ring3")[c])
             if c == 1:
                 first_product(7)
                 scatter(7)
-                planes = [turn_late(s, "h%d" % (s % PACK)) for s in TURNED_LATE]
-                for k, s in enumerate(TURNED_LATE):
-                    turn_late_back(s, planes[k], k)
-        olds[7] = load_old(7)
+        page_dealt = [tenant(("big00", "big01", "big10", "big11")[c], "page_dealt", [P, PACK, BANK], F32) for c in range(CHUNKS)]
+        for t in range(PACK):
+            for c in range(CHUNKS):
+                nc.sync.dma_start(page_dealt[c][:, t, :], pages[t][:, c * BANK : (c + 1) * BANK])
+        for k in range(2):
+            codes = tenant("big3%d" % k, "codes", [P, 2, BANK], U32)
+            for e in range(2):
+                z_c[0, 2 * k + e] = codes[:, e, :]
 
         def second_product(b, c, lo, width, accs):
+            shared = BANK // width
             for n in range(N // P):
-                if width == BANK:
-                    steps = [(accs[n][:], 0, BANK, True, True)]
-                else:
-                    steps = [
-                        (accs[n // 2][:, at : at + P], lo + at % HALF, P, at == 0, at == BANK - P)
-                        for at in ((n % 2) * HALF, (n % 2) * HALF + P)
-                    ]
-                for acc, col, cols, first, last in steps:
-                    nc.tensor.matmul_mx(
-                        acc,
-                        lhsT=w4_w[:, b, 2 * n * P : 2 * (n + 1) * P].bitcast(FP4X4),
-                        lhsT_scale=w4_s[:, b, n * P : (n + 1) * P],
-                        rhs=z_c[b, c][:, col : col + cols].bitcast(FP8X4),
-                        rhs_scale=z_s[b][c][:, col : col + cols],
-                        start=(b == 0 and first),
-                        stop=(b == 1 and last),
-                    )
+                at = (n % shared) * width
+                nc.tensor.matmul_mx(
+                    accs[n // shared][:, at : at + width],
+                    lhsT=w4_w[:, b, 2 * n * P : 2 * (n + 1) * P].bitcast(FP4X4),
+                    lhsT_scale=w4_s[:, b, n * P : (n + 1) * P],
+                    rhs=z_c[b, c][:, lo : lo + width].bitcast(FP8X4),
+                    rhs_scale=z_s[b][c][:, lo : lo + width],
+                    start=(b == 0 and at == 0),
+                    stop=(b == 1 and at == BANK - width),
+                )
 
         def open_piece(c, lo, width):
             ks = [PACK * (c % 2) + k for k in range(PACK)]
@@ -382,20 +333,14 @@ def tile_list_recommender_slot_memory_kernel(
             second_product(0, c, lo, width, accs)
             return accs
 
-        late = []
-
-        def piece_words(c, lo, width):
-            if c == CHUNKS - 1:
-                if lo == 0:
-                    late.append(tenant("h1", "z1_late", [P, 2, PACK, HALF], BF16))
-                slices, missing = late[0][:, lo // HALF], range(PACK, SLICES)
-            else:
-                slices, missing = z1_early[:, c, :, lo : lo + width], [SLICES - 1]
-            for s in missing:
-                larger_on_vector(slices[:, s - PACK : s - PACK + 1, :], s, c * BANK + lo)
-            k = pieces.index((c, lo, width))
-            words = tenant(("first0", "first1", "h0", "h1", "h2", "weights")[k], "words", [P, PACK * width], BF16)
-            return side_by_side(slices, VECTOR_SHARE[k], words)
+        def larger(words, at, c, lo):
+            cols = slice(lo, lo + HALF)
+            nc.vector.tensor_tensor(
+                words[:, at : at + PACK * HALF].rearrange("p (c i t) -> p c t i", i=2, t=PACK),
+                page_dealt[c][:, :, cols].rearrange("p t (c i) -> p c t i", i=2),
+                old_dealt[c][:, :, cols].rearrange("p t (c i) -> p c t i", i=2),
+                ALU.max,
+            )
 
         staged = {}
 
@@ -403,7 +348,7 @@ def tile_list_recommender_slot_memory_kernel(
             cols = slice(c * BANK + lo, c * BANK + lo + width)
             second_product(1, c, lo, width, accs)
             if lo == 0:
-                staged[c] = tenant(("big01", "big10", "big11", "big20")[c], "y", [P, N // P * BANK], F32)
+                staged[c] = tenant(("page0", "page1", "page2", "big20")[c], "y", [P, N // P * BANK], F32)
             y = staged[c][:, N // P * lo : N // P * (lo + width)].rearrange("p (n c) -> p n c", n=N // P)
             for k, acc in enumerate(accs):
                 if width == BANK:
@@ -426,20 +371,39 @@ def tile_list_recommender_slot_memory_kernel(
         accs = {}
 
         def open_chunk(c):
-            if c > 1:
-                z_c[0, c] = tenant("first%d" % (c - 2), "codes", [P, BANK], U32)[:]
-                quantise_z(0, c, left_words[c])
+            quantise_z(0, c, left_words[c])
             for piece in pieces:
                 if piece[0] == c:
                     accs[piece] = open_piece(*piece)
 
-        open_chunk(0)
-        words = piece_words(*pieces[0])
-        for k, (c, lo, width) in enumerate(pieces):
-            ahead = k + 1 < len(pieces) and pieces[k + 1][0] < CHUNKS - 1
-            following = piece_words(*pieces[k + 1]) if ahead else None
-            quantise_z(1, c, words, lo, width)
-            words = piece_words(*pieces[k + 1]) if k + 1 < len(pieces) and not ahead else following
+        words = [
+            tenant(("first0", "first1", "h0", "h1", "h2", "weights")[k], "words", [P, PACK * width], BF16)
+            for k, (c, lo, width) in enumerate(pieces)
+        ]
+
+        def finish(k):
+            c, lo, width = pieces[k]
+            quantise_z(1, c, words[k][:], lo, width)
             close_piece(c, lo, width, accs[c, lo, width])
-            if k + 1 < CHUNKS:
-                open_chunk(k + 1)
+
+        open_chunk(0)
+        open_chunk(1)
+        larger(words[0], 0, 0, 0)
+        quantise_z(0, 2, left_words[2])
+        finish(0)
+        larger(words[1], 0, 0, HALF)
+        quantise_z(0, 3, left_words[3])
+        finish(1)
+        accs[pieces[3]] = open_piece(*pieces[3])
+        larger(words[2], 0, 1, 0)
+        larger(words[2], PACK * HALF, 1, HALF)
+        larger(words[3], 0, 2, 0)
+        finish(2)
+        for k in (4, 5):
+            accs[pieces[k]] = open_piece(*pieces[k])
+        larger(words[3], PACK * HALF, 2, HALF)
+        larger(words[4], 0, 3, 0)
+        finish(3)
+        larger(words[5], 0, 3, HALF)
+        finish(4)
+        finish(5)

@@ -92,7 +92,7 @@ def tile_list_recommender_slot_memory_kernel(
             return rows
 
         def load_old_dealt(c):
-            rows = tenant(("old1", "old2", "old0", "old3")[c], "old_dealt", [P, PACK, BANK], F32)
+            rows = tenant(("old1", "old2", "old3", "old4")[c], "old_dealt", [P, PACK, BANK], F32)
             nc.sync.dma_start(rows[:], old[KP:, c * BANK : (c + 1) * BANK].rearrange("(p t) c -> p t c", t=PACK))
             return rows
 
@@ -110,7 +110,7 @@ def tile_list_recommender_slot_memory_kernel(
             nc.sync.dma_start(b1_rows[:, 1:, 0:1], b1[P:KP].rearrange("(s p o) -> p s o", p=P, o=1))
         olds = {0: load_old(0)}
         raw_dealt = {
-            (a, e): load_w1(("page3", "wg1", "wg2", "h3")[2 * a + e], a, slice(KP + e * HALF, KP + (e + 1) * HALF))
+            (a, e): load_w1(("old3", "wg1", "wg2", "page3")[2 * a + e], a, slice(KP + e * HALF, KP + (e + 1) * HALF))
             for a in range(2)
             for e in range(2)
         }
@@ -184,11 +184,6 @@ def tile_list_recommender_slot_memory_kernel(
             bias = b1_rows[:, s, 0:1] if s < PACK else b1_dealt[:, s - PACK : s - PACK + 1]
             nc.scalar.activation(dst, acc, ACT.Abs, bias=bias)
 
-        def magnitudes(s, accs):
-            hs[s] = tenant("h%d" % (s % PACK), "h", [P, S], F32)
-            for e in range(2):
-                magnitude(s, hs[s][:, e * BANK : (e + 1) * BANK], accs[e][:])
-
         def first_product(s, banks=(0, 1), room=None):
             hs[s] = tenant(room or "h%d" % (s % PACK), "h", [P, S], F32)
             for e in range(2):
@@ -231,23 +226,31 @@ def tile_list_recommender_slot_memory_kernel(
         def turned_out(dst, src, func, scale):
             nc.scalar.activation(dst, src.rearrange("p (i m t) -> p i t m", i=BLOCKS, t=PACK), func, scale=scale)
 
-        def turn(s, ahead):
-            quarter = slice(32 * s, 32 * s + 32)
-            order = [(c + 2 * s + 2) % CHUNKS for c in range(CHUNKS)]
-            for c in order:
-                difference = bank(c, "difference")
+        def block(c, i):
+            return slice(c * BANK + i * P, c * BANK + (i + 1) * P)
+
+        def open_differences(s):
+            banks = [bank(c, "difference") for c in range(CHUNKS)]
+            for c in range(CHUNKS):
                 for i in range(BLOCKS):
-                    cols = slice(c * BANK + i * P, c * BANK + (i + 1) * P)
-                    add_transposed(difference[:, i * P : (i + 1) * P], olds[s][:, cols], pages[s % PACK][:, cols])
-                turned_out(turned[c][0][:, :, :, quarter], difference[:], ACT.Relu, 1.0)
-            if ahead:
-                first_product(ahead, banks=order[:2])
-            for c in order[2:] + order[:2]:
-                copied = bank(c, "copied")
+                    dst = banks[c][:, i * P : (i + 1) * P]
+                    nc.tensor.matmul(dst, olds[s][:, block(c, i)], ident[:], start=(i == 0), stop=False, is_transpose=True)
+            return banks
+
+        def close_differences(s, banks):
+            for c in range(CHUNKS):
                 for i in range(BLOCKS):
-                    cols = slice(c * BANK + i * P, c * BANK + (i + 1) * P)
-                    nc.tensor.transpose(copied[:, i * P : (i + 1) * P], pages[s % PACK][:, cols], ident[:])
-                turned_out(turned[c][1][:, :, :, quarter], copied[:], ACT.Copy, -1.0)
+                    dst = banks[c][:, i * P : (i + 1) * P]
+                    last = i == BLOCKS - 1
+                    nc.tensor.matmul(dst, pages[s][:, block(c, i)], ident[:], start=False, stop=last, is_transpose=True)
+                turned_out(turned[c][0][:, :, :, 32 * s : 32 * s + 32], banks[c][:], ACT.Relu, 1.0)
+
+        def turn_page(s, banks):
+            for c in range(CHUNKS):
+                copied = bank(banks[c], "copied")
+                for i in range(BLOCKS):
+                    nc.tensor.transpose(copied[:, i * P : (i + 1) * P], pages[s][:, block(c, i)], ident[:])
+                turned_out(turned[c][1][:, :, :, 32 * s : 32 * s + 32], copied[:], ACT.Copy, -1.0)
 
         def turn_back(c, banks, room):
             words = quantiser_input(room)
@@ -265,10 +268,11 @@ def tile_list_recommender_slot_memory_kernel(
             nc.vector.quantize_mx(z_c[b, c][:, lo : lo + width].bitcast(FP8X4), z_s[b][c][:, lo : lo + width], words)
 
         first_product(2)
-        third_accs = [product(3, e, PACK + e) for e in range(2)]
+        first_product(3, banks=(4, 5))
         scatter(1)
-        turn(0, None)
+        close_differences(0, open_differences(0))
         olds[3] = load_old(3)
+        turn_page(0, (6, 7, 4, 5))
         dealt_grouped = []
         for a in range(2):
             grouped = quantiser_input("ring%d" % a)
@@ -288,30 +292,38 @@ def tile_list_recommender_slot_memory_kernel(
         scatter(2)
         for a in range(2):
             quantise_dealt(a)
-        magnitudes(3, third_accs)
-        old_dealt = {}
-        for s in range(1, PACK):
-            if s == 2:
-                first_product(4, banks=(0, 1))
-            turn(s, (None, 5, 6)[s - 1])
-            old_dealt[s - 1] = load_old_dealt(s - 1)
-            scatter(s + 2)
-        old_dealt[3] = load_old_dealt(3)
+        scatter(3)
+        old_dealt = {c: load_old_dealt(c) for c in (2, 3)}
+        close_differences(1, open_differences(1))
+        old_dealt[0] = load_old_dealt(0)
+        turn_page(1, (4, 5, 6, 7))
+        close_differences(2, open_differences(2))
+        old_dealt[1] = load_old_dealt(1)
+        first_product(4, banks=(4, 5))
+        turn_page(2, (6, 7, 0, 1))
+        scatter(4)
+        first_product(5, banks=(2, 3))
+        scatter(5)
+        close_differences(3, open_differences(3))
+        turn_page(3, (4, 5, 6, 7))
+        first_product(6, banks=(0, 1))
         scatter(6)
         left_words = {}
         for c in range(CHUNKS):
-            left_words[c] = turn_back(c, ((4, 5, 6, 7), (2, 3, 0, 1), (4, 5, 0, 1), (2, 3, 6, 7))[c], ("ring2", "ring0", "ring1", "ring3")[c])
-            if c == 1:
-                first_product(7)
+            banks = ((2, 3, 4, 5), (6, 7, 0, 1), (4, 5, 6, 7), (2, 3, 0, 1))[c]
+            left_words[c] = turn_back(c, banks, ("ring2", "ring0", "ring1", "weights")[c])
+            if c == 0:
+                first_product(7, banks=(4, 5))
                 scatter(7)
-        page_dealt = [tenant(("big00", "big01", "big10", "big11")[c], "page_dealt", [P, PACK, BANK], F32) for c in range(CHUNKS)]
+        page_dealt = [tenant(("side0", "old0", "big00", "big01")[c], "page_dealt", [P, PACK, BANK], F32) for c in range(CHUNKS)]
         for t in range(PACK):
             for c in range(CHUNKS):
-                nc.sync.dma_start(page_dealt[c][:, t, :], pages[t][:, c * BANK : (c + 1) * BANK])
-        for k in range(2):
-            codes = tenant("big3%d" % k, "codes", [P, 2, BANK], U32)
-            for e in range(2):
-                z_c[0, 2 * k + e] = codes[:, e, :]
+                if (t, c) != (PACK - 1, 0):
+                    nc.sync.dma_start(page_dealt[c][:, t, :], pages[t][:, c * BANK : (c + 1) * BANK])
+        z_c[0, 0] = tenant("wg3", "codes", [P, BANK], U32)[:]
+        codes = tenant("big30", "codes", [P, CHUNKS - 1, BANK], U32)
+        for c in range(1, CHUNKS):
+            z_c[0, c] = codes[:, c - 1, :]
 
         def second_product(b, c, lo, width, accs):
             shared = BANK // width
@@ -367,43 +379,44 @@ def tile_list_recommender_slot_memory_kernel(
                         y[:, 2 * k : 2 * k + 2, :],
                     )
 
-        pieces = [(0, 0, HALF), (0, HALF, HALF), (1, 0, BANK), (2, 0, BANK), (3, 0, HALF), (3, HALF, HALF)]
-        accs = {}
+        pieces = [(0, 0, BANK), (1, 0, BANK), (2, 0, HALF), (2, HALF, HALF), (3, 0, HALF), (3, HALF, HALF)]
+        accs, words = {}, {}
 
         def open_chunk(c):
-            quantise_z(0, c, left_words[c])
             for piece in pieces:
                 if piece[0] == c:
                     accs[piece] = open_piece(*piece)
 
-        words = [
-            tenant(("first0", "first1", "h0", "h1", "h2", "weights")[k], "words", [P, PACK * width], BF16)
-            for k, (c, lo, width) in enumerate(pieces)
-        ]
+        def quantise_first(c):
+            quantise_z(0, c, left_words[c])
+            words[c] = quantiser_input(("ring2", "ring0", "ring1", "weights")[c])
 
-        def finish(k):
-            c, lo, width = pieces[k]
-            quantise_z(1, c, words[k][:], lo, width)
+        def finish(c, lo, width):
+            quantise_z(1, c, words[c][:, PACK * lo : PACK * (lo + width)], lo, width)
             close_piece(c, lo, width, accs[c, lo, width])
 
+        quantise_first(0)
         open_chunk(0)
+        nc.vector.tensor_copy(page_dealt[0][:, PACK - 1, :], pages[PACK - 1][:, :BANK])
+        for e in range(2):
+            larger(words[0], e * PACK * HALF, 0, e * HALF)
+        for e in range(2):
+            quantise_z(1, 0, words[0][:, e * PACK * HALF : (e + 1) * PACK * HALF], e * HALF, HALF)
+        close_piece(0, 0, BANK, accs[0, 0, BANK])
+        quantise_first(1)
         open_chunk(1)
-        larger(words[0], 0, 0, 0)
-        quantise_z(0, 2, left_words[2])
-        finish(0)
-        larger(words[1], 0, 0, HALF)
-        quantise_z(0, 3, left_words[3])
-        finish(1)
-        accs[pieces[3]] = open_piece(*pieces[3])
-        larger(words[2], 0, 1, 0)
-        larger(words[2], PACK * HALF, 1, HALF)
-        larger(words[3], 0, 2, 0)
-        finish(2)
-        for k in (4, 5):
-            accs[pieces[k]] = open_piece(*pieces[k])
-        larger(words[3], PACK * HALF, 2, HALF)
-        larger(words[4], 0, 3, 0)
-        finish(3)
-        larger(words[5], 0, 3, HALF)
-        finish(4)
-        finish(5)
+        for e in range(2):
+            larger(words[1], e * PACK * HALF, 1, e * HALF)
+        quantise_first(2)
+        open_chunk(2)
+        finish(1, 0, BANK)
+        larger(words[2], 0, 2, 0)
+        quantise_first(3)
+        open_chunk(3)
+        finish(2, 0, HALF)
+        larger(words[2], PACK * HALF, 2, HALF)
+        larger(words[3], 0, 3, 0)
+        finish(2, HALF, HALF)
+        finish(3, 0, HALF)
+        larger(words[3], PACK * HALF, 3, HALF)
+        finish(3, HALF, HALF)

@@ -14,6 +14,7 @@ HALF = BANK // 2
 SLICES = H // P
 CHUNKS = T2 // BANK
 BLOCKS = BANK // P
+TURNED = 1
 
 F32 = mybir.dt.float32
 BF16 = mybir.dt.bfloat16
@@ -92,7 +93,7 @@ def tile_list_recommender_slot_memory_kernel(
             return rows
 
         def load_old_dealt(c):
-            rows = tenant(("old1", "old2", "old3", "old4")[c], "old_dealt", [P, PACK, BANK], F32)
+            rows = tenant(("old1", "old4", "old3", "old2")[c], "old_dealt", [P, PACK, BANK], F32)
             nc.sync.dma_start(rows[:], old[KP:, c * BANK : (c + 1) * BANK].rearrange("(p t) c -> p t c", t=PACK))
             return rows
 
@@ -189,6 +190,11 @@ def tile_list_recommender_slot_memory_kernel(
             for e in range(2):
                 magnitude(s, hs[s][:, e * BANK : (e + 1) * BANK], product(s, e, banks[e])[:])
 
+        def half_product(s, e, k):
+            if e == 0:
+                hs[s] = tenant("h%d" % (s % PACK), "h", [P, S], F32)
+            magnitude(s, hs[s][:, e * BANK : (e + 1) * BANK], product(s, e, k)[:])
+
         def scatter_part(room, acc, lo, width):
             h = tenant(room, "h", [P, width], F32)
             magnitude(0, h[:], acc[:, lo % BANK : lo % BANK + width])
@@ -252,27 +258,26 @@ def tile_list_recommender_slot_memory_kernel(
                     nc.tensor.transpose(copied[:, i * P : (i + 1) * P], pages[s][:, block(c, i)], ident[:])
                 turned_out(turned[c][1][:, :, :, 32 * s : 32 * s + 32], copied[:], ACT.Copy, -1.0)
 
-        def turn_back(c, banks, room):
-            words = quantiser_input(room)
-            for i in range(BLOCKS):
-                larger = bank(banks[i], "larger")
+        def turn_back(c, words, blocks, banks):
+            for i, k in zip(blocks, banks):
+                larger = bank(k, "larger")
                 for t in range(PACK):
                     add_transposed(larger[:, t * P : (t + 1) * P], turned[c][1][:, i, t, :], turned[c][0][:, i, t, :])
                 nc.scalar.copy(
                     words[:, i * BANK : (i + 1) * BANK].rearrange("p (c t) -> p c t", t=PACK),
                     larger[:].rearrange("p (t c) -> p c t", t=PACK),
                 )
-            return words[:]
 
         def quantise_z(b, c, words, lo=0, width=BANK):
             nc.vector.quantize_mx(z_c[b, c][:, lo : lo + width].bitcast(FP8X4), z_s[b][c][:, lo : lo + width], words)
 
-        first_product(2)
-        first_product(3, banks=(4, 5))
+        half_product(2, 0, 4)
         scatter(1)
         close_differences(0, open_differences(0))
         olds[3] = load_old(3)
+        half_product(2, 1, 5)
         turn_page(0, (6, 7, 4, 5))
+        half_product(3, 0, 6)
         dealt_grouped = []
         for a in range(2):
             grouped = quantiser_input("ring%d" % a)
@@ -292,38 +297,74 @@ def tile_list_recommender_slot_memory_kernel(
         scatter(2)
         for a in range(2):
             quantise_dealt(a)
-        scatter(3)
-        old_dealt = {c: load_old_dealt(c) for c in (2, 3)}
+        old_dealt = {c: load_old_dealt(c) for c in (1, 2)}
         close_differences(1, open_differences(1))
         old_dealt[0] = load_old_dealt(0)
+        half_product(3, 1, 7)
+        scatter(3)
         turn_page(1, (4, 5, 6, 7))
         close_differences(2, open_differences(2))
-        old_dealt[1] = load_old_dealt(1)
-        first_product(4, banks=(4, 5))
-        turn_page(2, (6, 7, 0, 1))
+        old_dealt[3] = load_old_dealt(3)
+        early = old_dealt[TURNED][:, : PACK - 1, :]
+        nc.scalar.activation(early, early, ACT.Copy, scale=-1.0)
+        half_product(4, 0, 4)
+        turn_page(2, (5, 6, 7, 4))
+        half_product(4, 1, 5)
         scatter(4)
-        first_product(5, banks=(2, 3))
+        differences = open_differences(3)
+        half_product(5, 0, 6)
+        close_differences(3, differences)
+        half_product(5, 1, 7)
         scatter(5)
-        close_differences(3, open_differences(3))
         turn_page(3, (4, 5, 6, 7))
-        first_product(6, banks=(0, 1))
+        left_words = {c: quantiser_input(("ring2", "ring0", "ring1", "weights")[c])[:] for c in range(CHUNKS)}
+        turn_back(0, left_words[0], (0, 1), (0, 1))
+        half_product(6, 0, 2)
+        turn_back(0, left_words[0], (2, 3), (3, 4))
+        half_product(6, 1, 5)
         scatter(6)
-        left_words = {}
-        for c in range(CHUNKS):
-            banks = ((2, 3, 4, 5), (6, 7, 0, 1), (4, 5, 6, 7), (2, 3, 0, 1))[c]
-            left_words[c] = turn_back(c, banks, ("ring2", "ring0", "ring1", "weights")[c])
-            if c == 0:
-                first_product(7, banks=(4, 5))
-                scatter(7)
-        page_dealt = [tenant(("side0", "old0", "big00", "big01")[c], "page_dealt", [P, PACK, BANK], F32) for c in range(CHUNKS)]
+        turn_back(1, left_words[1], (0, 1), (6, 7))
+        half_product(7, 0, 0)
+        turn_back(1, left_words[1], (2, 3), (1, 2))
+        half_product(7, 1, 3)
+        scatter(7)
+        planes = [tenant("big1%d" % k, "planes", [P, BLOCKS, PACK - 1, P], F32) for k in range(2)]
+
+        def turn_dealt(t, banks):
+            difference, copied = bank(banks[0], "difference"), bank(banks[1], "copied")
+            for i in range(BLOCKS):
+                dst = difference[:, i * P : (i + 1) * P]
+                nc.tensor.matmul(dst, early[:, t, i * P : (i + 1) * P], ident[:], start=(i == 0), stop=False, is_transpose=True)
+            for i in range(BLOCKS):
+                dst = difference[:, i * P : (i + 1) * P]
+                last = i == BLOCKS - 1
+                nc.tensor.matmul(dst, pages[t][:, block(TURNED, i)], ident[:], start=False, stop=last, is_transpose=True)
+            nc.scalar.activation(planes[0][:, :, t, :], difference[:].rearrange("p (i m) -> p i m", i=BLOCKS), ACT.Relu, scale=-1.0)
+            for i in range(BLOCKS):
+                nc.tensor.transpose(copied[:, i * P : (i + 1) * P], pages[t][:, block(TURNED, i)], ident[:])
+            nc.scalar.copy(planes[1][:, :, t, :], copied[:].rearrange("p (i m) -> p i m", i=BLOCKS))
+
+        turn_dealt(0, (4, 5))
+        turn_back(2, left_words[2], range(BLOCKS), (6, 7, 0, 1))
+        turn_dealt(1, (2, 3))
+        turn_back(3, left_words[3], range(BLOCKS), (4, 5, 6, 7))
+        turn_dealt(2, (0, 1))
+        turned_rows = tenant("h0", "turned_rows", [P, PACK, BANK], BF16)
+        for i in range(BLOCKS):
+            larger_rows = bank(2 + i, "larger")
+            for t in range(PACK - 1):
+                add_transposed(larger_rows[:, t * P : (t + 1) * P], planes[1][:, i, t, :], planes[0][:, i, t, :])
+            nc.scalar.copy(
+                turned_rows[:, : PACK - 1, i * P : (i + 1) * P],
+                larger_rows[:, : (PACK - 1) * P].rearrange("p (t c) -> p t c", t=PACK - 1),
+            )
+        page_dealt = {c: tenant(room, "page_dealt", [P, PACK, BANK], F32) for c, room in ((0, "side0"), (2, "old0"), (3, "big00"))}
         for t in range(PACK):
-            for c in range(CHUNKS):
+            for c in page_dealt:
                 if (t, c) != (PACK - 1, 0):
                     nc.sync.dma_start(page_dealt[c][:, t, :], pages[t][:, c * BANK : (c + 1) * BANK])
         z_c[0, 0] = tenant("wg3", "codes", [P, BANK], U32)[:]
-        codes = tenant("big30", "codes", [P, CHUNKS - 1, BANK], U32)
-        for c in range(1, CHUNKS):
-            z_c[0, c] = codes[:, c - 1, :]
+        z_c[0, 1] = tenant("big10", "codes", [P, BANK], U32)[:]
 
         def second_product(b, c, lo, width, accs):
             shared = BANK // width
@@ -340,7 +381,7 @@ def tile_list_recommender_slot_memory_kernel(
                 )
 
         def open_piece(c, lo, width):
-            ks = [PACK * (c % 2) + k for k in range(PACK)]
+            ks = [(2 + PACK * c + k) % 8 for k in range(PACK)]
             accs = [bank(k, "score") for k in ks[lo // P : (lo + width) // P]]
             second_product(0, c, lo, width, accs)
             return accs
@@ -379,8 +420,8 @@ def tile_list_recommender_slot_memory_kernel(
                         y[:, 2 * k : 2 * k + 2, :],
                     )
 
-        pieces = [(0, 0, BANK), (1, 0, BANK), (2, 0, HALF), (2, HALF, HALF), (3, 0, HALF), (3, HALF, HALF)]
-        accs, words = {}, {}
+        pieces = [(0, 0, HALF), (0, HALF, HALF), (1, 0, BANK), (2, 0, HALF), (2, HALF, HALF), (3, 0, HALF), (3, HALF, HALF)]
+        accs, words = {}, {TURNED: quantiser_input("h1")}
 
         def open_chunk(c):
             for piece in pieces:
@@ -389,34 +430,43 @@ def tile_list_recommender_slot_memory_kernel(
 
         def quantise_first(c):
             quantise_z(0, c, left_words[c])
-            words[c] = quantiser_input(("ring2", "ring0", "ring1", "weights")[c])
+            if c != TURNED:
+                words[c] = quantiser_input(("ring2", "ring0", "ring1", "weights")[c])
+            open_chunk(c)
 
         def finish(c, lo, width):
             quantise_z(1, c, words[c][:, PACK * lo : PACK * (lo + width)], lo, width)
             close_piece(c, lo, width, accs[c, lo, width])
 
+        def copy_last_page(lo):
+            nc.vector.tensor_copy(page_dealt[0][:, PACK - 1, lo : lo + HALF], pages[PACK - 1][:, lo : lo + HALF])
+
         quantise_first(0)
-        open_chunk(0)
-        nc.vector.tensor_copy(page_dealt[0][:, PACK - 1, :], pages[PACK - 1][:, :BANK])
-        for e in range(2):
-            larger(words[0], e * PACK * HALF, 0, e * HALF)
-        for e in range(2):
-            quantise_z(1, 0, words[0][:, e * PACK * HALF : (e + 1) * PACK * HALF], e * HALF, HALF)
-        close_piece(0, 0, BANK, accs[0, 0, BANK])
+        copy_last_page(0)
+        nc.vector.tensor_tensor(
+            turned_rows[:, PACK - 1, :],
+            pages[PACK - 1][:, TURNED * BANK : (TURNED + 1) * BANK],
+            old_dealt[TURNED][:, PACK - 1, :],
+            ALU.max,
+        )
+        nc.scalar.copy(
+            words[TURNED][:].rearrange("p (c i t) -> p c t i", i=4, t=PACK),
+            turned_rows[:].rearrange("p t (c i) -> p c t i", i=4),
+        )
+        codes = tenant("h0", "codes", [P, 2, BANK], U32)
+        for c in (2, 3):
+            z_c[0, c] = codes[:, c - 2, :]
+        larger(words[0], 0, 0, 0)
+        copy_last_page(HALF)
+        finish(0, 0, HALF)
+        larger(words[0], PACK * HALF, 0, HALF)
+        finish(0, HALF, HALF)
         quantise_first(1)
-        open_chunk(1)
-        for e in range(2):
-            larger(words[1], e * PACK * HALF, 1, e * HALF)
-        quantise_first(2)
-        open_chunk(2)
         finish(1, 0, BANK)
+        quantise_first(2)
         larger(words[2], 0, 2, 0)
         quantise_first(3)
-        open_chunk(3)
         finish(2, 0, HALF)
-        larger(words[2], PACK * HALF, 2, HALF)
-        larger(words[3], 0, 3, 0)
-        finish(2, HALF, HALF)
-        finish(3, 0, HALF)
-        larger(words[3], PACK * HALF, 3, HALF)
-        finish(3, HALF, HALF)
+        for c, lo in ((2, HALF), (3, 0), (3, HALF)):
+            larger(words[c], PACK * lo, c, lo)
+            finish(c, lo, HALF)

@@ -389,9 +389,9 @@ def tile_list_recommender_slot_memory_kernel(
         def larger(words, at, c, lo):
             cols = slice(lo, lo + HALF)
             nc.vector.tensor_tensor(
-                words[:, at : at + PACK * HALF].rearrange("p (c i t) -> p c t i", i=2, t=PACK),
-                page_dealt[c][:, :, cols].rearrange("p t (c i) -> p c t i", i=2),
-                old_dealt[c][:, :, cols].rearrange("p t (c i) -> p c t i", i=2),
+                words[:, at : at + PACK * HALF].rearrange("p (c i t) -> p c t i", i=4, t=PACK),
+                page_dealt[c][:, :, cols].rearrange("p t (c i) -> p c t i", i=4),
+                old_dealt[c][:, :, cols].rearrange("p t (c i) -> p c t i", i=4),
                 ALU.max,
             )
 

@@ -66,19 +66,13 @@ def tile_list_recommender_slot_memory_kernel(
         pages = [tenant("page0", "page", [P, T2], F32)]
         minus_wg = tenant("weights", "minus_wg", [P, S], F32)
         w4_w = held.tile([P, 2, 2 * N], U8, name="w4_w", align_bytes=64)
-        tab_s = tenant("page2", "tab_s", [P, T], U8)
-        scale_rows = tenant("page1", "scale_rows", [P, T // 4], I32)
+        tab_s = tenant("h2", "tab_s", [P, T], U8)
         tab_w = [tenant("big0%d" % a, "tab_w%d" % a, [P, T], I32) for a in range(2)]
 
+        nc.gpsimd.memset(tab_s[:].bitcast(I32), 0)
         make_identity(nc, ident[:])
-        nc.vector.memset(tab_s[:].bitcast(I32), 0)
         nc.vector.memset(pages[0][:].bitcast(I32), 0)
         nc.sync.dma_start(idx[:], offs)
-        for q in range(4):
-            nc.sync.dma_start(scale_rows[32 * q : 32 * q + 8, :], tab_scales[:, 4 * q : 4 * q + 4, :].bitcast(I32))
-        for q in range(4):
-            rows = slice(32 * q, 32 * q + 8)
-            nc.vector.tensor_copy(tab_s[rows, :].bitcast(I32), scale_rows[rows, :])
         nc.gpsimd.memset(w4_s[:].rearrange("p a n -> p (a n)").bitcast(I32), 0)
         tab_words_i = tab_words.rearrange("a p t i -> a p (t i)").bitcast(I32)
 
@@ -98,6 +92,8 @@ def tile_list_recommender_slot_memory_kernel(
             return rows
 
         nc.sync.dma_start(tab_w[0][:], tab_words_i[0])
+        for q in range(4):
+            nc.sync.dma_start(tab_s[32 * q : 32 * q + 8, :].bitcast(I32), tab_scales[:, 4 * q : 4 * q + 4, :].bitcast(I32))
         raw_first = [load_w1("first%d" % a, a, slice(0, P)) for a in range(2)]
         nc.sync.dma_start(tab_w[1][:], tab_words_i[1])
         for e in range(2):
@@ -151,31 +147,33 @@ def tile_list_recommender_slot_memory_kernel(
         def half(entries, e):
             return entries[:, e * BANK // 16 : (e + 1) * BANK // 16]
 
-        for e in range(2):
-            nc.vector.tensor_copy(v_s[e][:], tab_s[:].indirect(half(idx, e)))
         for k in (1, 2):
             pages.append(tenant("page%d" % k, "page", [P, T2], F32))
             nc.gpsimd.memset(pages[k][:].bitcast(I32), 0)
         for e in range(2):
             nc.vector.tensor_copy(v_w[0, e][:], tab_w[0][:].bitcast(U32).indirect(half(idx, e)))
-        quantise_w1([0], cast_rows(raw_first, 0, P, quantiser_input("ring0")))
         for e in range(2):
-            nc.vector.tensor_copy(v_w[1, e][:], tab_w[1][:].bitcast(U32).indirect(half(idx, e)))
+            nc.vector.tensor_copy(v_s[e][:], tab_s[:].indirect(half(idx, e)))
+        quantise_w1([0], cast_rows(raw_first, 0, P, quantiser_input("ring0")))
+        for lo in (0, HALF):
+            entries = idx[:, lo // 16 : (lo + HALF) // 16]
+            nc.vector.tensor_copy(v_w[1, 0][:, lo : lo + HALF], tab_w[1][:].bitcast(U32).indirect(entries))
+        nc.vector.tensor_copy(v_w[1, 1][:], tab_w[1][:].bitcast(U32).indirect(half(idx, 1)))
         for e in range(2):
             cols = slice(e * BANK, (e + 1) * BANK)
             nc.gpsimd.tensor_scalar(minus_wg[:, cols], minus_wg[:, cols], -1.0, 0.0, ALU.mult, ALU.add)
 
         hs = {}
 
-        def product(s, e, k):
+        def product(s, e, k, cols=slice(0, BANK)):
             acc = bank(k, "acc")
             for a in range(2):
                 nc.tensor.matmul_mx(
-                    acc[:],
+                    acc[:, cols],
                     lhsT=w1_c[a, s].bitcast(FP8X4),
                     lhsT_scale=w1_s[a, s],
-                    rhs=v_w[a, e][:].bitcast(FP8X4),
-                    rhs_scale=v_s[e][4 * a :, :],
+                    rhs=v_w[a, e][:, cols].bitcast(FP8X4),
+                    rhs_scale=v_s[e][4 * a :, cols],
                     start=(a == 0),
                     stop=(a == 1),
                 )
@@ -201,7 +199,8 @@ def tile_list_recommender_slot_memory_kernel(
             entries = idx2[:, lo // 16 : (lo + width) // 16]
             nc.vector.tensor_tensor(pages[0][:].indirect(entries), h[:], minus_wg[:, lo : lo + width], ALU.mult)
 
-        scatter_part("h0", product(0, 0, 0), 0, BANK)
+        for k, lo in ((0, 0), (4, HALF)):
+            scatter_part(("h0", "h1")[lo // HALF], product(0, 0, k, slice(lo, lo + HALF)), lo, HALF)
         second_half = product(0, 1, 1)
         quantise_w1([1], cast_rows(raw_second, 0, P, quantiser_input("ring1")))
         scatter_part("h0_second", second_half, BANK, HALF)

@@ -48,21 +48,16 @@ def tile_list_recommender_slot_memory_kernel(
 
         idx = held.tile([P, S // 16], U16, name="idx")
         idx2 = held.tile([P, S // 16], U16, name="idx2")
-        v_w = {
-            (a, e): held.tile([P, BANK], U32, name="v_w%d%d" % (a, e), align_bytes=64)
-            for a in range(2)
-            for e in range(2)
-        }
+        v_w = {(a, e): rooms.tile([P, BANK], U32, name="v_w", tag="v_w%d%d" % (a, e), align_bytes=64) for a in range(2) for e in range(2)}
         v_s = [held.tile([P, BANK], U8, name="v_s%d" % e, align_bytes=64) for e in range(2)]
         b1_rows = held.tile([P, PACK, 8], F32, name="b1_rows")
-        b1_dealt = held.tile([P, PACK], F32, name="b1_dealt")
+        b1_dealt = rooms.tile([P, PACK], F32, name="b1_dealt", tag="bias", align_bytes=64)
         b4_t = held.tile([P, N // P, 8], F32, name="b4_t")
         w4_s = held.tile([P, 2, N], U8, name="w4_s", align_bytes=64)
         ident = held.tile([P, P], F32, name="ident")
         z_s = [
             [held.tile([P, BANK], U8, name="z_s%d%d" % (b, c), align_bytes=64) for c in range(CHUNKS)] for b in range(2)
         ]
-        z_c = {(1, c): held.tile([P, BANK], U32, name="z_c%d" % c, align_bytes=64)[:] for c in range(CHUNKS)}
         pages = [tenant("page0", "page", [P, T2], F32)]
         minus_wg = tenant("weights", "minus_wg", [P, S], F32)
         w4_w = held.tile([P, 2, 2 * N], U8, name="w4_w", align_bytes=64)
@@ -159,8 +154,7 @@ def tile_list_recommender_slot_memory_kernel(
             entries = idx[:, lo // 16 : (lo + HALF) // 16]
             nc.vector.tensor_copy(v_w[1, 0][:, lo : lo + HALF], tab_w[1][:].bitcast(U32).indirect(entries))
         nc.vector.tensor_copy(v_w[1, 1][:], tab_w[1][:].bitcast(U32).indirect(half(idx, 1)))
-        for e in range(2):
-            cols = slice(e * BANK, (e + 1) * BANK)
+        for cols in (slice(0, BANK), slice(BANK, S)):
             nc.gpsimd.tensor_scalar(minus_wg[:, cols], minus_wg[:, cols], -1.0, 0.0, ALU.mult, ALU.add)
 
         hs = {}
@@ -193,19 +187,21 @@ def tile_list_recommender_slot_memory_kernel(
                 hs[s] = tenant("h%d" % (s % PACK), "h", [P, S], F32)
             magnitude(s, hs[s][:, e * BANK : (e + 1) * BANK], product(s, e, k)[:])
 
-        def scatter_part(room, acc, lo, width):
+        def scatter_part(room, sums, lo):
+            width = len(sums) * HALF
             h = tenant(room, "h", [P, width], F32)
-            magnitude(0, h[:], acc[:, lo % BANK : lo % BANK + width])
+            for k, acc in enumerate(sums):
+                magnitude(0, h[:, k * HALF : (k + 1) * HALF], acc)
             entries = idx2[:, lo // 16 : (lo + width) // 16]
             nc.vector.tensor_tensor(pages[0][:].indirect(entries), h[:], minus_wg[:, lo : lo + width], ALU.mult)
 
-        for k, lo in ((0, 0), (4, HALF)):
-            scatter_part(("h0", "h1")[lo // HALF], product(0, 0, k, slice(lo, lo + HALF)), lo, HALF)
+        for room, k, lo in (("h0", 0, 0), ("h1", 4, HALF)):
+            scatter_part(room, [product(0, 0, k, slice(lo, lo + HALF))[:, lo : lo + HALF]], lo)
         second_half = product(0, 1, 1)
         quantise_w1([1], cast_rows(raw_second, 0, P, quantiser_input("ring1")))
-        scatter_part("h0_second", second_half, BANK, HALF)
+        scatter_part("h0_second", [second_half[:, :HALF]], BANK)
         quantise_w1([2, 3], cast_rows(raw_rest, 0, 2 * P, quantiser_input("ring2")))
-        scatter_part("h0_third", second_half, BANK + HALF, HALF)
+        scatter_part("h0_third", [second_half[:, HALF:]], BANK + HALF)
         first_product(1, banks=(2, 3), room="ring2")
 
         def scatter(s):
@@ -263,12 +259,9 @@ def tile_list_recommender_slot_memory_kernel(
                 for t in range(PACK):
                     add_transposed(larger[:, t * P : (t + 1) * P], turned[c][1][:, i, t, :], turned[c][0][:, i, t, :])
                 nc.scalar.copy(
-                    words[:, i * BANK : (i + 1) * BANK].rearrange("p (c t) -> p c t", t=PACK),
+                    words[i].rearrange("p (c t) -> p c t", t=PACK),
                     larger[:].rearrange("p (t c) -> p c t", t=PACK),
                 )
-
-        def quantise_z(b, c, words, lo=0, width=BANK):
-            nc.vector.quantize_mx(z_c[b, c][:, lo : lo + width].bitcast(FP8X4), z_s[b][c][:, lo : lo + width], words)
 
         half_product(2, 0, 4)
         scatter(1)
@@ -316,7 +309,16 @@ def tile_list_recommender_slot_memory_kernel(
         half_product(5, 1, 7)
         scatter(5)
         turn_page(3, (4, 5, 6, 7))
-        left_words = {c: quantiser_input(("ring2", "ring0", "ring1", "weights")[c])[:] for c in range(CHUNKS)}
+        left_rooms = ("first0", "first1", "h0_second", "h0_third")
+        halves = [(c, lo) for c in range(2, CHUNKS) for lo in (0, HALF)]
+        left_tiles = {at: tenant(room, "left_words", [P, PACK * HALF], BF16)[:] for at, room in zip(halves, left_rooms)}
+        left_whole = [quantiser_input(room) for room in ("ring2", "ring0")]
+        for c in range(2):
+            for lo in (0, HALF):
+                left_tiles[c, lo] = left_whole[c][:, PACK * lo : PACK * (lo + HALF)]
+        left_words = {
+            c: [left_tiles[c, i // 2 * HALF][:, i % 2 * BANK : (i % 2 + 1) * BANK] for i in range(BLOCKS)] for c in range(CHUNKS)
+        }
         turn_back(0, left_words[0], (0, 1), (0, 1))
         half_product(6, 0, 2)
         turn_back(0, left_words[0], (2, 3), (3, 4))
@@ -343,6 +345,43 @@ def tile_list_recommender_slot_memory_kernel(
                 nc.tensor.transpose(copied[:, i * P : (i + 1) * P], pages[t][:, block(TURNED, i)], ident[:])
             nc.scalar.copy(planes[1][:, :, t, :], copied[:].rearrange("p (i m) -> p i m", i=BLOCKS))
 
+        pieces = [(0, 0, HALF), (0, HALF, HALF), (1, 0, BANK), (2, 0, HALF), (2, HALF, HALF), (3, 0, HALF), (3, HALF, HALF)]
+        left_codes, right_codes, accs, staged, words = {}, {}, {}, {}, {}
+
+        def quantise_left(c, lo, room):
+            left_codes[c, lo] = tenant(room, "left_codes", [P, HALF], U32)[:]
+            nc.vector.quantize_mx(left_codes[c, lo].bitcast(FP8X4), z_s[0][c][:, lo : lo + HALF], left_tiles[c, lo])
+
+        def quantise_left_whole(c, room):
+            codes = tenant(room, "left_codes", [P, BANK], U32)
+            nc.vector.quantize_mx(codes[:].bitcast(FP8X4), z_s[0][c][:], left_whole[c][:])
+            for piece in pieces:
+                if piece[0] == c:
+                    left_codes[c, piece[1]] = codes[:, piece[1] : piece[1] + piece[2]]
+
+        def score_pass(piece, b, n, codes, lo, width, start, stop):
+            c = piece[0]
+            shared = N // P // len(accs[piece])
+            at = n % shared * piece[2] + lo - piece[1]
+            nc.tensor.matmul_mx(
+                accs[piece][n // shared][:, at : at + width],
+                lhsT=w4_w[:, b, 2 * n * P : 2 * (n + 1) * P].bitcast(FP4X4),
+                lhsT_scale=w4_s[:, b, n * P : (n + 1) * P],
+                rhs=codes.bitcast(FP8X4),
+                rhs_scale=z_s[b][c][:, lo : lo + width],
+                start=start,
+                stop=stop,
+            )
+
+        def open_piece(piece):
+            c, lo, width = piece
+            ks = [(2 + PACK * c + k) % 8 for k in range(PACK)]
+            ks = (0, 1, 2, 3) if piece == pieces[-1] else ks[lo // P : (lo + width) // P]
+            accs[piece] = [bank(k, "score") for k in ks]
+            shared = N // P // len(ks)
+            for n in range(N // P):
+                score_pass(piece, 0, n, left_codes[c, lo], lo, width, n % shared == 0, False)
+
         turn_dealt(0, (4, 5))
         turn_back(2, left_words[2], range(BLOCKS), (6, 7, 0, 1))
         turn_dealt(1, (2, 3))
@@ -362,85 +401,52 @@ def tile_list_recommender_slot_memory_kernel(
             for c in page_dealt:
                 if (t, c) != (PACK - 1, 0):
                     nc.sync.dma_start(page_dealt[c][:, t, :], pages[t][:, c * BANK : (c + 1) * BANK])
-        z_c[0, 0] = tenant("wg3", "codes", [P, BANK], U32)[:]
-        z_c[0, 1] = tenant("big10", "codes", [P, BANK], U32)[:]
 
-        def second_product(b, c, lo, width, accs):
-            shared = BANK // width
-            for n in range(N // P):
-                at = (n % shared) * width
-                nc.tensor.matmul_mx(
-                    accs[n // shared][:, at : at + width],
-                    lhsT=w4_w[:, b, 2 * n * P : 2 * (n + 1) * P].bitcast(FP4X4),
-                    lhsT_scale=w4_s[:, b, n * P : (n + 1) * P],
-                    rhs=z_c[b, c][:, lo : lo + width].bitcast(FP8X4),
-                    rhs_scale=z_s[b][c][:, lo : lo + width],
-                    start=(b == 0 and at == 0),
-                    stop=(b == 1 and at == BANK - width),
-                )
-
-        def open_piece(c, lo, width):
-            ks = [(2 + PACK * c + k) % 8 for k in range(PACK)]
-            accs = [bank(k, "score") for k in ks[lo // P : (lo + width) // P]]
-            second_product(0, c, lo, width, accs)
-            return accs
-
-        def larger(words, at, c, lo):
-            cols = slice(lo, lo + HALF)
+        def larger(piece, room):
+            c, lo, width = piece
+            cols = slice(lo, lo + width)
+            words[piece] = tenant(room, "words", [P, PACK * width], BF16)
             nc.vector.tensor_tensor(
-                words[:, at : at + PACK * HALF].rearrange("p (c i t) -> p c t i", i=4, t=PACK),
+                words[piece][:].rearrange("p (c i t) -> p c t i", i=4, t=PACK),
                 page_dealt[c][:, :, cols].rearrange("p t (c i) -> p c t i", i=4),
                 old_dealt[c][:, :, cols].rearrange("p t (c i) -> p c t i", i=4),
                 ALU.max,
             )
 
-        staged = {}
+        def quantise_right(piece, room):
+            c, lo, width = piece
+            right_codes[piece] = tenant(room, "right_codes", [P, width], U32)
+            nc.vector.quantize_mx(right_codes[piece][:].bitcast(FP8X4), z_s[1][c][:, lo : lo + width], words[piece][:])
 
-        def close_piece(c, lo, width, accs):
+        def close_piece(piece, on_vector=()):
+            c, lo, width = piece
             cols = slice(c * BANK + lo, c * BANK + lo + width)
-            second_product(1, c, lo, width, accs)
+            shared = N // P // len(accs[piece])
+            for n in range(N // P):
+                score_pass(piece, 1, n, right_codes[piece][:], lo, width, False, n % shared == shared - 1)
             if lo == 0:
                 staged[c] = tenant(("page0", "page1", "page2", "big20")[c], "y", [P, N // P * BANK], F32)
             y = staged[c][:, N // P * lo : N // P * (lo + width)].rearrange("p (n c) -> p n c", n=N // P)
-            for k, acc in enumerate(accs):
-                if width == BANK:
-                    nc.scalar.activation(y[:, k, :], acc[:], ACT.Identity, bias=b4_t[:, k, 0:1])
-                    nc.sync.dma_start(out[k * P : (k + 1) * P, cols], y[:, k, :])
+            together = BANK // width
+            for n in range(N // P):
+                part = accs[piece][n // shared][:, n % shared * width : (n % shared + 1) * width]
+                if n in on_vector:
+                    nc.vector.tensor_scalar(y[:, n, :], part, b4_t[:, n, 0:1], None, ALU.add)
                 else:
-                    for i in range(2):
-                        n = 2 * k + i
-                        part = acc[:, i * width : (i + 1) * width]
-                        if k == 0 or (c, lo, width) != pieces[-1]:
-                            nc.scalar.activation(y[:, n, :], part, ACT.Identity, bias=b4_t[:, n, 0:1])
-                        else:
-                            nc.vector.tensor_scalar(y[:, n, :], part, b4_t[:, n, 0:1], None, ALU.add)
+                    nc.scalar.activation(y[:, n, :], part, ACT.Identity, bias=b4_t[:, n, 0:1])
+                if (n + 1) % together == 0:
+                    first = n + 1 - together
                     nc.sync.dma_start(
-                        out[2 * k * P : 2 * (k + 1) * P, cols].rearrange("(i p) c -> p i c", i=2),
-                        y[:, 2 * k : 2 * k + 2, :],
+                        out[first * P : (n + 1) * P, cols].rearrange("(i p) c -> p i c", i=together),
+                        y[:, first : n + 1, :],
                     )
-
-        pieces = [(0, 0, HALF), (0, HALF, HALF), (1, 0, BANK), (2, 0, HALF), (2, HALF, HALF), (3, 0, HALF), (3, HALF, HALF)]
-        accs, words = {}, {TURNED: quantiser_input("h1")}
-
-        def open_chunk(c):
-            for piece in pieces:
-                if piece[0] == c:
-                    accs[piece] = open_piece(*piece)
-
-        def quantise_first(c):
-            quantise_z(0, c, left_words[c])
-            if c != TURNED:
-                words[c] = quantiser_input(("ring2", "ring0", "ring1", "weights")[c])
-            open_chunk(c)
-
-        def finish(c, lo, width):
-            quantise_z(1, c, words[c][:, PACK * lo : PACK * (lo + width)], lo, width)
-            close_piece(c, lo, width, accs[c, lo, width])
 
         def copy_last_page(lo):
             nc.vector.tensor_copy(page_dealt[0][:, PACK - 1, lo : lo + HALF], pages[PACK - 1][:, lo : lo + HALF])
 
-        quantise_first(0)
+        quantise_left_whole(0, "bias")
+        for piece in pieces[:2]:
+            open_piece(piece)
         copy_last_page(0)
         nc.vector.tensor_tensor(
             turned_rows[:, PACK - 1, :],
@@ -448,24 +454,28 @@ def tile_list_recommender_slot_memory_kernel(
             old_dealt[TURNED][:, PACK - 1, :],
             ALU.max,
         )
+        words[pieces[2]] = quantiser_input("h1")
         nc.scalar.copy(
-            words[TURNED][:].rearrange("p (c i t) -> p c t i", i=4, t=PACK),
+            words[pieces[2]][:].rearrange("p (c i t) -> p c t i", i=4, t=PACK),
             turned_rows[:].rearrange("p t (c i) -> p c t i", i=4),
         )
-        codes = tenant("h0", "codes", [P, 2, BANK], U32)
-        for c in (2, 3):
-            z_c[0, c] = codes[:, c - 2, :]
-        larger(words[0], 0, 0, 0)
+        larger(pieces[0], "ring1")
         copy_last_page(HALF)
-        finish(0, 0, HALF)
-        larger(words[0], PACK * HALF, 0, HALF)
-        finish(0, HALF, HALF)
-        quantise_first(1)
-        finish(1, 0, BANK)
-        quantise_first(2)
-        larger(words[2], 0, 2, 0)
-        quantise_first(3)
-        finish(2, 0, HALF)
-        for c, lo in ((2, HALF), (3, 0), (3, HALF)):
-            larger(words[c], PACK * lo, c, lo)
-            finish(c, lo, HALF)
+        quantise_right(pieces[0], "v_w00")
+        close_piece(pieces[0])
+        larger(pieces[1], "ring2")
+        quantise_right(pieces[1], "v_w01")
+        close_piece(pieces[1])
+        quantise_left_whole(1, "big10")
+        open_piece(pieces[2])
+        quantise_left(2, 0, "h0")
+        quantise_right(pieces[2], "v_w10")
+        close_piece(pieces[2])
+        next_left = ("h1", "first0", "first1")
+        for k, piece in enumerate(pieces[3:]):
+            open_piece(piece)
+            larger(piece, left_rooms[k])
+            if k < len(next_left):
+                quantise_left(pieces[4 + k][0], pieces[4 + k][1], next_left[k])
+            quantise_right(piece, ("v_w11", "wg0", "wg1", "wg2")[k])
+            close_piece(piece, on_vector=(1, 3) if piece == pieces[-1] else ())

@@ -51,7 +51,7 @@ def tile_list_recommender_slot_memory_kernel(
         v_w = {(a, e): rooms.tile([P, BANK], U32, name="v_w", tag="v_w%d%d" % (a, e), align_bytes=64) for a in range(2) for e in range(2)}
         v_s = [held.tile([P, BANK], U8, name="v_s%d" % e, align_bytes=64) for e in range(2)]
         b1_rows = held.tile([P, PACK, 8], F32, name="b1_rows")
-        b1_dealt = rooms.tile([P, PACK], F32, name="b1_dealt", tag="bias", align_bytes=64)
+        b1_dealt = held.tile([P, PACK], F32, name="b1_dealt")
         b4_t = held.tile([P, N // P, 8], F32, name="b4_t")
         w4_s = held.tile([P, 2, N], U8, name="w4_s", align_bytes=64)
         ident = held.tile([P, P], F32, name="ident")
@@ -82,9 +82,15 @@ def tile_list_recommender_slot_memory_kernel(
             return rows
 
         def load_old_dealt(c):
-            rows = tenant(("old1", "old4", "old3", "old2")[c], "old_dealt", [P, PACK, BANK], F32)
+            rows = tenant(("old1", "old4", "old3", "old0")[c], "old_dealt", [P, PACK, BANK], F32)
             nc.sync.dma_start(rows[:], old[KP:, c * BANK : (c + 1) * BANK].rearrange("(p t) c -> p t c", t=PACK))
             return rows
+
+        def load_weights_dealt(t):
+            weights = tenant("wg%d" % t, "wg_dealt", [P, S], F32)
+            for g in (0, 2, 1, 3):
+                nc.sync.dma_start(weights[32 * g : 32 * g + 32, :], wgs.rearrange("(q t) c -> t q c", t=PACK)[t])
+            return weights
 
         nc.sync.dma_start(tab_w[0][:], tab_words_i[0])
         for q in range(4):
@@ -101,28 +107,20 @@ def tile_list_recommender_slot_memory_kernel(
         with nc.allow_non_contiguous_dma(reason="one bias value a partition"):
             nc.sync.dma_start(b1_rows[:, 1:, 0:1], b1[P:KP].rearrange("(s p o) -> p s o", p=P, o=1))
         olds = {0: load_old(0)}
-        raw_dealt = {
-            (a, e): load_w1(("old3", "wg1", "wg2", "page3")[2 * a + e], a, slice(KP + e * HALF, KP + (e + 1) * HALF))
-            for a in range(2)
-            for e in range(2)
-        }
+        raw_dealt = {}
+        for a in range(2):
+            for e in range(2):
+                room = ("old3", "wg2", "wg3", "h3")[2 * a + e]
+                raw_dealt[a, e] = load_w1(room, a, slice(KP + e * HALF, KP + (e + 1) * HALF))
         for s in (1, 2):
             olds[s] = load_old(s)
         nc.sync.dma_start(b1_dealt[:], b1[KP:].rearrange("(p t) -> p t", t=PACK))
-        nc.sync.dma_start(w4_w[:].bitcast(I32), w4_words.rearrange("a p n -> p a n").bitcast(I32))
-        for q in range(4):
-            nc.sync.dma_start(
-                w4_s[32 * q : 32 * q + 4, :, :].bitcast(I32),
-                w4_scales[:, 4 * q : 4 * q + 4, :].rearrange("a r n -> r a n").bitcast(I32),
-            )
-        with nc.allow_non_contiguous_dma(reason="one bias value a partition"):
-            nc.sync.dma_start(b4_t[:, :, 0:1], b4.rearrange("(i p o) -> p i o", p=P, o=1))
 
         w1_c, w1_s = {}, {}
 
         def quantise_w1(slices, grouped):
             n = len(slices)
-            codes = held.tile([P, 2 * n * P], U32, name="w1_c%d" % slices[0], align_bytes=64)
+            codes = tenant("page3" if slices == [1] else "w1_codes%d" % slices[0], "w1_codes", [P, 2 * n * P], U32)
             scales = held.tile([P, 2 * n * P], U8, name="w1_s%d" % slices[0], align_bytes=64)
             nc.vector.quantize_mx(codes[:].bitcast(FP8X4), scales[:], grouped[:, : 2 * n * KP])
             for a in range(2):
@@ -203,6 +201,8 @@ def tile_list_recommender_slot_memory_kernel(
         quantise_w1([2, 3], cast_rows(raw_rest, 0, 2 * P, quantiser_input("ring2")))
         scatter_part("h0_third", [second_half[:, HALF:]], BANK + HALF)
         first_product(1, banks=(2, 3), room="ring2")
+        pages.append(tenant("page3", "page", [P, T2], F32))
+        nc.gpsimd.memset(pages[3][:].bitcast(I32), 0)
 
         def scatter(s):
             weights = minus_wg[:] if s < PACK else wg_dealt[s - PACK][:]
@@ -267,9 +267,9 @@ def tile_list_recommender_slot_memory_kernel(
         scatter(1)
         close_differences(0, open_differences(0))
         olds[3] = load_old(3)
+        wg_dealt = {t: load_weights_dealt(t) for t in range(2)}
         half_product(2, 1, 5)
         turn_page(0, (6, 7, 4, 5))
-        half_product(3, 0, 6)
         dealt_grouped = []
         for a in range(2):
             grouped = quantiser_input("ring%d" % a)
@@ -280,35 +280,44 @@ def tile_list_recommender_slot_memory_kernel(
                 )
             dealt_grouped.append(grouped)
 
-        pages.append(tenant("page3", "page", [P, T2], F32))
-        nc.gpsimd.memset(pages[3][:].bitcast(I32), 0)
-        wg_dealt = [tenant("wg%d" % t, "wg_dealt", [P, S], F32) for t in range(PACK)]
-        for t in range(PACK):
-            for g in (0, 2, 1, 3):
-                nc.sync.dma_start(wg_dealt[t][32 * g : 32 * g + 32, :], wgs.rearrange("(q t) c -> t q c", t=PACK)[t])
+        half_product(3, 0, 6)
+        half_product(3, 1, 7)
+        for t in range(2, PACK):
+            wg_dealt[t] = load_weights_dealt(t)
+        old_dealt = {TURNED: load_old_dealt(TURNED)}
         scatter(2)
         for a in range(2):
             quantise_dealt(a)
-        old_dealt = {c: load_old_dealt(c) for c in (1, 2)}
         close_differences(1, open_differences(1))
-        old_dealt[0] = load_old_dealt(0)
-        half_product(3, 1, 7)
         scatter(3)
+        for c in (0, 2):
+            old_dealt[c] = load_old_dealt(c)
+        nc.sync.dma_start(w4_w[:].bitcast(I32), w4_words.rearrange("a p n -> p a n").bitcast(I32))
+        for q in range(4):
+            nc.sync.dma_start(
+                w4_s[32 * q : 32 * q + 4, :, :].bitcast(I32),
+                w4_scales[:, 4 * q : 4 * q + 4, :].rearrange("a r n -> r a n").bitcast(I32),
+            )
+        with nc.allow_non_contiguous_dma(reason="one bias value a partition"):
+            nc.sync.dma_start(b4_t[:, :, 0:1], b4.rearrange("(i p o) -> p i o", p=P, o=1))
         turn_page(1, (4, 5, 6, 7))
-        close_differences(2, open_differences(2))
-        old_dealt[3] = load_old_dealt(3)
-        early = old_dealt[TURNED][:, : PACK - 1, :]
-        nc.scalar.activation(early, early, ACT.Copy, scale=-1.0)
+        differences = open_differences(2)
         half_product(4, 0, 4)
-        turn_page(2, (5, 6, 7, 4))
         half_product(4, 1, 5)
         scatter(4)
-        differences = open_differences(3)
+        close_differences(2, differences)
+        turn_page(2, (6, 7, 4, 5))
         half_product(5, 0, 6)
-        close_differences(3, differences)
+        differences = open_differences(3)
         half_product(5, 1, 7)
         scatter(5)
-        turn_page(3, (4, 5, 6, 7))
+        early = tenant("old0", "minus_old", [P, PACK - 1, BANK], F32)
+        nc.scalar.activation(early[:], old_dealt[TURNED][:, : PACK - 1, :], ACT.Copy, scale=-1.0)
+        close_differences(3, differences)
+        half_product(6, 0, 4)
+        turn_page(3, (5, 6, 7, 4))
+        half_product(6, 1, 5)
+        scatter(6)
         left_rooms = ("first0", "first1", "h0_second", "h0_third")
         halves = [(c, lo) for c in range(2, CHUNKS) for lo in (0, HALF)]
         left_tiles = {at: tenant(room, "left_words", [P, PACK * HALF], BF16)[:] for at, room in zip(halves, left_rooms)}
@@ -320,15 +329,12 @@ def tile_list_recommender_slot_memory_kernel(
             c: [left_tiles[c, i // 2 * HALF][:, i % 2 * BANK : (i % 2 + 1) * BANK] for i in range(BLOCKS)] for c in range(CHUNKS)
         }
         turn_back(0, left_words[0], (0, 1), (0, 1))
-        half_product(6, 0, 2)
-        turn_back(0, left_words[0], (2, 3), (3, 4))
-        half_product(6, 1, 5)
-        scatter(6)
-        turn_back(1, left_words[1], (0, 1), (6, 7))
-        half_product(7, 0, 0)
-        turn_back(1, left_words[1], (2, 3), (1, 2))
-        half_product(7, 1, 3)
+        half_product(7, 0, 2)
+        turn_back(0, left_words[0], (2,), (3,))
+        half_product(7, 1, 7)
         scatter(7)
+        turn_back(0, left_words[0], (3,), (6,))
+        turn_back(1, left_words[1], range(BLOCKS), (4, 5, 0, 1))
         planes = [tenant("big1%d" % k, "planes", [P, BLOCKS, PACK - 1, P], F32) for k in range(2)]
 
         def turn_dealt(t, banks):
@@ -382,11 +388,12 @@ def tile_list_recommender_slot_memory_kernel(
             for n in range(N // P):
                 score_pass(piece, 0, n, left_codes[c, lo], lo, width, n % shared == 0, False)
 
-        turn_dealt(0, (4, 5))
-        turn_back(2, left_words[2], range(BLOCKS), (6, 7, 0, 1))
-        turn_dealt(1, (2, 3))
-        turn_back(3, left_words[3], range(BLOCKS), (4, 5, 6, 7))
+        turn_dealt(0, (2, 3))
+        turn_back(2, left_words[2], range(BLOCKS), (6, 7, 4, 5))
+        turn_dealt(1, (0, 1))
+        turn_back(3, left_words[3], range(BLOCKS), (2, 3, 6, 7))
         turn_dealt(2, (0, 1))
+        old_dealt[3] = load_old_dealt(3)
         turned_rows = tenant("h0", "turned_rows", [P, PACK, BANK], BF16)
         for i in range(BLOCKS):
             larger_rows = bank(2 + i, "larger")
@@ -396,7 +403,7 @@ def tile_list_recommender_slot_memory_kernel(
                 turned_rows[:, : PACK - 1, i * P : (i + 1) * P],
                 larger_rows[:, : (PACK - 1) * P].rearrange("p (t c) -> p t c", t=PACK - 1),
             )
-        page_dealt = {c: tenant(room, "page_dealt", [P, PACK, BANK], F32) for c, room in ((0, "side0"), (2, "old0"), (3, "big00"))}
+        page_dealt = {c: tenant(room, "page_dealt", [P, PACK, BANK], F32) for c, room in ((0, "side0"), (2, "old2"), (3, "big00"))}
         for t in range(PACK):
             for c in page_dealt:
                 if (t, c) != (PACK - 1, 0):
@@ -444,7 +451,7 @@ def tile_list_recommender_slot_memory_kernel(
         def copy_last_page(lo):
             nc.vector.tensor_copy(page_dealt[0][:, PACK - 1, lo : lo + HALF], pages[PACK - 1][:, lo : lo + HALF])
 
-        quantise_left_whole(0, "bias")
+        quantise_left_whole(0, "v_w11")
         for piece in pieces[:2]:
             open_piece(piece)
         copy_last_page(0)
@@ -477,5 +484,5 @@ def tile_list_recommender_slot_memory_kernel(
             larger(piece, left_rooms[k])
             if k < len(next_left):
                 quantise_left(pieces[4 + k][0], pieces[4 + k][1], next_left[k])
-            quantise_right(piece, ("v_w11", "wg0", "wg1", "wg2")[k])
+            quantise_right(piece, ("h3", "wg0", "wg1", "wg2")[k])
             close_piece(piece, on_vector=(1, 3) if piece == pieces[-1] else ())

@@ -48,8 +48,11 @@ def tile_list_recommender_slot_memory_kernel(
 
         idx = held.tile([P, S // 16], U16, name="idx")
         idx2 = held.tile([P, S // 16], U16, name="idx2")
-        v_w = {(a, e): rooms.tile([P, BANK], U32, name="v_w", tag="v_w%d%d" % (a, e), align_bytes=64) for a in range(2) for e in range(2)}
-        v_s = [held.tile([P, BANK], U8, name="v_s%d" % e, align_bytes=64) for e in range(2)]
+        v_first = tenant("v_w0", "v_first", [P, S], U32)
+        v_w = {(0, e): v_first[:, e * BANK : (e + 1) * BANK] for e in range(2)}
+        for e in range(2):
+            v_w[1, e] = tenant("v_w1%d" % e, "v_second", [P, BANK], U32)[:]
+        v_s = held.tile([P, S], U8, name="v_s", align_bytes=64)
         b1_rows = held.tile([P, PACK, 8], F32, name="b1_rows")
         b1_dealt = held.tile([P, PACK], F32, name="b1_dealt")
         b4_t = held.tile([P, N // P, 8], F32, name="b4_t")
@@ -67,7 +70,6 @@ def tile_list_recommender_slot_memory_kernel(
         nc.gpsimd.memset(tab_s[:].bitcast(I32), 0)
         make_identity(nc, ident[:])
         nc.vector.memset(pages[0][:].bitcast(I32), 0)
-        nc.sync.dma_start(idx[:], offs)
         nc.gpsimd.memset(w4_s[:].rearrange("p a n -> p (a n)").bitcast(I32), 0)
         tab_words_i = tab_words.rearrange("a p t i -> a p (t i)").bitcast(I32)
 
@@ -93,6 +95,7 @@ def tile_list_recommender_slot_memory_kernel(
             return weights
 
         nc.sync.dma_start(tab_w[0][:], tab_words_i[0])
+        nc.sync.dma_start(idx[:], offs)
         for q in range(4):
             nc.sync.dma_start(tab_s[32 * q : 32 * q + 8, :].bitcast(I32), tab_scales[:, 4 * q : 4 * q + 4, :].bitcast(I32))
         raw_first = [load_w1("first%d" % a, a, slice(0, P)) for a in range(2)]
@@ -103,7 +106,7 @@ def tile_list_recommender_slot_memory_kernel(
             nc.scalar.dma_start(b1_rows[:, 0, 0:1], b1[:P].rearrange("(p o) -> p o", o=1))
         nc.sync.dma_start(idx2[:], offs2)
         raw_second = [load_w1(room, a, slice(P, 2 * P)) for a, room in enumerate(("wg0", "h0_second"))]
-        raw_rest = [load_w1(room, a, slice(2 * P, KP)) for a, room in enumerate(("big11", "h0_third"))]
+        raw_rest = [load_w1(room, a, slice(2 * P, KP)) for a, room in enumerate(("big11", "page3"))]
         with nc.allow_non_contiguous_dma(reason="one bias value a partition"):
             nc.sync.dma_start(b1_rows[:, 1:, 0:1], b1[P:KP].rearrange("(s p o) -> p s o", p=P, o=1))
         olds = {0: load_old(0)}
@@ -120,7 +123,7 @@ def tile_list_recommender_slot_memory_kernel(
 
         def quantise_w1(slices, grouped):
             n = len(slices)
-            codes = tenant("page3" if slices == [1] else "w1_codes%d" % slices[0], "w1_codes", [P, 2 * n * P], U32)
+            codes = held.tile([P, 2 * n * P], U32, name="w1_c%d" % slices[0], align_bytes=64)
             scales = held.tile([P, 2 * n * P], U8, name="w1_s%d" % slices[0], align_bytes=64)
             nc.vector.quantize_mx(codes[:].bitcast(FP8X4), scales[:], grouped[:, : 2 * n * KP])
             for a in range(2):
@@ -137,21 +140,16 @@ def tile_list_recommender_slot_memory_kernel(
                 )
             return grouped
 
-        def half(entries, e):
-            return entries[:, e * BANK // 16 : (e + 1) * BANK // 16]
-
         for k in (1, 2):
             pages.append(tenant("page%d" % k, "page", [P, T2], F32))
             nc.gpsimd.memset(pages[k][:].bitcast(I32), 0)
-        for e in range(2):
-            nc.vector.tensor_copy(v_w[0, e][:], tab_w[0][:].bitcast(U32).indirect(half(idx, e)))
-        for e in range(2):
-            nc.vector.tensor_copy(v_s[e][:], tab_s[:].indirect(half(idx, e)))
+        nc.vector.tensor_copy(v_first[:], tab_w[0][:].bitcast(U32).indirect(idx[:]))
+        nc.vector.tensor_copy(v_s[:], tab_s[:].indirect(idx[:]))
         quantise_w1([0], cast_rows(raw_first, 0, P, quantiser_input("ring0")))
         for lo in (0, HALF):
             entries = idx[:, lo // 16 : (lo + HALF) // 16]
             nc.vector.tensor_copy(v_w[1, 0][:, lo : lo + HALF], tab_w[1][:].bitcast(U32).indirect(entries))
-        nc.vector.tensor_copy(v_w[1, 1][:], tab_w[1][:].bitcast(U32).indirect(half(idx, 1)))
+        nc.vector.tensor_copy(v_w[1, 1], tab_w[1][:].bitcast(U32).indirect(idx[:, BANK // 16 :]))
         for cols in (slice(0, BANK), slice(BANK, S)):
             nc.gpsimd.tensor_scalar(minus_wg[:, cols], minus_wg[:, cols], -1.0, 0.0, ALU.mult, ALU.add)
 
@@ -165,7 +163,7 @@ def tile_list_recommender_slot_memory_kernel(
                     lhsT=w1_c[a, s].bitcast(FP8X4),
                     lhsT_scale=w1_s[a, s],
                     rhs=v_w[a, e][:, cols].bitcast(FP8X4),
-                    rhs_scale=v_s[e][4 * a :, cols],
+                    rhs_scale=v_s[4 * a :, e * BANK + cols.start : e * BANK + cols.stop],
                     start=(a == 0),
                     stop=(a == 1),
                 )
@@ -193,13 +191,13 @@ def tile_list_recommender_slot_memory_kernel(
             entries = idx2[:, lo // 16 : (lo + width) // 16]
             nc.vector.tensor_tensor(pages[0][:].indirect(entries), h[:], minus_wg[:, lo : lo + width], ALU.mult)
 
-        for room, k, lo in (("h0", 0, 0), ("h1", 4, HALF)):
-            scatter_part(room, [product(0, 0, k, slice(lo, lo + HALF))[:, lo : lo + HALF]], lo)
+        scatter_part("h0", [product(0, 0, 0, slice(0, HALF))[:, :HALF]], 0)
+        second_quarter = product(0, 0, 4, slice(HALF, BANK))
         second_half = product(0, 1, 1)
         quantise_w1([1], cast_rows(raw_second, 0, P, quantiser_input("ring1")))
-        scatter_part("h0_second", [second_half[:, :HALF]], BANK)
+        scatter_part("h0_second", [second_quarter[:, HALF:], second_half[:, :HALF]], HALF)
         quantise_w1([2, 3], cast_rows(raw_rest, 0, 2 * P, quantiser_input("ring2")))
-        scatter_part("h0_third", [second_half[:, HALF:]], BANK + HALF)
+        scatter_part("page3", [second_half[:, HALF:]], BANK + HALF)
         first_product(1, banks=(2, 3), room="ring2")
         pages.append(tenant("page3", "page", [P, T2], F32))
         nc.gpsimd.memset(pages[3][:].bitcast(I32), 0)
@@ -290,8 +288,30 @@ def tile_list_recommender_slot_memory_kernel(
             quantise_dealt(a)
         close_differences(1, open_differences(1))
         scatter(3)
-        for c in (0, 2):
-            old_dealt[c] = load_old_dealt(c)
+        old_dealt[0] = load_old_dealt(0)
+        turn_page(1, (4, 5, 6, 7))
+        differences = open_differences(2)
+        half_product(4, 0, 4)
+        half_product(4, 1, 5)
+        scatter(4)
+        page_dealt = {0: tenant("side0", "page_dealt", [P, PACK, BANK], F32)}
+        nc.sync.dma_start(page_dealt[0][:, 0, :], pages[0][:, :BANK])
+        close_differences(2, differences)
+        turn_page(2, (6, 7, 4, 5))
+        half_product(5, 0, 6)
+        differences = open_differences(3)
+        half_product(5, 1, 7)
+        scatter(5)
+        nc.sync.dma_start(page_dealt[0][:, 1, :], pages[1][:, :BANK])
+        early = tenant("old0", "minus_old", [P, PACK - 1, BANK], F32)
+        nc.scalar.activation(early[:], old_dealt[TURNED][:, : PACK - 1, :], ACT.Copy, scale=-1.0)
+        close_differences(3, differences)
+        half_product(6, 0, 4)
+        turn_page(3, (5, 6, 7, 4))
+        half_product(6, 1, 5)
+        scatter(6)
+        nc.sync.dma_start(page_dealt[0][:, 2, :], pages[2][:, :BANK])
+        old_dealt[2] = load_old_dealt(2)
         nc.sync.dma_start(w4_w[:].bitcast(I32), w4_words.rearrange("a p n -> p a n").bitcast(I32))
         for q in range(4):
             nc.sync.dma_start(
@@ -300,24 +320,6 @@ def tile_list_recommender_slot_memory_kernel(
             )
         with nc.allow_non_contiguous_dma(reason="one bias value a partition"):
             nc.sync.dma_start(b4_t[:, :, 0:1], b4.rearrange("(i p o) -> p i o", p=P, o=1))
-        turn_page(1, (4, 5, 6, 7))
-        differences = open_differences(2)
-        half_product(4, 0, 4)
-        half_product(4, 1, 5)
-        scatter(4)
-        close_differences(2, differences)
-        turn_page(2, (6, 7, 4, 5))
-        half_product(5, 0, 6)
-        differences = open_differences(3)
-        half_product(5, 1, 7)
-        scatter(5)
-        early = tenant("old0", "minus_old", [P, PACK - 1, BANK], F32)
-        nc.scalar.activation(early[:], old_dealt[TURNED][:, : PACK - 1, :], ACT.Copy, scale=-1.0)
-        close_differences(3, differences)
-        half_product(6, 0, 4)
-        turn_page(3, (5, 6, 7, 4))
-        half_product(6, 1, 5)
-        scatter(6)
         left_rooms = ("first0", "first1", "h0_second", "h0_third")
         halves = [(c, lo) for c in range(2, CHUNKS) for lo in (0, HALF)]
         left_tiles = {at: tenant(room, "left_words", [P, PACK * HALF], BF16)[:] for at, room in zip(halves, left_rooms)}
@@ -328,12 +330,12 @@ def tile_list_recommender_slot_memory_kernel(
         left_words = {
             c: [left_tiles[c, i // 2 * HALF][:, i % 2 * BANK : (i % 2 + 1) * BANK] for i in range(BLOCKS)] for c in range(CHUNKS)
         }
-        turn_back(0, left_words[0], (0, 1), (0, 1))
+        turn_back(0, left_words[0], (0, 2), (0, 1))
         half_product(7, 0, 2)
-        turn_back(0, left_words[0], (2,), (3,))
+        turn_back(0, left_words[0], (3,), (3,))
         half_product(7, 1, 7)
         scatter(7)
-        turn_back(0, left_words[0], (3,), (6,))
+        turn_back(0, left_words[0], (1,), (6,))
         turn_back(1, left_words[1], range(BLOCKS), (4, 5, 0, 1))
         planes = [tenant("big1%d" % k, "planes", [P, BLOCKS, PACK - 1, P], F32) for k in range(2)]
 
@@ -394,20 +396,22 @@ def tile_list_recommender_slot_memory_kernel(
         turn_back(3, left_words[3], range(BLOCKS), (2, 3, 6, 7))
         turn_dealt(2, (0, 1))
         old_dealt[3] = load_old_dealt(3)
-        turned_rows = tenant("h0", "turned_rows", [P, PACK, BANK], BF16)
+        turned_rows = tenant("h0", "turned_rows", [P, 2, BANK], BF16)
+        words[pieces[2]] = quantiser_input("h1")
+        turned_words = words[pieces[2]][:].rearrange("p (c t) -> p c t", t=PACK)
         for i in range(BLOCKS):
             larger_rows = bank(2 + i, "larger")
             for t in range(PACK - 1):
                 add_transposed(larger_rows[:, t * P : (t + 1) * P], planes[1][:, i, t, :], planes[0][:, i, t, :])
             nc.scalar.copy(
-                turned_rows[:, : PACK - 1, i * P : (i + 1) * P],
-                larger_rows[:, : (PACK - 1) * P].rearrange("p (t c) -> p t c", t=PACK - 1),
+                turned_words[:, i * P : (i + 1) * P, :2], larger_rows[:, : 2 * P].rearrange("p (t c) -> p c t", t=2)
             )
-        page_dealt = {c: tenant(room, "page_dealt", [P, PACK, BANK], F32) for c, room in ((0, "side0"), (2, "old2"), (3, "big00"))}
+            nc.scalar.copy(turned_rows[:, 0, i * P : (i + 1) * P], larger_rows[:, 2 * P : 3 * P])
+        for c, room in ((2, "old2"), (3, "big00")):
+            page_dealt[c] = tenant(room, "page_dealt", [P, PACK, BANK], F32)
         for t in range(PACK):
-            for c in page_dealt:
-                if (t, c) != (PACK - 1, 0):
-                    nc.sync.dma_start(page_dealt[c][:, t, :], pages[t][:, c * BANK : (c + 1) * BANK])
+            for c in (2, 3):
+                nc.sync.dma_start(page_dealt[c][:, t, :], pages[t][:, c * BANK : (c + 1) * BANK])
 
         def larger(piece, room):
             c, lo, width = piece
@@ -451,27 +455,24 @@ def tile_list_recommender_slot_memory_kernel(
         def copy_last_page(lo):
             nc.vector.tensor_copy(page_dealt[0][:, PACK - 1, lo : lo + HALF], pages[PACK - 1][:, lo : lo + HALF])
 
-        quantise_left_whole(0, "v_w11")
-        for piece in pieces[:2]:
-            open_piece(piece)
+        quantise_left(0, 0, "v_w11")
+        open_piece(pieces[0])
         copy_last_page(0)
         nc.vector.tensor_tensor(
-            turned_rows[:, PACK - 1, :],
+            turned_rows[:, 1, :],
             pages[PACK - 1][:, TURNED * BANK : (TURNED + 1) * BANK],
             old_dealt[TURNED][:, PACK - 1, :],
             ALU.max,
         )
-        words[pieces[2]] = quantiser_input("h1")
-        nc.scalar.copy(
-            words[pieces[2]][:].rearrange("p (c i t) -> p c t i", i=4, t=PACK),
-            turned_rows[:].rearrange("p t (c i) -> p c t i", i=4),
-        )
+        nc.scalar.copy(turned_words[:, :, 2:], turned_rows[:].rearrange("p t c -> p c t"))
         larger(pieces[0], "ring1")
         copy_last_page(HALF)
-        quantise_right(pieces[0], "v_w00")
+        quantise_right(pieces[0], "v_w0")
         close_piece(pieces[0])
-        larger(pieces[1], "ring2")
-        quantise_right(pieces[1], "v_w01")
+        larger(pieces[1], "weights")
+        quantise_left(0, HALF, "ring1")
+        open_piece(pieces[1])
+        quantise_right(pieces[1], "h2")
         close_piece(pieces[1])
         quantise_left_whole(1, "big10")
         open_piece(pieces[2])

@@ -84,7 +84,7 @@ def tile_list_recommender_slot_memory_kernel(
             return rows
 
         def load_old_dealt(c):
-            rows = tenant(("old1", "old4", "old3", "old0")[c], "old_dealt", [P, PACK, BANK], F32)
+            rows = tenant(("old1", "old4", "old3", "old5")[c], "old_dealt", [P, PACK, BANK], F32)
             nc.sync.dma_start(rows[:], old[KP:, c * BANK : (c + 1) * BANK].rearrange("(p t) c -> p t c", t=PACK))
             return rows
 
@@ -312,6 +312,7 @@ def tile_list_recommender_slot_memory_kernel(
         scatter(6)
         nc.sync.dma_start(page_dealt[0][:, 2, :], pages[2][:, :BANK])
         old_dealt[2] = load_old_dealt(2)
+        old_dealt[3] = load_old_dealt(3)
         nc.sync.dma_start(w4_w[:].bitcast(I32), w4_words.rearrange("a p n -> p a n").bitcast(I32))
         for q in range(4):
             nc.sync.dma_start(
@@ -395,7 +396,6 @@ def tile_list_recommender_slot_memory_kernel(
         turn_dealt(1, (0, 1))
         turn_back(3, left_words[3], range(BLOCKS), (2, 3, 6, 7))
         turn_dealt(2, (0, 1))
-        old_dealt[3] = load_old_dealt(3)
         turned_rows = tenant("h0", "turned_rows", [P, 2, BANK], BF16)
         words[pieces[2]] = quantiser_input("h1")
         turned_words = words[pieces[2]][:].rearrange("p (c t) -> p c t", t=PACK)

@@ -418,9 +418,9 @@ def tile_list_recommender_slot_memory_kernel(
             cols = slice(lo, lo + width)
             words[piece] = tenant(room, "words", [P, PACK * width], BF16)
             nc.vector.tensor_tensor(
-                words[piece][:].rearrange("p (c i t) -> p c t i", i=4, t=PACK),
-                page_dealt[c][:, :, cols].rearrange("p t (c i) -> p c t i", i=4),
-                old_dealt[c][:, :, cols].rearrange("p t (c i) -> p c t i", i=4),
+                words[piece][:].rearrange("p (c i t) -> p c t i", i=8, t=PACK),
+                page_dealt[c][:, :, cols].rearrange("p t (c i) -> p c t i", i=8),
+                old_dealt[c][:, :, cols].rearrange("p t (c i) -> p c t i", i=8),
                 ALU.max,
             )
 

from contextlib import ExitStack

import concourse.mybir as mybir
from concourse.masks import make_identity

K, T, S, T2, H, N = 1024, 2048, 1024, 2048, 1024, 512
FLOPS = 2 * K * H * S + 2 * H * N * T2

P = 128
PACK = 4
KP = P * PACK
BANK = 512
HALF = BANK // 2
SLICES = H // P
CHUNKS = T2 // BANK
BLOCKS = BANK // P
TURNED = 1

F32 = mybir.dt.float32
BF16 = mybir.dt.bfloat16
I32 = mybir.dt.int32
U32 = mybir.dt.uint32
U16 = mybir.dt.uint16
U8 = mybir.dt.uint8
FP8X4 = mybir.dt.float8_e4m3fn_x4
FP4X4 = mybir.dt.float4_e2m1fn_x4
ALU = mybir.AluOpType
ACT = mybir.ActivationFunctionType


def tile_list_recommender_slot_memory_kernel(
    tc, tab_words, tab_scales, offs, w1, b1, wgs, offs2, old, w4_words, w4_scales, b4, out
):
    nc = tc.nc
    with ExitStack() as ctx:
        held = ctx.enter_context(tc.tile_pool(name="held", bufs=1))
        rooms = ctx.enter_context(tc.tile_pool(name="rooms", bufs=1))
        psum = ctx.enter_context(tc.psum_pool(name="psum", bufs=1))

        def tenant(room, name, shape, dtype):
            return rooms.tile(shape, dtype, name=name, tag=room, align_bytes=64)

        def quantiser_input(room):
            return tenant(room, "grouped", [P, PACK * BANK], BF16)

        def bank(k, name):
            return psum.tile([P, BANK], F32, name=name, tag="bank%d" % k)

        idx = held.tile([P, S // 16], U16, name="idx")
        idx2 = held.tile([P, S // 16], U16, name="idx2")
        v_first = tenant("v_w0", "v_first", [P, S], U32)
        v_w = {(0, e): v_first[:, e * BANK : (e + 1) * BANK] for e in range(2)}
        for e in range(2):
            v_w[1, e] = tenant("v_w1%d" % e, "v_second", [P, BANK], U32)[:]
        v_s = held.tile([P, S], U8, name="v_s", align_bytes=64)
        b1_rows = held.tile([P, PACK, 8], F32, name="b1_rows")
        b1_dealt = held.tile([P, PACK], F32, name="b1_dealt")
        b4_t = held.tile([P, N // P, 8], F32, name="b4_t")
        w4_s = held.tile([P, 2, N], U8, name="w4_s", align_bytes=64)
        ident = held.tile([P, P], F32, name="ident")
        z_s = [
            [held.tile([P, BANK], U8, name="z_s%d%d" % (b, c), align_bytes=64) for c in range(CHUNKS)] for b in range(2)
        ]
        pages = [tenant("page0", "page", [P, T2], F32)]
        minus_wg = tenant("weights", "minus_wg", [P, S], F32)
        w4_w = held.tile([P, 2, 2 * N], U8, name="w4_w", align_bytes=64)
        tab_s = tenant("h2", "tab_s", [P, T], U8)
        tab_w = [tenant("big0%d" % a, "tab_w%d" % a, [P, T], I32) for a in range(2)]

        nc.gpsimd.memset(tab_s[:].bitcast(I32), 0)
        make_identity(nc, ident[:])
        nc.vector.memset(pages[0][:].bitcast(I32), 0)
        nc.gpsimd.memset(w4_s[:].rearrange("p a n -> p (a n)").bitcast(I32), 0)
        tab_words_i = tab_words.rearrange("a p t i -> a p (t i)").bitcast(I32)

        def load_w1(room, a, cols):
            raw = tenant(room, "w1_raw", [P, PACK, cols.stop - cols.start], F32)
            nc.sync.dma_start(raw[:], w1[a * KP : (a + 1) * KP, cols].rearrange("(p j) c -> p j c", j=PACK))
            return raw

        def load_old(s):
            rows = tenant("old%d" % (s % 3), "old_rows", [P, T2], F32)
            nc.sync.dma_start(rows[:], old[s * P : (s + 1) * P, :])
            return rows

        def load_old_dealt(c):
            rows = tenant(("old1", "old4", "old3", "old5")[c], "old_dealt", [P, PACK, BANK], F32)
            nc.sync.dma_start(rows[:], old[KP:, c * BANK : (c + 1) * BANK].rearrange("(p t) c -> p t c", t=PACK))
            return rows

        def load_weights_dealt(t):
            weights = tenant("wg%d" % t, "wg_dealt", [P, S], F32)
            for g in (0, 2, 1, 3):
                nc.sync.dma_start(weights[32 * g : 32 * g + 32, :], wgs.rearrange("(q t) c -> t q c", t=PACK)[t])
            return weights

        nc.sync.dma_start(tab_w[0][:], tab_words_i[0])
        nc.sync.dma_start(idx[:], offs)
        for q in range(4):
            nc.sync.dma_start(tab_s[32 * q : 32 * q + 8, :].bitcast(I32), tab_scales[:, 4 * q : 4 * q + 4, :].bitcast(I32))
        raw_first = [load_w1("first%d" % a, a, slice(0, P)) for a in range(2)]
        nc.sync.dma_start(tab_w[1][:], tab_words_i[1])
        for e in range(2):
            nc.sync.dma_start(minus_wg[:, e * BANK : (e + 1) * BANK], wgs[:, e * BANK : (e + 1) * BANK])
        with nc.allow_non_contiguous_dma(reason="one bias value a partition"):
            nc.scalar.dma_start(b1_rows[:, 0, 0:1], b1[:P].rearrange("(p o) -> p o", o=1))
        nc.sync.dma_start(idx2[:], offs2)
        raw_second = [load_w1(room, a, slice(P, 2 * P)) for a, room in enumerate(("wg0", "h0_second"))]
        raw_rest = [load_w1(room, a, slice(2 * P, KP)) for a, room in enumerate(("big11", "page3"))]
        with nc.allow_non_contiguous_dma(reason="one bias value a partition"):
            nc.sync.dma_start(b1_rows[:, 1:, 0:1], b1[P:KP].rearrange("(s p o) -> p s o", p=P, o=1))
        olds = {0: load_old(0)}
        raw_dealt = {}
        for a in range(2):
            for e in range(2):
                room = ("old3", "wg2", "wg3", "h3")[2 * a + e]
                raw_dealt[a, e] = load_w1(room, a, slice(KP + e * HALF, KP + (e + 1) * HALF))
        for s in (1, 2):
            olds[s] = load_old(s)
        nc.sync.dma_start(b1_dealt[:], b1[KP:].rearrange("(p t) -> p t", t=PACK))

        w1_c, w1_s = {}, {}

        def quantise_w1(slices, grouped):
            n = len(slices)
            codes = held.tile([P, 2 * n * P], U32, name="w1_c%d" % slices[0], align_bytes=64)
            scales = held.tile([P, 2 * n * P], U8, name="w1_s%d" % slices[0], align_bytes=64)
            nc.vector.quantize_mx(codes[:].bitcast(FP8X4), scales[:], grouped[:, : 2 * n * KP])
            for a in range(2):
                for k, s in enumerate(slices):
                    at = (a * n + k) * P
                    w1_c[a, s] = codes[:, at : at + P]
                    w1_s[a, s] = scales[:, at : at + P]

        def cast_rows(raws, lo, width, grouped):
            for a in range(2):
                nc.scalar.copy(
                    grouped[:, a * width * PACK : (a + 1) * width * PACK].rearrange("p (c i j) -> p c j i", i=4, j=PACK),
                    raws[a][:, :, lo : lo + width].rearrange("p j (c i) -> p c j i", i=4),
                )
            return grouped

        for k in (1, 2):
            pages.append(tenant("page%d" % k, "page", [P, T2], F32))
            nc.gpsimd.memset(pages[k][:].bitcast(I32), 0)
        nc.vector.tensor_copy(v_first[:], tab_w[0][:].bitcast(U32).indirect(idx[:]))
        nc.vector.tensor_copy(v_s[:], tab_s[:].indirect(idx[:]))
        quantise_w1([0], cast_rows(raw_first, 0, P, quantiser_input("ring0")))
        for lo in (0, HALF):
            entries = idx[:, lo // 16 : (lo + HALF) // 16]
            nc.vector.tensor_copy(v_w[1, 0][:, lo : lo + HALF], tab_w[1][:].bitcast(U32).indirect(entries))
        nc.vector.tensor_copy(v_w[1, 1], tab_w[1][:].bitcast(U32).indirect(idx[:, BANK // 16 :]))
        for cols in (slice(0, BANK), slice(BANK, S)):
            nc.gpsimd.tensor_scalar(minus_wg[:, cols], minus_wg[:, cols], -1.0, 0.0, ALU.mult, ALU.add)

        hs = {}

        def product(s, e, k, cols=slice(0, BANK)):
            acc = bank(k, "acc")
            for a in range(2):
                nc.tensor.matmul_mx(
                    acc[:, cols],
                    lhsT=w1_c[a, s].bitcast(FP8X4),
                    lhsT_scale=w1_s[a, s],
                    rhs=v_w[a, e][:, cols].bitcast(FP8X4),
                    rhs_scale=v_s[4 * a :, e * BANK + cols.start : e * BANK + cols.stop],
                    start=(a == 0),
                    stop=(a == 1),
                )
            return acc

        def magnitude(s, dst, acc):
            bias = b1_rows[:, s, 0:1] if s < PACK else b1_dealt[:, s - PACK : s - PACK + 1]
            nc.scalar.activation(dst, acc, ACT.Abs, bias=bias)

        def first_product(s, banks=(0, 1), room=None):
            hs[s] = tenant(room or "h%d" % (s % PACK), "h", [P, S], F32)
            for e in range(2):
                magnitude(s, hs[s][:, e * BANK : (e + 1) * BANK], product(s, e, banks[e])[:])

        def half_product(s, e, k):
            if e == 0:
                hs[s] = tenant("h%d" % (s % PACK), "h", [P, S], F32)
            magnitude(s, hs[s][:, e * BANK : (e + 1) * BANK], product(s, e, k)[:])

        def scatter_part(room, sums, lo):
            width = len(sums) * HALF
            h = tenant(room, "h", [P, width], F32)
            for k, acc in enumerate(sums):
                magnitude(0, h[:, k * HALF : (k + 1) * HALF], acc)
            entries = idx2[:, lo // 16 : (lo + width) // 16]
            nc.vector.tensor_tensor(pages[0][:].indirect(entries), h[:], minus_wg[:, lo : lo + width], ALU.mult)

        scatter_part("h0", [product(0, 0, 0, slice(0, HALF))[:, :HALF]], 0)
        second_quarter = product(0, 0, 4, slice(HALF, BANK))
        second_half = product(0, 1, 1)
        quantise_w1([1], cast_rows(raw_second, 0, P, quantiser_input("ring1")))
        scatter_part("h0_second", [second_quarter[:, HALF:], second_half[:, :HALF]], HALF)
        quantise_w1([2, 3], cast_rows(raw_rest, 0, 2 * P, quantiser_input("ring2")))
        scatter_part("page3", [second_half[:, HALF:]], BANK + HALF)
        first_product(1, banks=(2, 3), room="ring2")
        pages.append(tenant("page3", "page", [P, T2], F32))
        nc.gpsimd.memset(pages[3][:].bitcast(I32), 0)

        def scatter(s):
            weights = minus_wg[:] if s < PACK else wg_dealt[s - PACK][:]
            nc.vector.tensor_tensor(pages[s % PACK][:].indirect(idx2[:]), hs[s][:], weights, ALU.mult)

        def quantise_dealt(a):
            codes = held.tile([P, KP], U32, name="w1_cd%d" % a, align_bytes=64)
            scales = held.tile([P, KP], U8, name="w1_sd%d" % a, align_bytes=64)
            nc.vector.quantize_mx(codes[:].bitcast(FP8X4), scales[:], dealt_grouped[a][:])
            for t in range(PACK):
                w1_c[a, PACK + t] = codes[:, t * P : (t + 1) * P]
                w1_s[a, PACK + t] = scales[:, t * P : (t + 1) * P]

        turned = [
            [tenant("big%d%d" % (c, k), "turned", [P, BLOCKS, PACK, P], F32) for k in range(2)] for c in range(CHUNKS)
        ]

        def add_transposed(dst, first, second):
            nc.tensor.matmul(dst, first, ident[:], start=True, stop=False, is_transpose=True)
            nc.tensor.matmul(dst, second, ident[:], start=False, stop=True, is_transpose=True)

        def turned_out(dst, src, func, scale):
            nc.scalar.activation(dst, src.rearrange("p (i m t) -> p i t m", i=BLOCKS, t=PACK), func, scale=scale)

        def block(c, i):
            return slice(c * BANK + i * P, c * BANK + (i + 1) * P)

        def open_differences(s):
            banks = [bank(c, "difference") for c in range(CHUNKS)]
            for c in range(CHUNKS):
                for i in range(BLOCKS):
                    dst = banks[c][:, i * P : (i + 1) * P]
                    nc.tensor.matmul(dst, olds[s][:, block(c, i)], ident[:], start=(i == 0), stop=False, is_transpose=True)
            return banks

        def close_differences(s, banks):
            for c in range(CHUNKS):
                for i in range(BLOCKS):
                    dst = banks[c][:, i * P : (i + 1) * P]
                    last = i == BLOCKS - 1
                    nc.tensor.matmul(dst, pages[s][:, block(c, i)], ident[:], start=False, stop=last, is_transpose=True)
                turned_out(turned[c][0][:, :, :, 32 * s : 32 * s + 32], banks[c][:], ACT.Relu, 1.0)

        def turn_page(s, banks):
            for c in range(CHUNKS):
                copied = bank(banks[c], "copied")
                for i in range(BLOCKS):
                    nc.tensor.transpose(copied[:, i * P : (i + 1) * P], pages[s][:, block(c, i)], ident[:])
                turned_out(turned[c][1][:, :, :, 32 * s : 32 * s + 32], copied[:], ACT.Copy, -1.0)

        def turn_back(c, words, blocks, banks):
            for i, k in zip(blocks, banks):
                larger = bank(k, "larger")
                for t in range(PACK):
                    add_transposed(larger[:, t * P : (t + 1) * P], turned[c][1][:, i, t, :], turned[c][0][:, i, t, :])
                nc.scalar.copy(
                    words[i].rearrange("p (c t) -> p c t", t=PACK),
                    larger[:].rearrange("p (t c) -> p c t", t=PACK),
                )

        half_product(2, 0, 4)
        scatter(1)
        close_differences(0, open_differences(0))
        olds[3] = load_old(3)
        wg_dealt = {t: load_weights_dealt(t) for t in range(2)}
        half_product(2, 1, 5)
        turn_page(0, (6, 7, 4, 5))
        dealt_grouped = []
        for a in range(2):
            grouped = quantiser_input("ring%d" % a)
            for e in range(2):
                nc.scalar.copy(
                    grouped[:].rearrange("p (u i m j) -> p u m j i", u=2, i=2, j=PACK)[:, :, e * P // 2 : (e + 1) * P // 2],
                    raw_dealt[a, e][:].rearrange("p j (m u i) -> p u m j i", u=2, i=2),
                )
            dealt_grouped.append(grouped)

        half_product(3, 0, 6)
        half_product(3, 1, 7)
        for t in range(2, PACK):
            wg_dealt[t] = load_weights_dealt(t)
        old_dealt = {TURNED: load_old_dealt(TURNED)}
        scatter(2)
        for a in range(2):
            quantise_dealt(a)
        close_differences(1, open_differences(1))
        scatter(3)
        old_dealt[0] = load_old_dealt(0)
        turn_page(1, (4, 5, 6, 7))
        differences = open_differences(2)
        half_product(4, 0, 4)
        half_product(4, 1, 5)
        scatter(4)
        page_dealt = {0: tenant("side0", "page_dealt", [P, PACK, BANK], F32)}
        nc.sync.dma_start(page_dealt[0][:, 0, :], pages[0][:, :BANK])
        close_differences(2, differences)
        turn_page(2, (6, 7, 4, 5))
        half_product(5, 0, 6)
        differences = open_differences(3)
        half_product(5, 1, 7)
        scatter(5)
        nc.sync.dma_start(page_dealt[0][:, 1, :], pages[1][:, :BANK])
        early = tenant("old0", "minus_old", [P, PACK - 1, BANK], F32)
        nc.scalar.activation(early[:], old_dealt[TURNED][:, : PACK - 1, :], ACT.Copy, scale=-1.0)
        close_differences(3, differences)
        half_product(6, 0, 4)
        turn_page(3, (5, 6, 7, 4))
        half_product(6, 1, 5)
        scatter(6)
        nc.sync.dma_start(page_dealt[0][:, 2, :], pages[2][:, :BANK])
        old_dealt[2] = load_old_dealt(2)
        old_dealt[3] = load_old_dealt(3)
        nc.sync.dma_start(w4_w[:].bitcast(I32), w4_words.rearrange("a p n -> p a n").bitcast(I32))
        for q in range(4):
            nc.sync.dma_start(
                w4_s[32 * q : 32 * q + 4, :, :].bitcast(I32),
                w4_scales[:, 4 * q : 4 * q + 4, :].rearrange("a r n -> r a n").bitcast(I32),
            )
        with nc.allow_non_contiguous_dma(reason="one bias value a partition"):
            nc.sync.dma_start(b4_t[:, :, 0:1], b4.rearrange("(i p o) -> p i o", p=P, o=1))
        left_rooms = ("first0", "first1", "h0_second", "h0_third")
        halves = [(c, lo) for c in range(2, CHUNKS) for lo in (0, HALF)]
        left_tiles = {at: tenant(room, "left_words", [P, PACK * HALF], BF16)[:] for at, room in zip(halves, left_rooms)}
        left_whole = [quantiser_input(room) for room in ("ring2", "ring0")]
        for c in range(2):
            for lo in (0, HALF):
                left_tiles[c, lo] = left_whole[c][:, PACK * lo : PACK * (lo + HALF)]
        left_words = {
            c: [left_tiles[c, i // 2 * HALF][:, i % 2 * BANK : (i % 2 + 1) * BANK] for i in range(BLOCKS)] for c in range(CHUNKS)
        }
        turn_back(0, left_words[0], (0, 2), (0, 1))
        half_product(7, 0, 2)
        turn_back(0, left_words[0], (3,), (3,))
        half_product(7, 1, 7)
        scatter(7)
        turn_back(0, left_words[0], (1,), (6,))
        turn_back(1, left_words[1], range(BLOCKS), (4, 5, 0, 1))
        planes = [tenant("big1%d" % k, "planes", [P, BLOCKS, PACK - 1, P], F32) for k in range(2)]

        def turn_dealt(t, banks):
            difference, copied = bank(banks[0], "difference"), bank(banks[1], "copied")
            for i in range(BLOCKS):
                dst = difference[:, i * P : (i + 1) * P]
                nc.tensor.matmul(dst, early[:, t, i * P : (i + 1) * P], ident[:], start=(i == 0), stop=False, is_transpose=True)
            for i in range(BLOCKS):
                dst = difference[:, i * P : (i + 1) * P]
                last = i == BLOCKS - 1
                nc.tensor.matmul(dst, pages[t][:, block(TURNED, i)], ident[:], start=False, stop=last, is_transpose=True)
            nc.scalar.activation(planes[0][:, :, t, :], difference[:].rearrange("p (i m) -> p i m", i=BLOCKS), ACT.Relu, scale=-1.0)
            for i in range(BLOCKS):
                nc.tensor.transpose(copied[:, i * P : (i + 1) * P], pages[t][:, block(TURNED, i)], ident[:])
            nc.scalar.copy(planes[1][:, :, t, :], copied[:].rearrange("p (i m) -> p i m", i=BLOCKS))

        pieces = [(0, 0, HALF), (0, HALF, HALF), (1, 0, BANK), (2, 0, HALF), (2, HALF, HALF), (3, 0, HALF), (3, HALF, HALF)]
        left_codes, right_codes, accs, staged, words = {}, {}, {}, {}, {}

        def quantise_left(c, lo, room):
            left_codes[c, lo] = tenant(room, "left_codes", [P, HALF], U32)[:]
            nc.vector.quantize_mx(left_codes[c, lo].bitcast(FP8X4), z_s[0][c][:, lo : lo + HALF], left_tiles[c, lo])

        def quantise_left_whole(c, room):
            codes = tenant(room, "left_codes", [P, BANK], U32)
            nc.vector.quantize_mx(codes[:].bitcast(FP8X4), z_s[0][c][:], left_whole[c][:])
            for piece in pieces:
                if piece[0] == c:
                    left_codes[c, piece[1]] = codes[:, piece[1] : piece[1] + piece[2]]

        def score_pass(piece, b, n, codes, lo, width, start, stop):
            c = piece[0]
            shared = N // P // len(accs[piece])
            at = n % shared * piece[2] + lo - piece[1]
            nc.tensor.matmul_mx(
                accs[piece][n // shared][:, at : at + width],
                lhsT=w4_w[:, b, 2 * n * P : 2 * (n + 1) * P].bitcast(FP4X4),
                lhsT_scale=w4_s[:, b, n * P : (n + 1) * P],
                rhs=codes.bitcast(FP8X4),
                rhs_scale=z_s[b][c][:, lo : lo + width],
                start=start,
                stop=stop,
            )

        def open_piece(piece):
            c, lo, width = piece
            ks = [(2 + PACK * c + k) % 8 for k in range(PACK)]
            ks = (0, 1, 2, 3) if piece == pieces[-1] else ks[lo // P : (lo + width) // P]
            accs[piece] = [bank(k, "score") for k in ks]
            shared = N // P // len(ks)
            for n in range(N // P):
                score_pass(piece, 0, n, left_codes[c, lo], lo, width, n % shared == 0, False)

        turn_dealt(0, (2, 3))
        turn_back(2, left_words[2], range(BLOCKS), (6, 7, 4, 5))
        turn_dealt(1, (0, 1))
        turn_back(3, left_words[3], range(BLOCKS), (2, 3, 6, 7))
        turn_dealt(2, (0, 1))
        turned_rows = tenant("h0", "turned_rows", [P, 2, BANK], BF16)
        words[pieces[2]] = quantiser_input("h1")
        turned_words = words[pieces[2]][:].rearrange("p (c t) -> p c t", t=PACK)
        for i in range(BLOCKS):
            larger_rows = bank(2 + i, "larger")
            for t in range(PACK - 1):
                add_transposed(larger_rows[:, t * P : (t + 1) * P], planes[1][:, i, t, :], planes[0][:, i, t, :])
            nc.scalar.copy(
                turned_words[:, i * P : (i + 1) * P, :2], larger_rows[:, : 2 * P].rearrange("p (t c) -> p c t", t=2)
            )
            nc.scalar.copy(turned_rows[:, 0, i * P : (i + 1) * P], larger_rows[:, 2 * P : 3 * P])
        for c, room in ((2, "old2"), (3, "big00")):
            page_dealt[c] = tenant(room, "page_dealt", [P, PACK, BANK], F32)
        for t in range(PACK):
            for c in (2, 3):
                nc.sync.dma_start(page_dealt[c][:, t, :], pages[t][:, c * BANK : (c + 1) * BANK])

        def larger(piece, room):
            c, lo, width = piece
            cols = slice(lo, lo + width)
            words[piece] = tenant(room, "words", [P, PACK * width], BF16)
            nc.vector.tensor_tensor(
                words[piece][:].rearrange("p (c i t) -> p c t i", i=8, t=PACK),
                page_dealt[c][:, :, cols].rearrange("p t (c i) -> p c t i", i=8),
                old_dealt[c][:, :, cols].rearrange("p t (c i) -> p c t i", i=8),
                ALU.max,
            )

        def quantise_right(piece, room):
            c, lo, width = piece
            right_codes[piece] = tenant(room, "right_codes", [P, width], U32)
            nc.vector.quantize_mx(right_codes[piece][:].bitcast(FP8X4), z_s[1][c][:, lo : lo + width], words[piece][:])

        def close_piece(piece, on_vector=()):
            c, lo, width = piece
            cols = slice(c * BANK + lo, c * BANK + lo + width)
            shared = N // P // len(accs[piece])
            for n in range(N // P):
                score_pass(piece, 1, n, right_codes[piece][:], lo, width, False, n % shared == shared - 1)
            if lo == 0:
                staged[c] = tenant(("page0", "page1", "page2", "big20")[c], "y", [P, N // P * BANK], F32)
            y = staged[c][:, N // P * lo : N // P * (lo + width)].rearrange("p (n c) -> p n c", n=N // P)
            together = BANK // width
            for n in range(N // P):
                part = accs[piece][n // shared][:, n % shared * width : (n % shared + 1) * width]
                if n in on_vector:
                    nc.vector.tensor_scalar(y[:, n, :], part, b4_t[:, n, 0:1], None, ALU.add)
                else:
                    nc.scalar.activation(y[:, n, :], part, ACT.Identity, bias=b4_t[:, n, 0:1])
                if (n + 1) % together == 0:
                    first = n + 1 - together
                    nc.sync.dma_start(
                        out[first * P : (n + 1) * P, cols].rearrange("(i p) c -> p i c", i=together),
                        y[:, first : n + 1, :],
                    )

        def copy_last_page(lo):
            nc.vector.tensor_copy(page_dealt[0][:, PACK - 1, lo : lo + HALF], pages[PACK - 1][:, lo : lo + HALF])

        quantise_left(0, 0, "v_w11")
        open_piece(pieces[0])
        copy_last_page(0)
        nc.vector.tensor_tensor(
            turned_rows[:, 1, :],
            pages[PACK - 1][:, TURNED * BANK : (TURNED + 1) * BANK],
            old_dealt[TURNED][:, PACK - 1, :],
            ALU.max,
        )
        nc.scalar.copy(turned_words[:, :, 2:], turned_rows[:].rearrange("p t c -> p c t"))
        larger(pieces[0], "ring1")
        copy_last_page(HALF)
        quantise_right(pieces[0], "v_w0")
        close_piece(pieces[0])
        larger(pieces[1], "weights")
        quantise_left(0, HALF, "ring1")
        open_piece(pieces[1])
        quantise_right(pieces[1], "h2")
        close_piece(pieces[1])
        quantise_left_whole(1, "big10")
        open_piece(pieces[2])
        quantise_left(2, 0, "h0")
        quantise_right(pieces[2], "v_w10")
        close_piece(pieces[2])
        next_left = ("h1", "first0", "first1")
        for k, piece in enumerate(pieces[3:]):
            open_piece(piece)
            larger(piece, left_rooms[k])
            if k < len(next_left):
                quantise_left(pieces[4 + k][0], pieces[4 + k][1], next_left[k])
            quantise_right(piece, ("h3", "wg0", "wg1", "wg2")[k])
            close_piece(piece, on_vector=(1, 3) if piece == pieces[-1] else ())
